import numpy as np
import ml_dtypes


def mxq(x, axis, fmt="e4m3"):
    dtype, down = {"e4m3": (ml_dtypes.float8_e4m3fn, 7), "e5m2": (ml_dtypes.float8_e5m2, 14)}[fmt]
    v = np.moveaxis(np.asarray(x, np.float32).astype(ml_dtypes.bfloat16).astype(np.float64), axis, -1)
    blocks = v.reshape(v.shape[:-1] + (-1, 32))
    amax = np.abs(blocks).max(-1, keepdims=True)
    byte = np.maximum(np.where(amax > 0, np.frexp(amax)[1] - 1 + 127, 0) - down, 1)
    scale = np.exp2(byte - 127.0)
    codes = (blocks / scale).astype(np.float32).astype(dtype).astype(np.float64)
    return np.moveaxis((codes * scale).reshape(v.shape), -1, axis)


WIDE = False


def mx_kscale(k):
    if not WIDE:
        return np.ones(k)
    levels = np.array([10, -10, 5, -5, 0])
    if k % 512:
        return np.exp2(np.random.permutation(np.resize(levels, k // 32))).repeat(32)
    a = np.empty((k // 512, 16))
    for p in range(k // 512):
        a[p, :8] = np.random.permutation(np.resize(levels, 8))
        for g in range(8):
            far = levels[np.abs(levels - a[p, g]) >= 10]
            a[p, g + 8] = far[np.random.randint(len(far))]
    return np.exp2(a.ravel()).repeat(32)


def f64(x):
    return np.asarray(x).astype(np.float64)


def striped(idx):
    return np.tile(idx.reshape(-1, 16).T, (8, 1)).astype(np.uint16)


def unstriped(offs):
    return offs[:16].T.reshape(-1).astype(np.int64)


E2M1 = np.array([0.0, 0.5, 1.0, 1.5, 2.0, 3.0, 4.0, 6.0, -0.0, -0.5, -1.0, -1.5, -2.0, -3.0, -4.0, -6.0])


def pack_weight(w, fmt):
    k, n = w.shape
    w = f64(np.asarray(w, np.float32).astype(ml_dtypes.bfloat16)).reshape(k // 32, 32, n)
    amax = np.abs(w).max(1)
    if fmt == "e4m3":
        byte = np.frexp(amax)[1] - 1 + 127 - 7
    else:
        mant, ex = np.frexp(amax / 6.0)
        byte = np.where(mant > 0.5, ex, ex - 1) + 127
    byte = np.clip(np.where(amax > 0, byte, 1), 1, 254)
    scaled = (w * np.exp2(127.0 - byte)[:, None, :]).reshape(k, n).astype(np.float32)
    by_word = np.ascontiguousarray(scaled.reshape(k // 512, 128, 4, n).transpose(0, 1, 3, 2))
    if fmt == "e4m3":
        words = by_word.astype(ml_dtypes.float8_e4m3fn).view(np.uint8)
    else:
        c = by_word.astype(ml_dtypes.float4_e2m1fn).view(np.uint8) & 0xF
        words = (c[..., 0::2] | (c[..., 1::2] << 4)).reshape(k // 512, 128, 2 * n)
    return np.ascontiguousarray(words), np.ascontiguousarray(byte.astype(np.uint8).reshape(k // 512, 16, n))


def unpack_weight(words, scales, fmt):
    g, _, n = scales.shape
    words = np.ascontiguousarray(words).reshape(g, 128, n, -1)
    if fmt == "e4m3":
        vals = words.view(ml_dtypes.float8_e4m3fn).astype(np.float64)
    else:
        nib = np.empty((g, 128, n, 4), np.uint8)
        nib[..., 0::2] = words & 0xF
        nib[..., 1::2] = words >> 4
        vals = E2M1[nib]
    vals = vals * np.repeat(np.exp2(scales.astype(np.float64) - 127.0), 8, axis=1)[..., None]
    return vals.transpose(0, 1, 3, 2).reshape(g * 512, n)


def gelu(v):
    return 0.5 * v * (1.0 + np.tanh(np.sqrt(2.0 / np.pi) * (v + 0.044715 * v**3)))


K, T, S, P, H, N = 1536, 2048, 1024, 512, 1024, 512

def setup_inputs():
    n = np.random.standard_normal
    s = mx_kscale(K)[:, None]
    u = mx_kscale(H)[:, None]
    tab_words, tab_scales = pack_weight(n((K, T)) * s, "e4m3")
    w1 = n((K, H)) / np.sqrt(K) / s
    gain = np.exp(0.3 * n(H)) * u[:, 0]
    w2_words, w2_scales = pack_weight(2.5 * n((H, N)) / np.sqrt(H) / u, "e2m1")
    return {
        "tab_words": tab_words, "tab_scales": tab_scales,
        "offs": striped(np.random.permutation(T)[:S]),
        "w1": w1.astype(np.float32),
        "pos1": striped(np.random.permutation(S)[:P]),
        "pos2": striped(np.random.permutation(S)[:P]),
        "gain": gain.astype(np.float32),
        "w2_words": w2_words, "w2_scales": w2_scales,
    }

def reference(tab_words, tab_scales, offs, w1, pos1, pos2, gain, w2_words, w2_scales):
    v = unpack_weight(tab_words, tab_scales, "e4m3")[:, unstriped(offs)]
    w1q = mxq(f64(w1), 0, "e4m3")
    h = w1q.T @ v
    a = h[:, unstriped(pos1)]
    b = h[:, unstriped(pos2)]
    z = np.exp(-np.abs(a - b)) * f64(gain)[:, None]
    zq = mxq(z, 0, "e4m3")
    w2 = unpack_weight(w2_words, w2_scales, "e2m1")
    y = w2.T @ zq
    return 1.0 / (1.0 + np.exp(-y))

@@ -1,0 +1,222 @@
+from contextlib import ExitStack
+
+import concourse.mybir as mybir
+
+K, T, S, PAIRS, H, N = 1536, 2048, 1024, 512, 1024, 512
+FLOPS = 2 * K * H * S + 2 * H * N * PAIRS
+
+F32 = mybir.dt.float32
+BF16 = mybir.dt.bfloat16
+I32 = mybir.dt.int32
+U32 = mybir.dt.uint32
+U16 = mybir.dt.uint16
+U8 = mybir.dt.uint8
+FP8X4 = mybir.dt.float8_e4m3fn_x4
+FP4X4 = mybir.dt.float4_e2m1fn_x4
+ACT = mybir.ActivationFunctionType
+ALU = mybir.AluOpType
+
+P = 128
+PACK = 4
+K_PASS = P * PACK
+K_PASSES = K // K_PASS
+R_PASSES = H // K_PASS
+BANK = 512
+JB = 128
+
+
+def tile_list_duplicate_pair_score_kernel(tc, tab_words, tab_scales, offs, w1, pos1, pos2, gain, w2_words, w2_scales, out):
+    nc = tc.nc
+    with ExitStack() as ctx:
+        keep = ctx.enter_context(tc.tile_pool(name="keep", bufs=1))
+        psum = ctx.enter_context(tc.psum_pool(name="psum", bufs=8))
+
+        offs_sb = keep.tile([P, S // 16], U16, name="offs_sb")
+        pos_sb = [keep.tile([P, PAIRS // 16], U16, name="pos_sb%d" % i) for i in range(2)]
+        tab_w = [keep.tile([P, T], I32, name="tab_w%d" % a, align_bytes=64) for a in range(K_PASSES)]
+        tab_s = keep.tile([P, T // 4], I32, name="tab_s", align_bytes=64)
+        v_w = [keep.tile([P, S], U32, name="v_w%d" % a, align_bytes=64) for a in range(K_PASSES)]
+        v_s = keep.tile([P, S], U8, name="v_s", align_bytes=64)
+        gain_sb = keep.tile([P, R_PASSES, PACK], F32, name="gain_sb")
+        w2_w = keep.tile([P, R_PASSES, 2 * N // 4], I32, name="w2_w", align_bytes=64)
+        w2_s = keep.tile([P, R_PASSES, N // 4], I32, name="w2_s", align_bytes=64)
+        warm = keep.tile([P, 2], F32, name="warm")
+
+        nc.vector.memset(warm[:, 0:1], 0.0)
+        nc.scalar.activation(warm[:, 1:2], warm[:, 0:1], ACT.Exp)
+
+        nc.gpsimd.memset(tab_s[:], 0)
+        for q in range(4):
+            nc.gpsimd.dma_start(tab_s[32 * q : 32 * q + 4 * K_PASSES, :], tab_scales[:, 4 * q : 4 * q + 4, :].bitcast(I32))
+        nc.gpsimd.memset(w2_s[:], 0)
+        for q in range(4):
+            nc.gpsimd.dma_start(w2_s[32 * q : 32 * q + 4, :, :], w2_scales[:, 4 * q : 4 * q + 4, :].bitcast(I32).rearrange("b r n -> r b n"))
+
+        raw = {}
+
+        def load_tab(a):
+            nc.sync.dma_start(tab_w[a][:], tab_words[a].rearrange("p t i -> p (t i)").bitcast(I32))
+
+        def load_w1(a, b, m0, m1):
+            t = keep.tile([P, PACK, PACK * (m1 - m0)], F32, name="w1_raw%d_%d_%d" % (a, b, m0))
+            cols = slice(K_PASS * b + PACK * m0, K_PASS * b + PACK * m1)
+            nc.sync.dma_start(t[:], w1[K_PASS * a : K_PASS * (a + 1), cols].rearrange("(p j) c -> p j c", j=PACK))
+            raw[(a, b, m0)] = t
+
+        nc.sync.dma_start(offs_sb[:], offs)
+        load_tab(0)
+        load_w1(0, 0, 0, P)
+        load_tab(1)
+        load_w1(1, 0, 0, P)
+        load_tab(2)
+        load_w1(2, 0, 0, P // 2)
+        load_w1(2, 0, P // 2, P)
+        nc.sync.dma_start(pos_sb[0][:], pos1)
+        nc.sync.dma_start(pos_sb[1][:], pos2)
+        for a in range(K_PASSES):
+            load_w1(a, 1, 0, P)
+        nc.sync.dma_start(gain_sb[:], gain.rearrange("(b p t) -> p b t", b=R_PASSES, t=PACK))
+        nc.sync.dma_start(w2_w[:], w2_words.bitcast(I32).rearrange("b p n -> p b n"))
+
+        w_bf = {}
+        w_c = {}
+        w_s = {}
+        for a in range(K_PASSES):
+            for b in range(R_PASSES):
+                w_bf[(a, b)] = keep.tile([P, PACK, P, PACK], BF16, name="w_bf%d_%d" % (a, b), align_bytes=64)
+                w_c[(a, b)] = keep.tile([P, K_PASS], U32, name="w_c%d_%d" % (a, b), align_bytes=64)
+                w_s[(a, b)] = keep.tile([P, K_PASS], U8, name="w_s%d_%d" % (a, b), align_bytes=64)
+
+        def round_w1(engine, a, b, base, m0, m1):
+            src = raw[(a, b, base)][:, :, PACK * (m0 - base) : PACK * (m1 - base)].rearrange("p j (m t) -> p m j t", t=PACK)
+            dst = w_bf[(a, b)][:, :, m0:m1, :].rearrange("p t m j -> p m j t")
+            if engine == "scalar":
+                nc.scalar.copy(dst, src)
+            elif engine == "vector":
+                nc.vector.tensor_copy(dst, src)
+            else:
+                nc.gpsimd.tensor_scalar(dst, src, 1.0, 0.0, ALU.mult, ALU.add)
+
+        def quant_w1(a, b, t0, t1):
+            cols = slice(P * t0, P * t1)
+            nc.vector.quantize_mx(
+                out=w_c[(a, b)][:, cols].bitcast(FP8X4),
+                scales=w_s[(a, b)][:, cols],
+                in_=w_bf[(a, b)][:, t0:t1, :, :].rearrange("p t m j -> p (t m j)"),
+            )
+
+        def gather_tab(a):
+            nc.vector.tensor_copy(v_w[a][:], tab_w[a][:].bitcast(U32).indirect(offs_sb[:]))
+
+        acc = {}
+
+        def embed_pass(a, b, t):
+            for half in range(S // BANK):
+                if a == 0:
+                    acc[(b, t, half)] = psum.tile([P, BANK], F32, name="bank")
+                cols = slice(BANK * half, BANK * (half + 1))
+                nc.tensor.matmul_mx(
+                    out=acc[(b, t, half)][:],
+                    lhsT=w_c[(a, b)][:, P * t : P * (t + 1)].bitcast(FP8X4),
+                    lhsT_scale=w_s[(a, b)][:, P * t : P * (t + 1)],
+                    rhs=v_w[a][:, cols].bitcast(FP8X4),
+                    rhs_scale=v_s[4 * a : P, cols],
+                    start=(a == 0),
+                    stop=(a == K_PASSES - 1),
+                )
+
+        h = {}
+
+        def drain_h(b, t, vec_halves):
+            h[(b, t)] = keep.tile([P, S], F32, name="h%d_%d" % (b, t))
+            for half in range(S // BANK):
+                dst = h[(b, t)][:, BANK * half : BANK * (half + 1)]
+                if half in vec_halves:
+                    nc.vector.tensor_copy(dst, acc[(b, t, half)][:])
+                else:
+                    nc.scalar.copy(dst, acc[(b, t, half)][:])
+
+        gather_tab(0)
+        round_w1("scalar", 0, 0, 0, 0, P)
+        nc.vector.tensor_copy(v_s[:], tab_s[:].bitcast(U8).indirect(offs_sb[:]))
+        quant_w1(0, 0, 0, PACK)
+        for t in range(PACK):
+            embed_pass(0, 0, t)
+        gather_tab(1)
+        round_w1("scalar", 1, 0, 0, 0, 80)
+        round_w1("vector", 1, 0, 0, 80, P)
+        quant_w1(1, 0, 0, PACK)
+        for t in range(PACK):
+            embed_pass(1, 0, t)
+        gather_tab(2)
+        round_w1("scalar", 2, 0, 0, 0, P // 2)
+        round_w1("scalar", 2, 0, P // 2, P // 2, 88)
+        round_w1("vector", 2, 0, P // 2, 88, P)
+        for t in range(PACK):
+            quant_w1(2, 0, t, t + 1)
+            embed_pass(2, 0, t)
+        for t in range(PACK):
+            drain_h(0, t, (1,) if t == 0 else ())
+
+        for a in range(K_PASSES):
+            round_w1("scalar", a, 1, 0, 0, P)
+            quant_w1(a, 1, 0, PACK)
+        for t in range(PACK):
+            for a in range(K_PASSES):
+                embed_pass(a, 1, t)
+            drain_h(1, t, ())
+
+        z_c = [keep.tile([P, PAIRS], U32, name="z_c%d" % b, align_bytes=64) for b in range(R_PASSES)]
+        z_s = [keep.tile([P, PAIRS], U8, name="z_s%d" % b, align_bytes=64) for b in range(R_PASSES)]
+
+        def similarity(b, j0, j1, t_step):
+            w = j1 - j0
+            lhs = keep.tile([P, PACK, w], F32, name="lhs%d_%d" % (b, j0))
+            rhs = keep.tile([P, PACK, w], F32, name="rhs%d_%d" % (b, j0))
+            z_bf = keep.tile([P, w, PACK], BF16, name="z_bf%d_%d" % (b, j0), align_bytes=64)
+            for t0 in range(0, PACK, t_step):
+                for t in range(t0, t0 + t_step):
+                    nc.vector.tensor_copy(lhs[:, t, :], h[(b, t)][:].indirect(pos_sb[0][:, j0 // 16 : j1 // 16]))
+                    nc.vector.tensor_copy(rhs[:, t, :], h[(b, t)][:].indirect(pos_sb[1][:, j0 // 16 : j1 // 16]))
+                d = lhs[:, t0 : t0 + t_step, :]
+                nc.vector.tensor_tensor(d, d, rhs[:, t0 : t0 + t_step, :], ALU.subtract)
+                nc.scalar.activation(d, d, ACT.Abs)
+                nc.scalar.activation(d, d, ACT.Exp, scale=-1.0)
+            step = min(w, 256)
+            for c0 in range(0, w, step):
+                nc.vector.tensor_tensor(
+                    z_bf[:, c0 : c0 + step, :].rearrange("p (c i) t -> p c t i", i=4),
+                    lhs[:, :, c0 : c0 + step].rearrange("p t (c i) -> p c t i", i=4),
+                    gain_sb[:, b, :].unsqueeze(1).unsqueeze(3).to_broadcast([P, step // 4, PACK, 4]),
+                    ALU.mult,
+                )
+            nc.vector.quantize_mx(
+                out=z_c[b][:, j0:j1].bitcast(FP8X4),
+                scales=z_s[b][:, j0:j1],
+                in_=z_bf[:].rearrange("p j t -> p (j t)"),
+            )
+
+        def score(j0):
+            y = psum.tile([P, N // P, JB], F32, name="bank")
+            cols = slice(j0, j0 + JB)
+            for nt in range(N // P):
+                for b in range(R_PASSES):
+                    nc.tensor.matmul_mx(
+                        out=y[:, nt, :],
+                        lhsT=w2_w[:, b, :].bitcast(U8)[:, 2 * P * nt : 2 * P * (nt + 1)].bitcast(FP4X4),
+                        lhsT_scale=w2_s[:, b, :].bitcast(U8)[:, P * nt : P * (nt + 1)],
+                        rhs=z_c[b][:, cols].bitcast(FP8X4),
+                        rhs_scale=z_s[b][:, cols],
+                        start=(b == 0),
+                        stop=(b == R_PASSES - 1),
+                    )
+            o = keep.tile([P, N // P, JB], F32, name="o%d" % j0)
+            nc.scalar.activation(o[:], y[:], ACT.Tanh, scale=0.5)
+            nc.vector.tensor_scalar(o[:], o[:], 0.5, 0.5, ALU.mult, ALU.add)
+            nc.sync.dma_start(out[:, cols].rearrange("(nt p) j -> p nt j", p=P), o[:])
+
+        similarity(0, 0, PAIRS, 2)
+        for j0, j1, t_step in ((0, 256, 2), (256, 384, 2), (384, 512, 1)):
+            similarity(1, j0, j1, t_step)
+            for j in range(j0, j1, JB):
+                score(j)

@@ -42,15 +42,13 @@ def tile_list_duplicate_pair_score_kernel(tc, tab_words, tab_scales, offs, w1, p
         w2_s = keep.tile([P, R_PASSES, N // 4], I32, name="w2_s", align_bytes=64)
         warm = keep.tile([P, 2], F32, name="warm")
 
-        nc.vector.memset(warm[:, 0:1], 0.0)
-        nc.scalar.activation(warm[:, 1:2], warm[:, 0:1], ACT.Exp)
 
         nc.gpsimd.memset(tab_s[:], 0)
-        for q in range(4):
-            nc.gpsimd.dma_start(tab_s[32 * q : 32 * q + 4 * K_PASSES, :], tab_scales[:, 4 * q : 4 * q + 4, :].bitcast(I32))
+        for q in range(2):
+            nc.scalar.dma_start(tab_s[32 * q : 32 * q + 4 * K_PASSES, :], tab_scales[:, 4 * q : 4 * q + 4, :].bitcast(I32))
+        nc.gpsimd.memset(warm[:, 0:1], 0.0)
+        nc.scalar.activation(warm[:, 1:2], warm[:, 0:1], ACT.Exp)
         nc.gpsimd.memset(w2_s[:], 0)
-        for q in range(4):
-            nc.gpsimd.dma_start(w2_s[32 * q : 32 * q + 4, :, :], w2_scales[:, 4 * q : 4 * q + 4, :].bitcast(I32).rearrange("b r n -> r b n"))
 
         raw = {}
 
@@ -58,13 +56,15 @@ def tile_list_duplicate_pair_score_kernel(tc, tab_words, tab_scales, offs, w1, p
             nc.sync.dma_start(tab_w[a][:], tab_words[a].rearrange("p t i -> p (t i)").bitcast(I32))
 
         def load_w1(a, b, m0, m1):
-            t = keep.tile([P, PACK, PACK * (m1 - m0)], F32, name="w1_raw%d_%d_%d" % (a, b, m0))
+            t = keep.tile([P, PACK, PACK * (m1 - m0)], F32, name="w1_raw%d_%d_%d" % (a, b, m0), tag="w1_raw%d_%d_%d" % (a, b, m0), align_bytes=64)
             cols = slice(K_PASS * b + PACK * m0, K_PASS * b + PACK * m1)
             nc.sync.dma_start(t[:], w1[K_PASS * a : K_PASS * (a + 1), cols].rearrange("(p j) c -> p j c", j=PACK))
             raw[(a, b, m0)] = t
 
         nc.sync.dma_start(offs_sb[:], offs)
         load_tab(0)
+        for q in range(2, 4):
+            nc.sync.dma_start(tab_s[32 * q : 32 * q + 4 * K_PASSES, :], tab_scales[:, 4 * q : 4 * q + 4, :].bitcast(I32))
         load_w1(0, 0, 0, P)
         load_tab(1)
         load_w1(1, 0, 0, P)
@@ -73,9 +73,12 @@ def tile_list_duplicate_pair_score_kernel(tc, tab_words, tab_scales, offs, w1, p
         load_w1(2, 0, P // 2, P)
         nc.sync.dma_start(pos_sb[0][:], pos1)
         nc.sync.dma_start(pos_sb[1][:], pos2)
-        for a in range(K_PASSES):
-            load_w1(a, 1, 0, P)
+        load_w1(0, 1, 0, P)
         nc.sync.dma_start(gain_sb[:], gain.rearrange("(b p t) -> p b t", b=R_PASSES, t=PACK))
+        for q in range(4):
+            nc.sync.dma_start(w2_s[32 * q : 32 * q + 4, :, :], w2_scales[:, 4 * q : 4 * q + 4, :].bitcast(I32).rearrange("b r n -> r b n"))
+        load_w1(1, 1, 0, P)
+        load_w1(2, 1, 0, P)
         nc.sync.dma_start(w2_w[:], w2_words.bitcast(I32).rearrange("b p n -> p b n"))
 
         w_bf = {}
@@ -83,8 +86,7 @@ def tile_list_duplicate_pair_score_kernel(tc, tab_words, tab_scales, offs, w1, p
         w_s = {}
         for a in range(K_PASSES):
             for b in range(R_PASSES):
-                w_bf[(a, b)] = keep.tile([P, PACK, P, PACK], BF16, name="w_bf%d_%d" % (a, b), align_bytes=64)
-                w_c[(a, b)] = keep.tile([P, K_PASS], U32, name="w_c%d_%d" % (a, b), align_bytes=64)
+                w_bf[(a, b)] = keep.tile([P, PACK, P, PACK], BF16, name="w_bf%d_%d" % (a, b), tag="w_bf%d_%d" % (a, b), align_bytes=64)
                 w_s[(a, b)] = keep.tile([P, K_PASS], U8, name="w_s%d_%d" % (a, b), align_bytes=64)
 
         def round_w1(engine, a, b, base, m0, m1):
@@ -97,7 +99,10 @@ def tile_list_duplicate_pair_score_kernel(tc, tab_words, tab_scales, offs, w1, p
             else:
                 nc.gpsimd.tensor_scalar(dst, src, 1.0, 0.0, ALU.mult, ALU.add)
 
-        def quant_w1(a, b, t0, t1):
+        def quant_w1(a, b, t0, t1, tag=None):
+            if (a, b) not in w_c:
+                key = "w_c%d_%d" % (a, b)
+                w_c[(a, b)] = keep.tile([P, K_PASS], U32, name=key, tag=tag or key, align_bytes=64)
             cols = slice(P * t0, P * t1)
             nc.vector.quantize_mx(
                 out=w_c[(a, b)][:, cols].bitcast(FP8X4),
@@ -128,7 +133,7 @@ def tile_list_duplicate_pair_score_kernel(tc, tab_words, tab_scales, offs, w1, p
         h = {}
 
         def drain_h(b, t, vec_halves):
-            h[(b, t)] = keep.tile([P, S], F32, name="h%d_%d" % (b, t))
+            h[(b, t)] = keep.tile([P, S], F32, name="h%d_%d" % (b, t), tag="h%d_%d" % (b, t), align_bytes=64)
             for half in range(S // BANK):
                 dst = h[(b, t)][:, BANK * half : BANK * (half + 1)]
                 if half in vec_halves:
@@ -137,86 +142,158 @@ def tile_list_duplicate_pair_score_kernel(tc, tab_words, tab_scales, offs, w1, p
                     nc.scalar.copy(dst, acc[(b, t, half)][:])
 
         gather_tab(0)
-        round_w1("scalar", 0, 0, 0, 0, P)
         nc.vector.tensor_copy(v_s[:], tab_s[:].bitcast(U8).indirect(offs_sb[:]))
+        gather_tab(1)
+        round_w1("scalar", 0, 0, 0, 0, 96)
+        round_w1("vector", 0, 0, 0, 96, 128)
         quant_w1(0, 0, 0, PACK)
         for t in range(PACK):
             embed_pass(0, 0, t)
-        gather_tab(1)
+        gather_tab(2)
         round_w1("scalar", 1, 0, 0, 0, 80)
-        round_w1("vector", 1, 0, 0, 80, P)
+        round_w1("vector", 1, 0, 0, 80, 128)
         quant_w1(1, 0, 0, PACK)
         for t in range(PACK):
             embed_pass(1, 0, t)
-        gather_tab(2)
-        round_w1("scalar", 2, 0, 0, 0, P // 2)
-        round_w1("scalar", 2, 0, P // 2, P // 2, 88)
-        round_w1("vector", 2, 0, P // 2, 88, P)
+        round_w1("scalar", 2, 0, 0, 0, 64)
+        round_w1("scalar", 2, 0, 64, 64, 88)
+        round_w1("vector", 2, 0, 64, 88, 128)
         for t in range(PACK):
             quant_w1(2, 0, t, t + 1)
             embed_pass(2, 0, t)
-        for t in range(PACK):
-            drain_h(0, t, (1,) if t == 0 else ())
-
-        for a in range(K_PASSES):
-            round_w1("scalar", a, 1, 0, 0, P)
-            quant_w1(a, 1, 0, PACK)
-        for t in range(PACK):
-            for a in range(K_PASSES):
-                embed_pass(a, 1, t)
-            drain_h(1, t, ())
-
         z_c = [keep.tile([P, PAIRS], U32, name="z_c%d" % b, align_bytes=64) for b in range(R_PASSES)]
         z_s = [keep.tile([P, PAIRS], U8, name="z_s%d" % b, align_bytes=64) for b in range(R_PASSES)]
+        z_bf = {1: keep.tile([P, PAIRS, PACK], BF16, name="z_bf1", align_bytes=64)}
+        diff = {}
+        GROUPS = (((0, 2), (2, 4)), ((0, 2), (2, 3), (3, 4)))
+        sim = [keep.tile([P, PACK, PAIRS], F32, name="sim%d" % b, tag="sim%d" % b, align_bytes=64) for b in range(R_PASSES)]
+        z_planes = keep.tile([P, PACK, PAIRS], BF16, name="z_planes")
+        SH = {"pick0_2":"w_bf0_1","pick0_3_0":"w_bf1_1","pick0_3_1":"w_bf2_1","dist0_0_0":"w1_raw2_1_0","dist0_2_0":"w_c2_1","diff0_0":"w1_raw0_1_0","pick1_0":"w_bf0_0","pick1_1":"w_bf1_0","pick1_2":"w_bf2_0","pick1_3":"w1_raw2_0_0","diff0_2":"w1_raw2_0_64","diff1_0":"w1_raw0_0_0","dist1_0_0":"w1_raw1_0_0"}
 
-        def similarity(b, j0, j1, t_step):
-            w = j1 - j0
-            lhs = keep.tile([P, PACK, w], F32, name="lhs%d_%d" % (b, j0))
-            rhs = keep.tile([P, PACK, w], F32, name="rhs%d_%d" % (b, j0))
-            z_bf = keep.tile([P, w, PACK], BF16, name="z_bf%d_%d" % (b, j0), align_bytes=64)
-            for t0 in range(0, PACK, t_step):
-                for t in range(t0, t0 + t_step):
-                    nc.vector.tensor_copy(lhs[:, t, :], h[(b, t)][:].indirect(pos_sb[0][:, j0 // 16 : j1 // 16]))
-                    nc.vector.tensor_copy(rhs[:, t, :], h[(b, t)][:].indirect(pos_sb[1][:, j0 // 16 : j1 // 16]))
-                d = lhs[:, t0 : t0 + t_step, :]
-                nc.vector.tensor_tensor(d, d, rhs[:, t0 : t0 + t_step, :], ALU.subtract)
-                nc.scalar.activation(d, d, ACT.Abs)
-                nc.scalar.activation(d, d, ACT.Exp, scale=-1.0)
-            step = min(w, 256)
-            for c0 in range(0, w, step):
-                nc.vector.tensor_tensor(
-                    z_bf[:, c0 : c0 + step, :].rearrange("p (c i) t -> p c t i", i=4),
-                    lhs[:, :, c0 : c0 + step].rearrange("p t (c i) -> p c t i", i=4),
-                    gain_sb[:, b, :].unsqueeze(1).unsqueeze(3).to_broadcast([P, step // 4, PACK, 4]),
-                    ALU.mult,
-                )
+        picked = {}
+
+        def pick(b, t, side):
+            key = "pick%d_%d_%d" % (b, t, side)
+            picked[(b, t, side)] = keep.tile([P, PAIRS], F32, name=key, tag=SH.get(key, key), align_bytes=64)
+            nc.vector.tensor_copy(picked[(b, t, side)][:], h[(b, t)][:].indirect(pos_sb[side][:]))
+
+        def pick_both(b, t):
+            key = "pick%d_%d" % (b, t)
+            both = keep.tile([P, 2, PAIRS], F32, name=key, tag=SH.get(key, key), align_bytes=64)
+            for side in range(2):
+                picked[(b, t, side)] = both[:, side, :]
+                nc.vector.tensor_copy(both[:, side, :], h[(b, t)][:].indirect(pos_sb[side][:]))
+
+        def subtract(b, t, engine):
+            t0, t1 = [g for g in GROUPS[b] if g[0] <= t < g[1]][0]
+            if (b, t0) not in diff:
+                key = "diff%d_%d" % (b, t0)
+                diff[(b, t0)] = keep.tile([P, t1 - t0, PAIRS], F32, name=key, tag=SH.get(key, key), align_bytes=64)
+            step = PAIRS // 1 if engine is nc.gpsimd else PAIRS // 2
+            for j0 in range(0, PAIRS, step):
+                engine.tensor_tensor(diff[(b, t0)][:, t - t0, j0 : j0 + step], picked[(b, t, 0)][:, j0 : j0 + step], picked[(b, t, 1)][:, j0 : j0 + step], ALU.subtract)
+
+        def closeness(b, t0, t1, j0, j1):
+            key = "dist%d_%d_%d" % (b, t0, j0)
+            dist = keep.tile([P, t1 - t0, j1 - j0], F32, name=key, tag=SH.get(key, key), align_bytes=64)
+            nc.scalar.activation(dist[:], diff[(b, t0)][:, :, j0:j1], ACT.Abs)
+            nc.scalar.activation(sim[b][:, t0:t1, j0:j1], dist[:], ACT.Exp, scale=-1.0)
+
+        def weigh(b, j0, j1):
+            nc.vector.tensor_tensor(
+                z_bf[b][:, j0:j1, :].rearrange("p (c i) t -> p c t i", i=4),
+                sim[b][:, :, j0:j1].rearrange("p t (c i) -> p c t i", i=4),
+                gain_sb[:, b, :].unsqueeze(1).unsqueeze(3).to_broadcast([P, (j1 - j0) // 4, PACK, 4]),
+                ALU.mult,
+            )
+
+        def weigh_plane(t):
+            nc.gpsimd.tensor_scalar(z_planes[:, t, :], sim[0][:, t, :], gain_sb[:, 0, t : t + 1], 0.0, ALU.mult, ALU.add)
+
+        def interleave(j0, j1):
+            nc.vector.tensor_copy(
+                z_bf[0][:, j0:j1, :].rearrange("p (c i) t -> p c t i", i=4),
+                z_planes[:, :, j0:j1].rearrange("p t (c i) -> p c t i", i=4),
+            )
+
+        def quant_z(b, j0, j1):
             nc.vector.quantize_mx(
                 out=z_c[b][:, j0:j1].bitcast(FP8X4),
                 scales=z_s[b][:, j0:j1],
-                in_=z_bf[:].rearrange("p j t -> p (j t)"),
+                in_=z_bf[b][:, j0:j1, :].rearrange("p j t -> p (j t)"),
+            )
+
+        def score_pass(y, nt, b, cols, start, stop):
+            nc.tensor.matmul_mx(
+                out=y,
+                lhsT=w2_w[:, b, :].bitcast(U8)[:, 2 * P * nt : 2 * P * (nt + 1)].bitcast(FP4X4),
+                lhsT_scale=w2_s[:, b, :].bitcast(U8)[:, P * nt : P * (nt + 1)],
+                rhs=z_c[b][:, cols].bitcast(FP8X4),
+                rhs_scale=z_s[b][:, cols],
+                start=start,
+                stop=stop,
             )
 
         def score(j0):
             y = psum.tile([P, N // P, JB], F32, name="bank")
             cols = slice(j0, j0 + JB)
             for nt in range(N // P):
-                for b in range(R_PASSES):
-                    nc.tensor.matmul_mx(
-                        out=y[:, nt, :],
-                        lhsT=w2_w[:, b, :].bitcast(U8)[:, 2 * P * nt : 2 * P * (nt + 1)].bitcast(FP4X4),
-                        lhsT_scale=w2_s[:, b, :].bitcast(U8)[:, P * nt : P * (nt + 1)],
-                        rhs=z_c[b][:, cols].bitcast(FP8X4),
-                        rhs_scale=z_s[b][:, cols],
-                        start=(b == 0),
-                        stop=(b == R_PASSES - 1),
-                    )
+                for b in (1, 0):
+                    score_pass(y[:, nt, :], nt, b, cols, b == 1, b == 0)
             o = keep.tile([P, N // P, JB], F32, name="o%d" % j0)
-            nc.scalar.activation(o[:], y[:], ACT.Tanh, scale=0.5)
-            nc.vector.tensor_scalar(o[:], o[:], 0.5, 0.5, ALU.mult, ALU.add)
+            nc.scalar.activation(o[:], y[:], ACT.Sigmoid)
             nc.sync.dma_start(out[:, cols].rearrange("(nt p) j -> p nt j", p=P), o[:])
 
-        similarity(0, 0, PAIRS, 2)
-        for j0, j1, t_step in ((0, 256, 2), (256, 384, 2), (384, 512, 1)):
-            similarity(1, j0, j1, t_step)
-            for j in range(j0, j1, JB):
-                score(j)
+        drain_h(0, 0, (1,))
+        drain_h(0, 1, ())
+        for t in range(PACK):
+            src = raw[(0, 1, 0)][:].rearrange("p j (m t) -> p t m j", t=PACK)[:, t, :, :]
+            for m0 in range(0, 80, 80 // 1):
+                nc.gpsimd.tensor_scalar(w_bf[(0, 1)][:, t, m0 : m0 + 80 // 1, :], src[:, m0 : m0 + 80 // 1, :], 1.0, 0.0, ALU.mult, ALU.add)
+        round_w1("scalar", 0, 1, 0, 80, P)
+        drain_h(0, 2, ())
+        drain_h(0, 3, ())
+        pick_both(0, 0)
+        pick_both(0, 1)
+        quant_w1(0, 1, 0, PACK)
+        for t in range(PACK):
+            embed_pass(0, 1, t)
+        subtract(0, 1, nc.gpsimd)
+        subtract(0, 0, nc.gpsimd)
+        pick_both(0, 2)
+        round_w1("scalar", 1, 1, 0, 0, P)
+        quant_w1(1, 1, 0, PACK, "h0_2")
+        subtract(0, 2, nc.gpsimd)
+        pick(0, 3, 0)
+        round_w1("scalar", 2, 1, 0, 0, P)
+        quant_w1(2, 1, 0, PACK)
+        for t in range(PACK):
+            embed_pass(1, 1, t)
+            embed_pass(2, 1, t)
+        pick(0, 3, 1)
+        subtract(0, 3, nc.gpsimd)
+        drain_h(1, 0, ())
+        drain_h(1, 1, ())
+        closeness(0, 0, 2, 0, PAIRS)
+        closeness(0, 2, 4, 0, PAIRS)
+        for t in range(PACK):
+            weigh_plane(t)
+        drain_h(1, 2, ())
+        drain_h(1, 3, ())
+        for t in range(PACK):
+            pick_both(1, t)
+            subtract(1, t, nc.gpsimd if t < 3 else nc.vector)
+        closeness(1, 0, 2, 0, PAIRS)
+        closeness(1, 2, 3, 0, PAIRS)
+        closeness(1, 3, 4, 0, PAIRS // 2)
+        closeness(1, 3, 4, PAIRS // 2, PAIRS)
+        z_bf[0] = keep.tile([P, PAIRS, PACK], BF16, name="z_bf0", tag="h1_3", align_bytes=64)
+        interleave(0, PAIRS)
+        quant_z(0, 0, PAIRS)
+        spare = psum.tile([P, BANK], F32, name="bank")
+        for nt in range(4):
+            score_pass(spare[:], nt, 0, slice(0, PAIRS), True, True)
+        for j0 in range(0, PAIRS, JB):
+            weigh(1, j0, j0 + JB)
+            quant_z(1, j0, j0 + JB)
+            score(j0)

@@ -1,6 +1,7 @@
 from contextlib import ExitStack
 
 import concourse.mybir as mybir
+from concourse.masks import make_identity
 
 K, T, S, PAIRS, H, N = 1536, 2048, 1024, 512, 1024, 512
 FLOPS = 2 * K * H * S + 2 * H * N * PAIRS
@@ -29,7 +30,7 @@ def tile_list_duplicate_pair_score_kernel(tc, tab_words, tab_scales, offs, w1, p
     nc = tc.nc
     with ExitStack() as ctx:
         keep = ctx.enter_context(tc.tile_pool(name="keep", bufs=1))
-        psum = ctx.enter_context(tc.psum_pool(name="psum", bufs=8))
+        psum = ctx.enter_context(tc.psum_pool(name="psum", bufs=1))
 
         offs_sb = keep.tile([P, S // 16], U16, name="offs_sb")
         pos_sb = [keep.tile([P, PAIRS // 16], U16, name="pos_sb%d" % i) for i in range(2)]
@@ -49,6 +50,10 @@ def tile_list_duplicate_pair_score_kernel(tc, tab_words, tab_scales, offs, w1, p
         nc.gpsimd.memset(warm[:, 0:1], 0.0)
         nc.scalar.activation(warm[:, 1:2], warm[:, 0:1], ACT.Exp)
         nc.gpsimd.memset(w2_s[:], 0)
+        ident = keep.tile([P, P], F32, name="ident")
+        make_identity(nc, ident[:])
+        minus_one = keep.tile([P, PAIRS], F32, name="minus_one")
+        nc.gpsimd.memset(minus_one[:], -1.0)
 
         raw = {}
 
@@ -118,7 +123,7 @@ def tile_list_duplicate_pair_score_kernel(tc, tab_words, tab_scales, offs, w1, p
         def embed_pass(a, b, t):
             for half in range(S // BANK):
                 if a == 0:
-                    acc[(b, t, half)] = psum.tile([P, BANK], F32, name="bank")
+                    acc[(b, t, half)] = psum.tile([P, BANK], F32, name="acc", tag="bank%d" % (2 * (t if b == 0 else t % 2) + half))
                 cols = slice(BANK * half, BANK * (half + 1))
                 nc.tensor.matmul_mx(
                     out=acc[(b, t, half)][:],
@@ -150,8 +155,8 @@ def tile_list_duplicate_pair_score_kernel(tc, tab_words, tab_scales, offs, w1, p
         for t in range(PACK):
             embed_pass(0, 0, t)
         gather_tab(2)
-        round_w1("scalar", 1, 0, 0, 0, 80)
-        round_w1("vector", 1, 0, 0, 80, 128)
+        round_w1("scalar", 1, 0, 0, 0, 72)
+        round_w1("vector", 1, 0, 0, 72, 128)
         quant_w1(1, 0, 0, PACK)
         for t in range(PACK):
             embed_pass(1, 0, t)
@@ -163,33 +168,38 @@ def tile_list_duplicate_pair_score_kernel(tc, tab_words, tab_scales, offs, w1, p
             embed_pass(2, 0, t)
         z_c = [keep.tile([P, PAIRS], U32, name="z_c%d" % b, align_bytes=64) for b in range(R_PASSES)]
         z_s = [keep.tile([P, PAIRS], U8, name="z_s%d" % b, align_bytes=64) for b in range(R_PASSES)]
-        z_bf = {1: keep.tile([P, PAIRS, PACK], BF16, name="z_bf1", align_bytes=64)}
         diff = {}
-        GROUPS = (((0, 2), (2, 4)), ((0, 2), (2, 3), (3, 4)))
+        GROUPS = ((), ((2, 3), (3, 4)))
         sim = [keep.tile([P, PACK, PAIRS], F32, name="sim%d" % b, tag="sim%d" % b, align_bytes=64) for b in range(R_PASSES)]
-        z_planes = keep.tile([P, PACK, PAIRS], BF16, name="z_planes")
-        SH = {"pick0_2":"w_bf0_1","pick0_3_0":"w_bf1_1","pick0_3_1":"w_bf2_1","dist0_0_0":"w1_raw2_1_0","dist0_2_0":"w_c2_1","diff0_0":"w1_raw0_1_0","pick1_0":"w_bf0_0","pick1_1":"w_bf1_0","pick1_2":"w_bf2_0","pick1_3":"w1_raw2_0_0","diff0_2":"w1_raw2_0_64","diff1_0":"w1_raw0_0_0","dist1_0_0":"w1_raw1_0_0"}
+        SH = {"pick0_2":"w_bf0_1","pick0_3_0":"w_bf1_1","pick0_3_1":"w_bf2_1","pick1_0":"w_bf0_0","pick1_1":"w_bf1_0","pick1_2":"w_bf2_0","pick1_3":"w1_raw2_0_0","dist1_2_0":"dist1_1","dist1_3_0":"dist1_1"}
 
         picked = {}
+        ON_VECTOR = ((1,2),(1,3))
 
         def pick(b, t, side):
             key = "pick%d_%d_%d" % (b, t, side)
             picked[(b, t, side)] = keep.tile([P, PAIRS], F32, name=key, tag=SH.get(key, key), align_bytes=64)
-            nc.vector.tensor_copy(picked[(b, t, side)][:], h[(b, t)][:].indirect(pos_sb[side][:]))
+            if side == 0 or (b, t) in ON_VECTOR:
+                nc.vector.tensor_copy(picked[(b, t, side)][:], h[(b, t)][:].indirect(pos_sb[side][:]))
+            else:
+                nc.vector.tensor_tensor(picked[(b, t, side)][:], h[(b, t)][:].indirect(pos_sb[side][:]), minus_one[:], ALU.mult)
 
         def pick_both(b, t):
             key = "pick%d_%d" % (b, t)
             both = keep.tile([P, 2, PAIRS], F32, name=key, tag=SH.get(key, key), align_bytes=64)
             for side in range(2):
                 picked[(b, t, side)] = both[:, side, :]
-                nc.vector.tensor_copy(both[:, side, :], h[(b, t)][:].indirect(pos_sb[side][:]))
+                if side == 0 or (b, t) in ON_VECTOR:
+                    nc.vector.tensor_copy(both[:, side, :], h[(b, t)][:].indirect(pos_sb[side][:]))
+                else:
+                    nc.vector.tensor_tensor(both[:, side, :], h[(b, t)][:].indirect(pos_sb[side][:]), minus_one[:], ALU.mult)
 
         def subtract(b, t, engine):
             t0, t1 = [g for g in GROUPS[b] if g[0] <= t < g[1]][0]
             if (b, t0) not in diff:
                 key = "diff%d_%d" % (b, t0)
                 diff[(b, t0)] = keep.tile([P, t1 - t0, PAIRS], F32, name=key, tag=SH.get(key, key), align_bytes=64)
-            step = PAIRS // 1 if engine is nc.gpsimd else PAIRS // 2
+            step = PAIRS
             for j0 in range(0, PAIRS, step):
                 engine.tensor_tensor(diff[(b, t0)][:, t - t0, j0 : j0 + step], picked[(b, t, 0)][:, j0 : j0 + step], picked[(b, t, 1)][:, j0 : j0 + step], ALU.subtract)
 
@@ -199,28 +209,41 @@ def tile_list_duplicate_pair_score_kernel(tc, tab_words, tab_scales, offs, w1, p
             nc.scalar.activation(dist[:], diff[(b, t0)][:, :, j0:j1], ACT.Abs)
             nc.scalar.activation(sim[b][:, t0:t1, j0:j1], dist[:], ACT.Exp, scale=-1.0)
 
-        def weigh(b, j0, j1):
+        dists = {}
+
+        def turn(b, t, bank):
+            turned = psum.tile([P, PAIRS // P, P], F32, name="turned", tag="bank%d" % bank)
+            for c in range(PAIRS // P):
+                for side in range(2):
+                    nc.tensor.matmul(turned[:, c, :], picked[(b, t, side)][:, P * c : P * (c + 1)], ident[:], start=(side == 0), stop=(side == 1), is_transpose=True)
+            if b == 0:
+                if 0 not in dists:
+                    dists[0] = keep.tile([P, PACK, PAIRS // P, P], F32, name="dist0", tag="w1_raw2_1_0", align_bytes=64)
+                dists[(b, t)] = dists[0][:, t]
+            else:
+                dists[(b, t)] = keep.tile([P, PAIRS // P, P], F32, name="dist1_%d" % t, tag=SH.get("dist1_%d" % t, "dist1_%d" % t), align_bytes=64)[:]
+            nc.scalar.activation(dists[(b, t)], turned[:], ACT.Abs)
+
+        def turn_back(b, t, bank):
+            back = psum.tile([P, PAIRS // P, P], F32, name="back", tag="bank%d" % bank)
+            for c in range(PAIRS // P):
+                nc.tensor.transpose(back[:, c, :], dists[(b, t)][:, c, :], ident[:])
+            nc.scalar.activation(sim[b][:, t, :], back[:].rearrange("p c j -> p (c j)"), ACT.Exp, scale=-1.0)
+
+        def weigh(b, j0, z_bf):
             nc.vector.tensor_tensor(
-                z_bf[b][:, j0:j1, :].rearrange("p (c i) t -> p c t i", i=4),
-                sim[b][:, :, j0:j1].rearrange("p t (c i) -> p c t i", i=4),
-                gain_sb[:, b, :].unsqueeze(1).unsqueeze(3).to_broadcast([P, (j1 - j0) // 4, PACK, 4]),
+                z_bf.rearrange("p (c i) t -> p c t i", i=4),
+                sim[b][:, :, j0 : j0 + JB].rearrange("p t (c i) -> p c t i", i=4),
+                gain_sb[:, b, :].unsqueeze(1).unsqueeze(3).to_broadcast([P, JB // 4, PACK, 4]),
                 ALU.mult,
             )
 
-        def weigh_plane(t):
-            nc.gpsimd.tensor_scalar(z_planes[:, t, :], sim[0][:, t, :], gain_sb[:, 0, t : t + 1], 0.0, ALU.mult, ALU.add)
-
-        def interleave(j0, j1):
-            nc.vector.tensor_copy(
-                z_bf[0][:, j0:j1, :].rearrange("p (c i) t -> p c t i", i=4),
-                z_planes[:, :, j0:j1].rearrange("p t (c i) -> p c t i", i=4),
-            )
-
-        def quant_z(b, j0, j1):
+        def quant_z(b, j0, z_bf):
+            cols = slice(j0, j0 + z_bf.shape[1])
             nc.vector.quantize_mx(
-                out=z_c[b][:, j0:j1].bitcast(FP8X4),
-                scales=z_s[b][:, j0:j1],
-                in_=z_bf[b][:, j0:j1, :].rearrange("p j t -> p (j t)"),
+                out=z_c[b][:, cols].bitcast(FP8X4),
+                scales=z_s[b][:, cols],
+                in_=z_bf.rearrange("p j t -> p (j t)"),
             )
 
         def score_pass(y, nt, b, cols, start, stop):
@@ -235,7 +258,7 @@ def tile_list_duplicate_pair_score_kernel(tc, tab_words, tab_scales, offs, w1, p
             )
 
         def score(j0):
-            y = psum.tile([P, N // P, JB], F32, name="bank")
+            y = psum.tile([P, N // P, JB], F32, name="y", tag="bank%d" % (1, 3, 7, 6)[j0 // JB])
             cols = slice(j0, j0 + JB)
             for nt in range(N // P):
                 for b in (1, 0):
@@ -246,54 +269,65 @@ def tile_list_duplicate_pair_score_kernel(tc, tab_words, tab_scales, offs, w1, p
 
         drain_h(0, 0, (1,))
         drain_h(0, 1, ())
-        for t in range(PACK):
-            src = raw[(0, 1, 0)][:].rearrange("p j (m t) -> p t m j", t=PACK)[:, t, :, :]
-            for m0 in range(0, 80, 80 // 1):
-                nc.gpsimd.tensor_scalar(w_bf[(0, 1)][:, t, m0 : m0 + 80 // 1, :], src[:, m0 : m0 + 80 // 1, :], 1.0, 0.0, ALU.mult, ALU.add)
-        round_w1("scalar", 0, 1, 0, 80, P)
+        round_w1("scalar", 0, 1, 0, 0, P)
         drain_h(0, 2, ())
-        drain_h(0, 3, ())
         pick_both(0, 0)
         pick_both(0, 1)
         quant_w1(0, 1, 0, PACK)
-        for t in range(PACK):
+        for t in range(2):
             embed_pass(0, 1, t)
-        subtract(0, 1, nc.gpsimd)
-        subtract(0, 0, nc.gpsimd)
         pick_both(0, 2)
         round_w1("scalar", 1, 1, 0, 0, P)
+        drain_h(0, 3, ())
         quant_w1(1, 1, 0, PACK, "h0_2")
-        subtract(0, 2, nc.gpsimd)
-        pick(0, 3, 0)
-        round_w1("scalar", 2, 1, 0, 0, P)
-        quant_w1(2, 1, 0, PACK)
-        for t in range(PACK):
+        for t in range(2):
             embed_pass(1, 1, t)
+        round_w1("scalar", 2, 1, 0, 0, 96)
+        round_w1("vector", 2, 1, 0, 96, P)
+        pick(0, 3, 0)
+        quant_w1(2, 1, 0, PACK)
+        for t in range(2):
             embed_pass(2, 1, t)
         pick(0, 3, 1)
-        subtract(0, 3, nc.gpsimd)
-        drain_h(1, 0, ())
+        drain_h(1, 0, (1,))
         drain_h(1, 1, ())
-        closeness(0, 0, 2, 0, PAIRS)
-        closeness(0, 2, 4, 0, PAIRS)
         for t in range(PACK):
-            weigh_plane(t)
-        drain_h(1, 2, ())
-        drain_h(1, 3, ())
+            turn(0, t, 4 + t)
+        for t in range(2, PACK):
+            for a in range(K_PASSES):
+                embed_pass(a, 1, t)
+            drain_h(1, t, ())
         for t in range(PACK):
-            pick_both(1, t)
-            subtract(1, t, nc.gpsimd if t < 3 else nc.vector)
-        closeness(1, 0, 2, 0, PAIRS)
+            turn_back(0, t, 4 + t)
+        pick_both(1, 0)
+        turn(1, 0, 0)
+        pick_both(1, 1)
+        turn(1, 1, 2)
+        turn_back(1, 0, 4)
+        turn_back(1, 1, 5)
+        pick_both(1, 2)
+        subtract(1, 2, nc.vector)
         closeness(1, 2, 3, 0, PAIRS)
-        closeness(1, 3, 4, 0, PAIRS // 2)
-        closeness(1, 3, 4, PAIRS // 2, PAIRS)
-        z_bf[0] = keep.tile([P, PAIRS, PACK], BF16, name="z_bf0", tag="h1_3", align_bytes=64)
-        interleave(0, PAIRS)
-        quant_z(0, 0, PAIRS)
-        spare = psum.tile([P, BANK], F32, name="bank")
-        for nt in range(4):
-            score_pass(spare[:], nt, 0, slice(0, PAIRS), True, True)
-        for j0 in range(0, PAIRS, JB):
-            weigh(1, j0, j0 + JB)
-            quant_z(1, j0, j0 + JB)
-            score(j0)
+        pick_both(1, 3)
+        subtract(1, 3, nc.vector)
+        closeness(1, 3, 4, 0, PAIRS)
+        z0_front = keep.tile([P, 2 * JB, PACK], BF16, name="z0_front", tag="h1_3", align_bytes=64)
+        z1_front = keep.tile([P, 2 * JB, PACK], BF16, name="z1_front", tag="z1_front", align_bytes=64)
+        for c in range(2):
+            weigh(0, JB * c, z0_front[:, JB * c : JB * (c + 1), :])
+        quant_z(0, 0, z0_front[:])
+        spare = psum.tile([P, 2 * JB], F32, name="spare", tag="bank5")
+        for i in range(6):
+            score_pass(spare[:], i % (N // P), 0, slice(0, 2 * JB), True, True)
+        for c in range(2):
+            weigh(1, JB * c, z1_front[:, JB * c : JB * (c + 1), :])
+            quant_z(1, JB * c, z1_front[:, JB * c : JB * (c + 1), :])
+            score(JB * c)
+        for c, tag in ((2, "w1_raw2_0_0"), (3, "z1_front")):
+            z0 = keep.tile([P, JB, PACK], BF16, name="z0_%d" % c, tag=tag, align_bytes=64)
+            z1 = keep.tile([P, JB, PACK], BF16, name="z1_%d" % c, align_bytes=64)
+            weigh(0, JB * c, z0[:])
+            weigh(1, JB * c, z1[:])
+            quant_z(0, JB * c, z0[:])
+            quant_z(1, JB * c, z1[:])
+            score(JB * c)

@@ -1,7 +1,6 @@
 from contextlib import ExitStack
 
 import concourse.mybir as mybir
-from concourse.masks import make_identity
 
 K, T, S, PAIRS, H, N = 1536, 2048, 1024, 512, 1024, 512
 FLOPS = 2 * K * H * S + 2 * H * N * PAIRS
@@ -50,10 +49,6 @@ def tile_list_duplicate_pair_score_kernel(tc, tab_words, tab_scales, offs, w1, p
         nc.gpsimd.memset(warm[:, 0:1], 0.0)
         nc.scalar.activation(warm[:, 1:2], warm[:, 0:1], ACT.Exp)
         nc.gpsimd.memset(w2_s[:], 0)
-        ident = keep.tile([P, P], F32, name="ident")
-        make_identity(nc, ident[:])
-        minus_one = keep.tile([P, PAIRS], F32, name="minus_one")
-        nc.gpsimd.memset(minus_one[:], -1.0)
 
         raw = {}
 
@@ -123,7 +118,7 @@ def tile_list_duplicate_pair_score_kernel(tc, tab_words, tab_scales, offs, w1, p
         def embed_pass(a, b, t):
             for half in range(S // BANK):
                 if a == 0:
-                    acc[(b, t, half)] = psum.tile([P, BANK], F32, name="acc", tag="bank%d" % (2 * (t if b == 0 else t % 2) + half))
+                    acc[(b, t, half)] = psum.tile([P, BANK], F32, name="acc", tag="bank%d" % (2 * t + half))
                 cols = slice(BANK * half, BANK * (half + 1))
                 nc.tensor.matmul_mx(
                     out=acc[(b, t, half)][:],
@@ -169,30 +164,23 @@ def tile_list_duplicate_pair_score_kernel(tc, tab_words, tab_scales, offs, w1, p
         z_c = [keep.tile([P, PAIRS], U32, name="z_c%d" % b, align_bytes=64) for b in range(R_PASSES)]
         z_s = [keep.tile([P, PAIRS], U8, name="z_s%d" % b, align_bytes=64) for b in range(R_PASSES)]
         diff = {}
-        GROUPS = ((), ((2, 3), (3, 4)))
+        GROUPS = (((0, 2), (2, 4)), ((0, 2), (2, 3), (3, 4)))
         sim = [keep.tile([P, PACK, PAIRS], F32, name="sim%d" % b, tag="sim%d" % b, align_bytes=64) for b in range(R_PASSES)]
-        SH = {"pick0_2":"w_bf0_1","pick0_3_0":"w_bf1_1","pick0_3_1":"w_bf2_1","pick1_0":"w_bf0_0","pick1_1":"w_bf1_0","pick1_2":"w_bf2_0","pick1_3":"w1_raw2_0_0","dist1_2_0":"dist1_1","dist1_3_0":"dist1_1"}
+        SH = {"pick0_2":"w_bf0_1","pick0_3_0":"w_bf1_1","pick1_0":"w_bf0_0","pick1_1":"w_bf1_0","pick1_2":"w_bf2_0","pick1_3":"w1_raw2_0_0","dist0_0_0":"w1_raw2_1_0","dist0_2_0":"w_c2_1","dist1_0_0":"w1_raw2_1_0","dist1_2_0":"w_c2_1","dist1_3_0":"w_c2_1"}
 
         picked = {}
-        ON_VECTOR = ((1,2),(1,3))
 
         def pick(b, t, side):
             key = "pick%d_%d_%d" % (b, t, side)
             picked[(b, t, side)] = keep.tile([P, PAIRS], F32, name=key, tag=SH.get(key, key), align_bytes=64)
-            if side == 0 or (b, t) in ON_VECTOR:
-                nc.vector.tensor_copy(picked[(b, t, side)][:], h[(b, t)][:].indirect(pos_sb[side][:]))
-            else:
-                nc.vector.tensor_tensor(picked[(b, t, side)][:], h[(b, t)][:].indirect(pos_sb[side][:]), minus_one[:], ALU.mult)
+            nc.vector.tensor_copy(picked[(b, t, side)][:], h[(b, t)][:].indirect(pos_sb[side][:]))
 
         def pick_both(b, t):
             key = "pick%d_%d" % (b, t)
             both = keep.tile([P, 2, PAIRS], F32, name=key, tag=SH.get(key, key), align_bytes=64)
             for side in range(2):
                 picked[(b, t, side)] = both[:, side, :]
-                if side == 0 or (b, t) in ON_VECTOR:
-                    nc.vector.tensor_copy(both[:, side, :], h[(b, t)][:].indirect(pos_sb[side][:]))
-                else:
-                    nc.vector.tensor_tensor(both[:, side, :], h[(b, t)][:].indirect(pos_sb[side][:]), minus_one[:], ALU.mult)
+                nc.vector.tensor_copy(both[:, side, :], h[(b, t)][:].indirect(pos_sb[side][:]))
 
         def subtract(b, t, engine):
             t0, t1 = [g for g in GROUPS[b] if g[0] <= t < g[1]][0]
@@ -208,27 +196,6 @@ def tile_list_duplicate_pair_score_kernel(tc, tab_words, tab_scales, offs, w1, p
             dist = keep.tile([P, t1 - t0, j1 - j0], F32, name=key, tag=SH.get(key, key), align_bytes=64)
             nc.scalar.activation(dist[:], diff[(b, t0)][:, :, j0:j1], ACT.Abs)
             nc.scalar.activation(sim[b][:, t0:t1, j0:j1], dist[:], ACT.Exp, scale=-1.0)
-
-        dists = {}
-
-        def turn(b, t, bank):
-            turned = psum.tile([P, PAIRS // P, P], F32, name="turned", tag="bank%d" % bank)
-            for c in range(PAIRS // P):
-                for side in range(2):
-                    nc.tensor.matmul(turned[:, c, :], picked[(b, t, side)][:, P * c : P * (c + 1)], ident[:], start=(side == 0), stop=(side == 1), is_transpose=True)
-            if b == 0:
-                if 0 not in dists:
-                    dists[0] = keep.tile([P, PACK, PAIRS // P, P], F32, name="dist0", tag="w1_raw2_1_0", align_bytes=64)
-                dists[(b, t)] = dists[0][:, t]
-            else:
-                dists[(b, t)] = keep.tile([P, PAIRS // P, P], F32, name="dist1_%d" % t, tag=SH.get("dist1_%d" % t, "dist1_%d" % t), align_bytes=64)[:]
-            nc.scalar.activation(dists[(b, t)], turned[:], ACT.Abs)
-
-        def turn_back(b, t, bank):
-            back = psum.tile([P, PAIRS // P, P], F32, name="back", tag="bank%d" % bank)
-            for c in range(PAIRS // P):
-                nc.tensor.transpose(back[:, c, :], dists[(b, t)][:, c, :], ident[:])
-            nc.scalar.activation(sim[b][:, t, :], back[:].rearrange("p c j -> p (c j)"), ACT.Exp, scale=-1.0)
 
         def weigh(b, j0, z_bf):
             nc.vector.tensor_tensor(
@@ -258,14 +225,16 @@ def tile_list_duplicate_pair_score_kernel(tc, tab_words, tab_scales, offs, w1, p
             )
 
         def score(j0):
-            y = psum.tile([P, N // P, JB], F32, name="y", tag="bank%d" % (1, 3, 7, 6)[j0 // JB])
+            y = psum.tile([P, N // P, JB], F32, name="y", tag="bank%d" % (0, 1, 2, 3)[j0 // JB])
             cols = slice(j0, j0 + JB)
             for nt in range(N // P):
                 for b in (1, 0):
                     score_pass(y[:, nt, :], nt, b, cols, b == 1, b == 0)
             o = keep.tile([P, N // P, JB], F32, name="o%d" % j0)
-            nc.scalar.activation(o[:], y[:], ACT.Sigmoid)
-            nc.sync.dma_start(out[:, cols].rearrange("(nt p) j -> p nt j", p=P), o[:])
+            step = 2 if j0 == PAIRS - JB else N // P
+            for n0 in range(0, N // P, step):
+                nc.scalar.activation(o[:, n0 : n0 + step, :], y[:, n0 : n0 + step, :], ACT.Sigmoid)
+                nc.sync.dma_start(out[P * n0 : P * (n0 + step), cols].rearrange("(nt p) j -> p nt j", p=P), o[:, n0 : n0 + step, :])
 
         drain_h(0, 0, (1,))
         drain_h(0, 1, ())
@@ -274,39 +243,39 @@ def tile_list_duplicate_pair_score_kernel(tc, tab_words, tab_scales, offs, w1, p
         pick_both(0, 0)
         pick_both(0, 1)
         quant_w1(0, 1, 0, PACK)
-        for t in range(2):
-            embed_pass(0, 1, t)
         pick_both(0, 2)
         round_w1("scalar", 1, 1, 0, 0, P)
         drain_h(0, 3, ())
+        for t in range(PACK):
+            embed_pass(0, 1, t)
         quant_w1(1, 1, 0, PACK, "h0_2")
-        for t in range(2):
-            embed_pass(1, 1, t)
         round_w1("scalar", 2, 1, 0, 0, 96)
         round_w1("vector", 2, 1, 0, 96, P)
         pick(0, 3, 0)
         quant_w1(2, 1, 0, PACK)
-        for t in range(2):
+        for t in range(PACK):
+            embed_pass(1, 1, t)
             embed_pass(2, 1, t)
-        pick(0, 3, 1)
+        late = keep.tile([P, 1 + PACK, PAIRS], F32, name="late", tag="w_bf2_1", align_bytes=64)
+        picked[(0, 3, 1)] = late[:, 0, :]
+        nc.vector.tensor_copy(late[:, 0, :], h[(0, 3)][:].indirect(pos_sb[1][:]))
+        diff[(0, 0)] = late[:, 1:3, :]
+        diff[(0, 2)] = late[:, 3:5, :]
+        for t in range(PACK):
+            subtract(0, t, nc.gpsimd)
         drain_h(1, 0, (1,))
         drain_h(1, 1, ())
-        for t in range(PACK):
-            turn(0, t, 4 + t)
-        for t in range(2, PACK):
-            for a in range(K_PASSES):
-                embed_pass(a, 1, t)
-            drain_h(1, t, ())
-        for t in range(PACK):
-            turn_back(0, t, 4 + t)
+        drain_h(1, 2, ())
+        drain_h(1, 3, ())
+        closeness(0, 0, 2, 0, PAIRS)
+        closeness(0, 2, 4, 0, PAIRS)
         pick_both(1, 0)
-        turn(1, 0, 0)
+        subtract(1, 0, nc.gpsimd)
         pick_both(1, 1)
-        turn(1, 1, 2)
-        turn_back(1, 0, 4)
-        turn_back(1, 1, 5)
+        subtract(1, 1, nc.gpsimd)
+        closeness(1, 0, 2, 0, PAIRS)
         pick_both(1, 2)
-        subtract(1, 2, nc.vector)
+        subtract(1, 2, nc.gpsimd)
         closeness(1, 2, 3, 0, PAIRS)
         pick_both(1, 3)
         subtract(1, 3, nc.vector)

@@ -1,6 +1,7 @@
 from contextlib import ExitStack
 
 import concourse.mybir as mybir
+from concourse.masks import make_identity
 
 K, T, S, PAIRS, H, N = 1536, 2048, 1024, 512, 1024, 512
 FLOPS = 2 * K * H * S + 2 * H * N * PAIRS
@@ -31,24 +32,34 @@ def tile_list_duplicate_pair_score_kernel(tc, tab_words, tab_scales, offs, w1, p
         keep = ctx.enter_context(tc.tile_pool(name="keep", bufs=1))
         psum = ctx.enter_context(tc.psum_pool(name="psum", bufs=1))
 
+        def sb(shape, dtype, name, tag=None):
+            return keep.tile(shape, dtype, name=name, tag=tag or name, align_bytes=64)
+
+        def bank(name, i):
+            return psum.tile([P, BANK], F32, name=name, tag="bank%d" % i)
+
         offs_sb = keep.tile([P, S // 16], U16, name="offs_sb")
         pos_sb = [keep.tile([P, PAIRS // 16], U16, name="pos_sb%d" % i) for i in range(2)]
-        tab_w = [keep.tile([P, T], I32, name="tab_w%d" % a, align_bytes=64) for a in range(K_PASSES)]
-        tab_s = keep.tile([P, T // 4], I32, name="tab_s", align_bytes=64)
-        v_w = [keep.tile([P, S], U32, name="v_w%d" % a, align_bytes=64) for a in range(K_PASSES)]
-        v_s = keep.tile([P, S], U8, name="v_s", align_bytes=64)
-        gain_sb = keep.tile([P, R_PASSES, PACK], F32, name="gain_sb")
-        w2_w = keep.tile([P, R_PASSES, 2 * N // 4], I32, name="w2_w", align_bytes=64)
-        w2_s = keep.tile([P, R_PASSES, N // 4], I32, name="w2_s", align_bytes=64)
-        warm = keep.tile([P, 2], F32, name="warm")
+        tab_w = [sb([P, T], I32, "tab_w%d" % a) for a in range(K_PASSES)]
+        tab_s = sb([P, T // 4], I32, "tab_s")
+        v_w = [sb([P, S], U32, "v_w%d" % a) for a in range(K_PASSES)]
+        v_s = sb([P, S], U8, "v_s")
+        gain_sb = sb([P, R_PASSES, PACK], F32, "gain_sb")
+        w2_w = sb([P, R_PASSES, 2 * N // 4], I32, "w2_w")
+        w2_s = sb([P, R_PASSES, N // 4], I32, "w2_s")
+        warm = sb([P, 2], F32, "warm")
+        ident = sb([P, P], F32, "ident")
+        h = [sb([P, 2 * S], F32, "h%d" % t) for t in range(PACK)]
 
-
-        nc.gpsimd.memset(tab_s[:], 0)
+        nc.vector.memset(tab_s[:], 0)
         for q in range(2):
             nc.scalar.dma_start(tab_s[32 * q : 32 * q + 4 * K_PASSES, :], tab_scales[:, 4 * q : 4 * q + 4, :].bitcast(I32))
         nc.gpsimd.memset(warm[:, 0:1], 0.0)
         nc.scalar.activation(warm[:, 1:2], warm[:, 0:1], ACT.Exp)
         nc.gpsimd.memset(w2_s[:], 0)
+        make_identity(nc, ident[:])
+        for t in range(PACK):
+            nc.gpsimd.memset(h[t][:, S:], 0.0)
 
         raw = {}
 
@@ -56,7 +67,7 @@ def tile_list_duplicate_pair_score_kernel(tc, tab_words, tab_scales, offs, w1, p
             nc.sync.dma_start(tab_w[a][:], tab_words[a].rearrange("p t i -> p (t i)").bitcast(I32))
 
         def load_w1(a, b, m0, m1):
-            t = keep.tile([P, PACK, PACK * (m1 - m0)], F32, name="w1_raw%d_%d_%d" % (a, b, m0), tag="w1_raw%d_%d_%d" % (a, b, m0), align_bytes=64)
+            t = sb([P, PACK, PACK * (m1 - m0)], F32, "raw%d%d_%d" % (a, b, m0))
             cols = slice(K_PASS * b + PACK * m0, K_PASS * b + PACK * m1)
             nc.sync.dma_start(t[:], w1[K_PASS * a : K_PASS * (a + 1), cols].rearrange("(p j) c -> p j c", j=PACK))
             raw[(a, b, m0)] = t
@@ -65,20 +76,21 @@ def tile_list_duplicate_pair_score_kernel(tc, tab_words, tab_scales, offs, w1, p
         load_tab(0)
         for q in range(2, 4):
             nc.sync.dma_start(tab_s[32 * q : 32 * q + 4 * K_PASSES, :], tab_scales[:, 4 * q : 4 * q + 4, :].bitcast(I32))
-        load_w1(0, 0, 0, P)
         load_tab(1)
-        load_w1(1, 0, 0, P)
+        load_w1(0, 0, 0, P)
         load_tab(2)
+        load_w1(1, 0, 0, P)
         load_w1(2, 0, 0, P // 2)
         load_w1(2, 0, P // 2, P)
         nc.sync.dma_start(pos_sb[0][:], pos1)
         nc.sync.dma_start(pos_sb[1][:], pos2)
         load_w1(0, 1, 0, P)
+        load_w1(1, 1, 0, P)
+        load_w1(2, 1, 0, P // 2)
+        load_w1(2, 1, P // 2, P)
         nc.sync.dma_start(gain_sb[:], gain.rearrange("(b p t) -> p b t", b=R_PASSES, t=PACK))
         for q in range(4):
             nc.sync.dma_start(w2_s[32 * q : 32 * q + 4, :, :], w2_scales[:, 4 * q : 4 * q + 4, :].bitcast(I32).rearrange("b r n -> r b n"))
-        load_w1(1, 1, 0, P)
-        load_w1(2, 1, 0, P)
         nc.sync.dma_start(w2_w[:], w2_words.bitcast(I32).rearrange("b p n -> p b n"))
 
         w_bf = {}
@@ -86,39 +98,41 @@ def tile_list_duplicate_pair_score_kernel(tc, tab_words, tab_scales, offs, w1, p
         w_s = {}
         for a in range(K_PASSES):
             for b in range(R_PASSES):
-                w_bf[(a, b)] = keep.tile([P, PACK, P, PACK], BF16, name="w_bf%d_%d" % (a, b), tag="w_bf%d_%d" % (a, b), align_bytes=64)
-                w_s[(a, b)] = keep.tile([P, K_PASS], U8, name="w_s%d_%d" % (a, b), align_bytes=64)
+                w_c[(a, b)] = sb([P, K_PASS], U32, "w_c%d%d" % (a, b))
+                w_s[(a, b)] = sb([P, K_PASS], U8, "w_s%d%d" % (a, b))
+                if (a, b) != (2, 1):
+                    w_bf[(a, b)] = sb([P, PACK * K_PASS], BF16, "w_bf%d%d" % (a, b))[:]
 
         def round_w1(engine, a, b, base, m0, m1):
-            src = raw[(a, b, base)][:, :, PACK * (m0 - base) : PACK * (m1 - base)].rearrange("p j (m t) -> p m j t", t=PACK)
-            dst = w_bf[(a, b)][:, :, m0:m1, :].rearrange("p t m j -> p m j t")
-            if engine == "scalar":
-                nc.scalar.copy(dst, src)
-            elif engine == "vector":
-                nc.vector.tensor_copy(dst, src)
+            src = raw[(a, b, base)][:, :, PACK * (m0 - base) : PACK * (m1 - base)]
+            dst = w_bf[(a, b)].rearrange("p (t m j) -> p t m j", t=PACK, j=PACK)[:, :, m0:m1, :]
+            if engine == "gpsimd":
+                nc.gpsimd.tensor_scalar(dst.rearrange("p t m j -> p m t j"), src.rearrange("p j (m t) -> p m t j", t=PACK), 1.0, 0.0, ALU.mult, ALU.add)
+            elif engine == "scalar":
+                nc.scalar.copy(dst.rearrange("p t m j -> p m j t"), src.rearrange("p j (m t) -> p m j t", t=PACK))
             else:
-                nc.gpsimd.tensor_scalar(dst, src, 1.0, 0.0, ALU.mult, ALU.add)
+                nc.vector.tensor_copy(dst.rearrange("p t m j -> p m j t"), src.rearrange("p j (m t) -> p m j t", t=PACK))
 
-        def quant_w1(a, b, t0, t1, tag=None):
-            if (a, b) not in w_c:
-                key = "w_c%d_%d" % (a, b)
-                w_c[(a, b)] = keep.tile([P, K_PASS], U32, name=key, tag=tag or key, align_bytes=64)
+        def quant_w1(a, b, t0, t1):
             cols = slice(P * t0, P * t1)
             nc.vector.quantize_mx(
                 out=w_c[(a, b)][:, cols].bitcast(FP8X4),
                 scales=w_s[(a, b)][:, cols],
-                in_=w_bf[(a, b)][:, t0:t1, :, :].rearrange("p t m j -> p (t m j)"),
+                in_=w_bf[(a, b)][:, K_PASS * t0 : K_PASS * t1],
             )
 
         def gather_tab(a):
             nc.vector.tensor_copy(v_w[a][:], tab_w[a][:].bitcast(U32).indirect(offs_sb[:]))
 
         acc = {}
+        ACC_BANK = {(0, 0): 0, (0, 1): 2, (0, 2): 4, (0, 3): 6, (1, 0): 0, (1, 1): 2, (1, 2): 4, (1, 3): 0}
+        TURNED_BANK = {(0, 2): 2, (0, 3): 4, (1, 0): 0, (1, 1): 1}
+        BACK_BANK = {(0, 2): 3, (0, 3): 5, (1, 0): 6, (1, 1): 7}
 
-        def embed_pass(a, b, t):
+        def embed_pass(a, b, t, last=K_PASSES - 1):
             for half in range(S // BANK):
                 if a == 0:
-                    acc[(b, t, half)] = psum.tile([P, BANK], F32, name="acc", tag="bank%d" % (2 * t + half))
+                    acc[(b, t, half)] = bank("acc", ACC_BANK[(b, t)] + half)
                 cols = slice(BANK * half, BANK * (half + 1))
                 nc.tensor.matmul_mx(
                     out=acc[(b, t, half)][:],
@@ -127,176 +141,222 @@ def tile_list_duplicate_pair_score_kernel(tc, tab_words, tab_scales, offs, w1, p
                     rhs=v_w[a][:, cols].bitcast(FP8X4),
                     rhs_scale=v_s[4 * a : P, cols],
                     start=(a == 0),
-                    stop=(a == K_PASSES - 1),
+                    stop=(a == last),
                 )
 
-        h = {}
-
-        def drain_h(b, t, vec_halves):
-            h[(b, t)] = keep.tile([P, S], F32, name="h%d_%d" % (b, t), tag="h%d_%d" % (b, t), align_bytes=64)
+        def drain_h(b, t, vec_halves=()):
             for half in range(S // BANK):
-                dst = h[(b, t)][:, BANK * half : BANK * (half + 1)]
+                dst = h[t][:, BANK * half : BANK * (half + 1)]
                 if half in vec_halves:
                     nc.vector.tensor_copy(dst, acc[(b, t, half)][:])
                 else:
                     nc.scalar.copy(dst, acc[(b, t, half)][:])
 
+        turned = {}
+
+        def turn(src, b, t, first):
+            if first:
+                turned[(b, t)] = bank("turned", TURNED_BANK[(b, t)])
+            for c in range(PAIRS // P):
+                cols = slice(P * c, P * (c + 1))
+                nc.tensor.matmul(turned[(b, t)][:, cols], src[:, cols], ident[:], start=first and c == 0, stop=not first and c == PAIRS // P - 1, is_transpose=True)
+
+        def pick(t, side, dst):
+            nc.vector.tensor_copy(dst, h[t][:].indirect(pos_sb[side][:]))
+
+        def pick_first(b, t, dst):
+            pick(t, 0, dst)
+            turn(dst, b, t, True)
+
+        def pick_negated(t, dst):
+            nc.vector.tensor_scalar(dst, h[t][:].indirect(pos_sb[1][:]), -1.0, 0.0, ALU.mult, ALU.add)
+
+        def pick_second(b, t, dst):
+            pick_negated(t, dst)
+            turn(dst, b, t, False)
+
+        back = {}
+
+        def distance(b, t, dist):
+            nc.scalar.activation(dist, turned[(b, t)][:], ACT.Abs)
+            back[(b, t)] = bank("back", BACK_BANK[(b, t)])
+            for c in range(PAIRS // P):
+                cols = slice(P * c, P * (c + 1))
+                nc.tensor.transpose(back[(b, t)][:, cols], dist[:, cols], ident[:])
+
+        def closeness(b, t, dist):
+            nc.scalar.activation(sim[b][t], dist, ACT.Exp, scale=-1.0)
+            nc.gpsimd.tensor_scalar(lanes[b][:, PAIRS * t : PAIRS * (t + 1)], sim[b][t], gain_sb[:, b, t : t + 1], 0.0, ALU.mult, ALU.add)
+
         gather_tab(0)
         nc.vector.tensor_copy(v_s[:], tab_s[:].bitcast(U8).indirect(offs_sb[:]))
         gather_tab(1)
-        round_w1("scalar", 0, 0, 0, 0, 96)
-        round_w1("vector", 0, 0, 0, 96, 128)
+        round_w1("scalar", 0, 0, 0, 0, P)
         quant_w1(0, 0, 0, PACK)
         for t in range(PACK):
             embed_pass(0, 0, t)
         gather_tab(2)
-        round_w1("scalar", 1, 0, 0, 0, 72)
-        round_w1("vector", 1, 0, 0, 72, 128)
+        round_w1("scalar", 1, 0, 0, 0, 80)
+        round_w1("gpsimd", 1, 0, 0, 80, P)
         quant_w1(1, 0, 0, PACK)
-        for t in range(PACK):
-            embed_pass(1, 0, t)
         round_w1("scalar", 2, 0, 0, 0, 64)
         round_w1("scalar", 2, 0, 64, 64, 88)
         round_w1("vector", 2, 0, 64, 88, 128)
         for t in range(PACK):
             quant_w1(2, 0, t, t + 1)
-            embed_pass(2, 0, t)
-        z_c = [keep.tile([P, PAIRS], U32, name="z_c%d" % b, align_bytes=64) for b in range(R_PASSES)]
-        z_s = [keep.tile([P, PAIRS], U8, name="z_s%d" % b, align_bytes=64) for b in range(R_PASSES)]
-        diff = {}
-        GROUPS = (((0, 2), (2, 4)), ((0, 2), (2, 3), (3, 4)))
-        sim = [keep.tile([P, PACK, PAIRS], F32, name="sim%d" % b, tag="sim%d" % b, align_bytes=64) for b in range(R_PASSES)]
-        SH = {"pick0_2":"w_bf0_1","pick0_3_0":"w_bf1_1","pick1_0":"w_bf0_0","pick1_1":"w_bf1_0","pick1_2":"w_bf2_0","pick1_3":"w1_raw2_0_0","dist0_0_0":"w1_raw2_1_0","dist0_2_0":"w_c2_1","dist1_0_0":"w1_raw2_1_0","dist1_2_0":"w_c2_1","dist1_3_0":"w_c2_1"}
-
-        picked = {}
-
-        def pick(b, t, side):
-            key = "pick%d_%d_%d" % (b, t, side)
-            picked[(b, t, side)] = keep.tile([P, PAIRS], F32, name=key, tag=SH.get(key, key), align_bytes=64)
-            nc.vector.tensor_copy(picked[(b, t, side)][:], h[(b, t)][:].indirect(pos_sb[side][:]))
-
-        def pick_both(b, t):
-            key = "pick%d_%d" % (b, t)
-            both = keep.tile([P, 2, PAIRS], F32, name=key, tag=SH.get(key, key), align_bytes=64)
-            for side in range(2):
-                picked[(b, t, side)] = both[:, side, :]
-                nc.vector.tensor_copy(both[:, side, :], h[(b, t)][:].indirect(pos_sb[side][:]))
-
-        def subtract(b, t, engine):
-            t0, t1 = [g for g in GROUPS[b] if g[0] <= t < g[1]][0]
-            if (b, t0) not in diff:
-                key = "diff%d_%d" % (b, t0)
-                diff[(b, t0)] = keep.tile([P, t1 - t0, PAIRS], F32, name=key, tag=SH.get(key, key), align_bytes=64)
-            step = PAIRS
-            for j0 in range(0, PAIRS, step):
-                engine.tensor_tensor(diff[(b, t0)][:, t - t0, j0 : j0 + step], picked[(b, t, 0)][:, j0 : j0 + step], picked[(b, t, 1)][:, j0 : j0 + step], ALU.subtract)
-
-        def closeness(b, t0, t1, j0, j1):
-            key = "dist%d_%d_%d" % (b, t0, j0)
-            dist = keep.tile([P, t1 - t0, j1 - j0], F32, name=key, tag=SH.get(key, key), align_bytes=64)
-            nc.scalar.activation(dist[:], diff[(b, t0)][:, :, j0:j1], ACT.Abs)
-            nc.scalar.activation(sim[b][:, t0:t1, j0:j1], dist[:], ACT.Exp, scale=-1.0)
-
-        def weigh(b, j0, z_bf):
-            nc.vector.tensor_tensor(
-                z_bf.rearrange("p (c i) t -> p c t i", i=4),
-                sim[b][:, :, j0 : j0 + JB].rearrange("p t (c i) -> p c t i", i=4),
-                gain_sb[:, b, :].unsqueeze(1).unsqueeze(3).to_broadcast([P, JB // 4, PACK, 4]),
-                ALU.mult,
-            )
-
-        def quant_z(b, j0, z_bf):
-            cols = slice(j0, j0 + z_bf.shape[1])
-            nc.vector.quantize_mx(
-                out=z_c[b][:, cols].bitcast(FP8X4),
-                scales=z_s[b][:, cols],
-                in_=z_bf.rearrange("p j t -> p (j t)"),
-            )
-
-        def score_pass(y, nt, b, cols, start, stop):
-            nc.tensor.matmul_mx(
-                out=y,
-                lhsT=w2_w[:, b, :].bitcast(U8)[:, 2 * P * nt : 2 * P * (nt + 1)].bitcast(FP4X4),
-                lhsT_scale=w2_s[:, b, :].bitcast(U8)[:, P * nt : P * (nt + 1)],
-                rhs=z_c[b][:, cols].bitcast(FP8X4),
-                rhs_scale=z_s[b][:, cols],
-                start=start,
-                stop=stop,
-            )
-
-        def score(j0):
-            y = psum.tile([P, N // P, JB], F32, name="y", tag="bank%d" % (0, 1, 2, 3)[j0 // JB])
-            cols = slice(j0, j0 + JB)
-            for nt in range(N // P):
-                for b in (1, 0):
-                    score_pass(y[:, nt, :], nt, b, cols, b == 1, b == 0)
-            o = keep.tile([P, N // P, JB], F32, name="o%d" % j0)
-            step = 2 if j0 == PAIRS - JB else N // P
-            for n0 in range(0, N // P, step):
-                nc.scalar.activation(o[:, n0 : n0 + step, :], y[:, n0 : n0 + step, :], ACT.Sigmoid)
-                nc.sync.dma_start(out[P * n0 : P * (n0 + step), cols].rearrange("(nt p) j -> p nt j", p=P), o[:, n0 : n0 + step, :])
+            order = (1, 2) if t < 1 else (2, 1)
+            for a in order:
+                embed_pass(a, 0, t, order[-1])
 
         drain_h(0, 0, (1,))
-        drain_h(0, 1, ())
-        round_w1("scalar", 0, 1, 0, 0, P)
-        drain_h(0, 2, ())
-        pick_both(0, 0)
-        pick_both(0, 1)
-        quant_w1(0, 1, 0, PACK)
-        pick_both(0, 2)
+        drain_h(0, 1)
+        drain_h(0, 2)
+        for m0 in (0, 64):
+            round_w1("gpsimd", 0, 1, 0, m0, m0 + 64)
         round_w1("scalar", 1, 1, 0, 0, P)
-        drain_h(0, 3, ())
-        for t in range(PACK):
-            embed_pass(0, 1, t)
-        quant_w1(1, 1, 0, PACK, "h0_2")
-        round_w1("scalar", 2, 1, 0, 0, 96)
-        round_w1("vector", 2, 1, 0, 96, P)
-        pick(0, 3, 0)
+        pick00 = sb([P, 2, PAIRS], F32, "pick00", "tab_w0")
+        pick(0, 0, pick00[:, 0, :])
+        pick(0, 1, pick00[:, 1, :])
+        pick01 = sb([P, PAIRS], F32, "pick01", "tab_w1")
+        pick(1, 0, pick01[:])
+        early = [sb([P, PAIRS], F32, "early0", "raw01_0"), sb([P, PAIRS], F32, "early1", "raw21_0")]
+        nc.gpsimd.tensor_tensor(early[0][:], pick00[:, 0, :], pick00[:, 1, :], ALU.subtract)
+        quant_w1(0, 1, 0, PACK)
+        embed_pass(0, 1, 0)
+        embed_pass(0, 1, 1)
+        mid = sb([P, 3 * PAIRS], F32, "mid", "w_bf01")
+        w_bf[(2, 1)] = mid[:, : 2 * PAIRS].bitcast(BF16)
+        round_w1("gpsimd", 2, 1, 0, 0, 64)
+        round_w1("scalar", 2, 1, 64, 64, P)
+        drain_h(0, 3)
+        pick(1, 1, mid[:, 2 * PAIRS :])
+        nc.gpsimd.tensor_tensor(early[1][:], pick01[:], mid[:, 2 * PAIRS :], ALU.subtract)
+        quant_w1(1, 1, 0, PACK)
+        embed_pass(1, 1, 0)
+        embed_pass(1, 1, 1)
+        pick02 = sb([P, PAIRS], F32, "pick02", "w_bf11")
+        sim0 = sb([P, PACK, PAIRS], F32, "sim0", "raw11_0")
+        sim1 = sb([P, PACK - 1, PAIRS], F32, "sim1", "tab_w2")
+        sim = [[sim0[:, t, :] for t in range(PACK)], [sb([P, PAIRS], F32, "sim10")[:]] + [sim1[:, t, :] for t in range(PACK - 1)]]
+        dist_a = sb([P, 3, PAIRS], F32, "dist_a", "raw21_64")
+        for t in range(2):
+            nc.scalar.activation(dist_a[:, t, :], early[t][:], ACT.Abs)
+        pick(2, 0, pick02[:])
         quant_w1(2, 1, 0, PACK)
-        for t in range(PACK):
-            embed_pass(1, 1, t)
-            embed_pass(2, 1, t)
-        late = keep.tile([P, 1 + PACK, PAIRS], F32, name="late", tag="w_bf2_1", align_bytes=64)
-        picked[(0, 3, 1)] = late[:, 0, :]
-        nc.vector.tensor_copy(late[:, 0, :], h[(0, 3)][:].indirect(pos_sb[1][:]))
-        diff[(0, 0)] = late[:, 1:3, :]
-        diff[(0, 2)] = late[:, 3:5, :]
-        for t in range(PACK):
-            subtract(0, t, nc.gpsimd)
-        drain_h(1, 0, (1,))
-        drain_h(1, 1, ())
-        drain_h(1, 2, ())
-        drain_h(1, 3, ())
-        closeness(0, 0, 2, 0, PAIRS)
-        closeness(0, 2, 4, 0, PAIRS)
-        pick_both(1, 0)
-        subtract(1, 0, nc.gpsimd)
-        pick_both(1, 1)
-        subtract(1, 1, nc.gpsimd)
-        closeness(1, 0, 2, 0, PAIRS)
-        pick_both(1, 2)
-        subtract(1, 2, nc.gpsimd)
-        closeness(1, 2, 3, 0, PAIRS)
-        pick_both(1, 3)
-        subtract(1, 3, nc.vector)
-        closeness(1, 3, 4, 0, PAIRS)
-        z0_front = keep.tile([P, 2 * JB, PACK], BF16, name="z0_front", tag="h1_3", align_bytes=64)
-        z1_front = keep.tile([P, 2 * JB, PACK], BF16, name="z1_front", tag="z1_front", align_bytes=64)
-        for c in range(2):
-            weigh(0, JB * c, z0_front[:, JB * c : JB * (c + 1), :])
-        quant_z(0, 0, z0_front[:])
-        spare = psum.tile([P, 2 * JB], F32, name="spare", tag="bank5")
-        for i in range(6):
-            score_pass(spare[:], i % (N // P), 0, slice(0, 2 * JB), True, True)
-        for c in range(2):
-            weigh(1, JB * c, z1_front[:, JB * c : JB * (c + 1), :])
-            quant_z(1, JB * c, z1_front[:, JB * c : JB * (c + 1), :])
-            score(JB * c)
-        for c, tag in ((2, "w1_raw2_0_0"), (3, "z1_front")):
-            z0 = keep.tile([P, JB, PACK], BF16, name="z0_%d" % c, tag=tag, align_bytes=64)
-            z1 = keep.tile([P, JB, PACK], BF16, name="z1_%d" % c, align_bytes=64)
-            weigh(0, JB * c, z0[:])
-            weigh(1, JB * c, z1[:])
-            quant_z(0, JB * c, z0[:])
-            quant_z(1, JB * c, z1[:])
-            score(JB * c)
+        embed_pass(2, 1, 0)
+        embed_pass(2, 1, 1)
+        late = sb([P, 5 * PAIRS], F32, "late", "w_bf01")
+        lanes = [late[:, 3 * PAIRS :].bitcast(BF16)]
+        closeness(0, 0, dist_a[:, 0, :])
+        closeness(0, 1, dist_a[:, 1, :])
+        for a in range(K_PASSES):
+            embed_pass(a, 1, 2)
+        pick_negated(2, late[:, :PAIRS])
+        pick(3, 0, late[:, PAIRS : 2 * PAIRS])
+        pick_negated(3, late[:, 2 * PAIRS : 3 * PAIRS])
+        drain_h(1, 0)
+        for a in range(K_PASSES):
+            embed_pass(a, 1, 3)
+        drain_h(1, 1)
+        turn(pick02[:], 0, 2, True)
+        turn(late[:, :PAIRS], 0, 2, False)
+        distance(0, 2, dist_a[:, 2, :])
+        drain_h(1, 2)
+        closeness(0, 2, back[(0, 2)][:])
+        turn(late[:, PAIRS : 2 * PAIRS], 0, 3, True)
+        turn(late[:, 2 * PAIRS : 3 * PAIRS], 0, 3, False)
+        distance(0, 3, sb([P, PAIRS], F32, "dist03", "dist")[:])
+        drain_h(1, 3)
+        closeness(0, 3, back[(0, 3)][:])
+        z0 = sb([P, PAIRS, PACK], BF16, "z0", "raw20_64")
+        for j0 in (0, PAIRS // 2):
+            cols = slice(j0, j0 + PAIRS // 2)
+            nc.gpsimd.tensor_scalar(z0[:, cols, :], lanes[0].rearrange("p (t j) -> p j t", t=PACK)[:, cols, :], 1.0, 0.0, ALU.mult, ALU.add)
+        for t, tag in enumerate(("raw00_0", "raw10_0")):
+            both = sb([P, 2, PAIRS], F32, "pick1%d" % t, tag)
+            pick_first(1, t, both[:, 0, :])
+            pick_second(1, t, both[:, 1, :])
+            distance(1, t, sb([P, PAIRS], F32, "dist1%d" % t, ("dist_other", "dist")[t])[:])
+
+        halves = [slice(0, PAIRS // 2), slice(PAIRS // 2, PAIRS)]
+        both = sb([P, 2, PAIRS], F32, "pick12", "w_bf00")
+        last = sb([P, 2, PAIRS], F32, "last", "w_bf10")
+        diff = sb([P, 2, PAIRS], F32, "diff", "w_bf01")
+        dist_c = sb([P, 2, PAIRS], F32, "dist_c", "dist")
+        for side in range(2):
+            pick(2, side, both[:, side, :])
+        for cols in halves:
+            nc.gpsimd.tensor_tensor(diff[:, 0, cols], both[:, 0, cols], both[:, 1, cols], ALU.subtract)
+        lanes.append(sb([P, PACK * PAIRS], BF16, "lanes1", "w_bf00")[:])
+        closeness(1, 0, back[(1, 0)][:])
+        nc.scalar.activation(sim[1][1], back[(1, 1)][:], ACT.Exp, scale=-1.0)
+        for cols in halves:
+            nc.scalar.activation(dist_c[:, 0, cols], diff[:, 0, cols], ACT.Abs)
+            nc.scalar.activation(sim[1][2][:, cols], dist_c[:, 0, cols], ACT.Exp, scale=-1.0)
+        for side in range(2):
+            pick(3, side, last[:, side, :])
+        for cols in halves:
+            nc.vector.tensor_tensor(diff[:, 1, cols], last[:, 0, cols], last[:, 1, cols], ALU.subtract)
+            nc.scalar.activation(dist_c[:, 1, cols], diff[:, 1, cols], ACT.Abs)
+            nc.scalar.activation(sim[1][3][:, cols], dist_c[:, 1, cols], ACT.Exp, scale=-1.0)
+
+        z_c = [sb([P, PAIRS], U32, "z_c0", "h3"), sb([P, PAIRS], U32, "z_c1")]
+        z_s = [sb([P, PAIRS], U8, "z_s%d" % b) for b in range(R_PASSES)]
+        z1 = sb([P, PAIRS, PACK], BF16, "z1")
+
+        def quant_z(b, z_bf, cols):
+            nc.vector.quantize_mx(out=z_c[b][:, cols].bitcast(FP8X4), scales=z_s[b][:, cols], in_=z_bf[:, cols, :].rearrange("p j t -> p (j t)"))
+
+        y = [psum.tile([P, N // P, JB], F32, name="y", tag="bank%d" % (4 + c)) for c in range(PAIRS // JB)]
+
+        def score(b, c):
+            cols = slice(JB * c, JB * (c + 1))
+            for nt in range(N // P):
+                nc.tensor.matmul_mx(
+                    out=y[c][:, nt, :],
+                    lhsT=w2_w[:, b, :].bitcast(U8)[:, 2 * P * nt : 2 * P * (nt + 1)].bitcast(FP4X4),
+                    lhsT_scale=w2_s[:, b, :].bitcast(U8)[:, P * nt : P * (nt + 1)],
+                    rhs=z_c[b][:, cols].bitcast(FP8X4),
+                    rhs_scale=z_s[b][:, cols],
+                    start=(b == 0 and nt == 0),
+                    stop=(b == 1 and nt == N // P - 1),
+                )
+
+        def finish(c):
+            cols = slice(JB * c, JB * (c + 1))
+            o = sb([P, N // P, JB], F32, "o%d" % c)
+            step = 2 if c == PAIRS // JB - 1 else N // P
+            for n0 in range(0, N // P, step):
+                nc.scalar.activation(o[:, n0 : n0 + step, :], y[c][:, n0 : n0 + step, :], ACT.Sigmoid)
+                nc.sync.dma_start(out[P * n0 : P * (n0 + step), cols].rearrange("(nt p) j -> p nt j", p=P), o[:, n0 : n0 + step, :])
+
+        def weigh(t, cols):
+            nc.vector.tensor_scalar(lanes[1][:, t * PAIRS : (t + 1) * PAIRS][:, cols], sim[1][t][:, cols], gain_sb[:, 1, t : t + 1], None, ALU.mult)
+
+        def weave(c):
+            cols = slice(JB * c, JB * (c + 1))
+            nc.vector.tensor_copy(
+                z1[:, cols, :].rearrange("p (c i) t -> p c t i", i=4),
+                lanes[1].rearrange("p (t j) -> p t j", t=PACK)[:, :, cols].rearrange("p t (c i) -> p c t i", i=4),
+            )
+
+        def close(c):
+            quant_z(1, z1, slice(JB * c, JB * (c + 1)))
+            score(1, c)
+            finish(c)
+
+        quant_z(0, z0, slice(0, PAIRS))
+        for c in range(PAIRS // JB):
+            score(0, c)
+        weigh(1, slice(0, PAIRS))
+        weigh(2, slice(0, PAIRS))
+        weigh(3, halves[0])
+        weave(0)
+        weave(1)
+        close(0)
+        weigh(3, halves[1])
+        close(1)
+        weave(2)
+        weave(3)
+        close(2)
+        close(3)

@@ -1,7 +1,6 @@
 from contextlib import ExitStack
 
 import concourse.mybir as mybir
-from concourse.masks import make_identity
 
 K, T, S, PAIRS, H, N = 1536, 2048, 1024, 512, 1024, 512
 FLOPS = 2 * K * H * S + 2 * H * N * PAIRS
@@ -48,8 +47,7 @@ def tile_list_duplicate_pair_score_kernel(tc, tab_words, tab_scales, offs, w1, p
         w2_w = sb([P, R_PASSES, 2 * N // 4], I32, "w2_w")
         w2_s = sb([P, R_PASSES, N // 4], I32, "w2_s")
         warm = sb([P, 2], F32, "warm")
-        ident = sb([P, P], F32, "ident")
-        h = [sb([P, 2 * S], F32, "h%d" % t) for t in range(PACK)]
+        h = [sb([P, S], F32, "h%d" % t) for t in range(PACK)]
 
         nc.vector.memset(tab_s[:], 0)
         for q in range(2):
@@ -57,9 +55,6 @@ def tile_list_duplicate_pair_score_kernel(tc, tab_words, tab_scales, offs, w1, p
         nc.gpsimd.memset(warm[:, 0:1], 0.0)
         nc.scalar.activation(warm[:, 1:2], warm[:, 0:1], ACT.Exp)
         nc.gpsimd.memset(w2_s[:], 0)
-        make_identity(nc, ident[:])
-        for t in range(PACK):
-            nc.gpsimd.memset(h[t][:, S:], 0.0)
 
         raw = {}
 
@@ -86,8 +81,7 @@ def tile_list_duplicate_pair_score_kernel(tc, tab_words, tab_scales, offs, w1, p
         nc.sync.dma_start(pos_sb[1][:], pos2)
         load_w1(0, 1, 0, P)
         load_w1(1, 1, 0, P)
-        load_w1(2, 1, 0, P // 2)
-        load_w1(2, 1, P // 2, P)
+        load_w1(2, 1, 0, P)
         nc.sync.dma_start(gain_sb[:], gain.rearrange("(b p t) -> p b t", b=R_PASSES, t=PACK))
         for q in range(4):
             nc.sync.dma_start(w2_s[32 * q : 32 * q + 4, :, :], w2_scales[:, 4 * q : 4 * q + 4, :].bitcast(I32).rearrange("b r n -> r b n"))
@@ -100,15 +94,12 @@ def tile_list_duplicate_pair_score_kernel(tc, tab_words, tab_scales, offs, w1, p
             for b in range(R_PASSES):
                 w_c[(a, b)] = sb([P, K_PASS], U32, "w_c%d%d" % (a, b))
                 w_s[(a, b)] = sb([P, K_PASS], U8, "w_s%d%d" % (a, b))
-                if (a, b) != (2, 1):
-                    w_bf[(a, b)] = sb([P, PACK * K_PASS], BF16, "w_bf%d%d" % (a, b))[:]
+                w_bf[(a, b)] = sb([P, PACK * K_PASS], BF16, "w_bf%d%d" % (a, b))[:]
 
         def round_w1(engine, a, b, base, m0, m1):
             src = raw[(a, b, base)][:, :, PACK * (m0 - base) : PACK * (m1 - base)]
             dst = w_bf[(a, b)].rearrange("p (t m j) -> p t m j", t=PACK, j=PACK)[:, :, m0:m1, :]
-            if engine == "gpsimd":
-                nc.gpsimd.tensor_scalar(dst.rearrange("p t m j -> p m t j"), src.rearrange("p j (m t) -> p m t j", t=PACK), 1.0, 0.0, ALU.mult, ALU.add)
-            elif engine == "scalar":
+            if engine == "scalar":
                 nc.scalar.copy(dst.rearrange("p t m j -> p m j t"), src.rearrange("p j (m t) -> p m j t", t=PACK))
             else:
                 nc.vector.tensor_copy(dst.rearrange("p t m j -> p m j t"), src.rearrange("p j (m t) -> p m j t", t=PACK))
@@ -125,14 +116,11 @@ def tile_list_duplicate_pair_score_kernel(tc, tab_words, tab_scales, offs, w1, p
             nc.vector.tensor_copy(v_w[a][:], tab_w[a][:].bitcast(U32).indirect(offs_sb[:]))
 
         acc = {}
-        ACC_BANK = {(0, 0): 0, (0, 1): 2, (0, 2): 4, (0, 3): 6, (1, 0): 0, (1, 1): 2, (1, 2): 4, (1, 3): 0}
-        TURNED_BANK = {(0, 2): 2, (0, 3): 4, (1, 0): 0, (1, 1): 1}
-        BACK_BANK = {(0, 2): 3, (0, 3): 5, (1, 0): 6, (1, 1): 7}
 
-        def embed_pass(a, b, t, last=K_PASSES - 1):
-            for half in range(S // BANK):
+        def embed_pass(a, b, t, last=K_PASSES - 1, halves=(0, 1)):
+            for half in halves:
                 if a == 0:
-                    acc[(b, t, half)] = bank("acc", ACC_BANK[(b, t)] + half)
+                    acc[(b, t, half)] = bank("acc", 2 * t + half)
                 cols = slice(BANK * half, BANK * (half + 1))
                 nc.tensor.matmul_mx(
                     out=acc[(b, t, half)][:],
@@ -152,41 +140,19 @@ def tile_list_duplicate_pair_score_kernel(tc, tab_words, tab_scales, offs, w1, p
                 else:
                     nc.scalar.copy(dst, acc[(b, t, half)][:])
 
-        turned = {}
+        halves = [slice(0, PAIRS // 2), slice(PAIRS // 2, PAIRS)]
 
-        def turn(src, b, t, first):
-            if first:
-                turned[(b, t)] = bank("turned", TURNED_BANK[(b, t)])
-            for c in range(PAIRS // P):
-                cols = slice(P * c, P * (c + 1))
-                nc.tensor.matmul(turned[(b, t)][:, cols], src[:, cols], ident[:], start=first and c == 0, stop=not first and c == PAIRS // P - 1, is_transpose=True)
+        def pick(t, dst):
+            for cols in halves:
+                nc.vector.tensor_copy(dst[:, cols], h[t][:].indirect(pos_sb[0][:, cols.start // 16 : cols.stop // 16]))
 
-        def pick(t, side, dst):
-            nc.vector.tensor_copy(dst, h[t][:].indirect(pos_sb[side][:]))
+        def pick_less(t, first, dst):
+            for cols in halves:
+                nc.vector.tensor_tensor(dst[:, cols], h[t][:].indirect(pos_sb[1][:, cols.start // 16 : cols.stop // 16]), first[:, cols], ALU.subtract)
 
-        def pick_first(b, t, dst):
-            pick(t, 0, dst)
-            turn(dst, b, t, True)
-
-        def pick_negated(t, dst):
-            nc.vector.tensor_scalar(dst, h[t][:].indirect(pos_sb[1][:]), -1.0, 0.0, ALU.mult, ALU.add)
-
-        def pick_second(b, t, dst):
-            pick_negated(t, dst)
-            turn(dst, b, t, False)
-
-        back = {}
-
-        def distance(b, t, dist):
-            nc.scalar.activation(dist, turned[(b, t)][:], ACT.Abs)
-            back[(b, t)] = bank("back", BACK_BANK[(b, t)])
-            for c in range(PAIRS // P):
-                cols = slice(P * c, P * (c + 1))
-                nc.tensor.transpose(back[(b, t)][:, cols], dist[:, cols], ident[:])
-
-        def closeness(b, t, dist):
-            nc.scalar.activation(sim[b][t], dist, ACT.Exp, scale=-1.0)
-            nc.gpsimd.tensor_scalar(lanes[b][:, PAIRS * t : PAIRS * (t + 1)], sim[b][t], gain_sb[:, b, t : t + 1], 0.0, ALU.mult, ALU.add)
+        def closeness(diff, dist, sim):
+            nc.scalar.activation(dist, diff, ACT.Abs)
+            nc.scalar.activation(sim, dist, ACT.Exp, scale=-1.0)
 
         gather_tab(0)
         nc.vector.tensor_copy(v_s[:], tab_s[:].bitcast(U8).indirect(offs_sb[:]))
@@ -196,10 +162,9 @@ def tile_list_duplicate_pair_score_kernel(tc, tab_words, tab_scales, offs, w1, p
         for t in range(PACK):
             embed_pass(0, 0, t)
         gather_tab(2)
-        round_w1("scalar", 1, 0, 0, 0, 80)
-        round_w1("gpsimd", 1, 0, 0, 80, P)
+        round_w1("scalar", 1, 0, 0, 0, P)
         quant_w1(1, 0, 0, PACK)
-        round_w1("scalar", 2, 0, 0, 0, 64)
+        round_w1("vector", 2, 0, 0, 0, 64)
         round_w1("scalar", 2, 0, 64, 64, 88)
         round_w1("vector", 2, 0, 64, 88, 128)
         for t in range(PACK):
@@ -209,100 +174,58 @@ def tile_list_duplicate_pair_score_kernel(tc, tab_words, tab_scales, offs, w1, p
                 embed_pass(a, 0, t, order[-1])
 
         drain_h(0, 0, (1,))
-        drain_h(0, 1)
-        drain_h(0, 2)
-        for m0 in (0, 64):
-            round_w1("gpsimd", 0, 1, 0, m0, m0 + 64)
+        for t in range(1, PACK):
+            drain_h(0, t)
+        round_w1("scalar", 0, 1, 0, 0, P)
         round_w1("scalar", 1, 1, 0, 0, P)
-        pick00 = sb([P, 2, PAIRS], F32, "pick00", "tab_w0")
-        pick(0, 0, pick00[:, 0, :])
-        pick(0, 1, pick00[:, 1, :])
-        pick01 = sb([P, PAIRS], F32, "pick01", "tab_w1")
-        pick(1, 0, pick01[:])
-        early = [sb([P, PAIRS], F32, "early0", "raw01_0"), sb([P, PAIRS], F32, "early1", "raw21_0")]
-        nc.gpsimd.tensor_tensor(early[0][:], pick00[:, 0, :], pick00[:, 1, :], ALU.subtract)
-        quant_w1(0, 1, 0, PACK)
-        embed_pass(0, 1, 0)
-        embed_pass(0, 1, 1)
-        mid = sb([P, 3 * PAIRS], F32, "mid", "w_bf01")
-        w_bf[(2, 1)] = mid[:, : 2 * PAIRS].bitcast(BF16)
-        round_w1("gpsimd", 2, 1, 0, 0, 64)
-        round_w1("scalar", 2, 1, 64, 64, P)
-        drain_h(0, 3)
-        pick(1, 1, mid[:, 2 * PAIRS :])
-        nc.gpsimd.tensor_tensor(early[1][:], pick01[:], mid[:, 2 * PAIRS :], ALU.subtract)
-        quant_w1(1, 1, 0, PACK)
-        embed_pass(1, 1, 0)
-        embed_pass(1, 1, 1)
-        pick02 = sb([P, PAIRS], F32, "pick02", "w_bf11")
-        sim0 = sb([P, PACK, PAIRS], F32, "sim0", "raw11_0")
-        sim1 = sb([P, PACK - 1, PAIRS], F32, "sim1", "tab_w2")
-        sim = [[sim0[:, t, :] for t in range(PACK)], [sb([P, PAIRS], F32, "sim10")[:]] + [sim1[:, t, :] for t in range(PACK - 1)]]
-        dist_a = sb([P, 3, PAIRS], F32, "dist_a", "raw21_64")
+        round_w1("scalar", 2, 1, 0, 0, 32)
+        first = [sb([P, PACK, PAIRS], F32, "first%d" % b, "tab_w%d" % b) for b in range(R_PASSES)]
+        sim = [sb([P, PACK, PAIRS], F32, "sim0", "tab_w2"), sb([P, PACK, PAIRS], F32, "sim1", "raw00_0")]
+        diff0 = sb([P, 2, PAIRS], F32, "diff0", "w_bf00")
         for t in range(2):
-            nc.scalar.activation(dist_a[:, t, :], early[t][:], ACT.Abs)
-        pick(2, 0, pick02[:])
+            pick(t, first[0][:, t, :])
+            pick_less(t, first[0][:, t, :], diff0[:, t, :])
+        pick(2, first[0][:, 2, :])
+        quant_w1(0, 1, 0, PACK)
+        for t in range(PACK):
+            embed_pass(0, 1, t)
+        diff02 = sb([P, PAIRS], F32, "diff02", "w_bf01")
+        pick_less(2, first[0][:, 2, :], diff02[:])
+        round_w1("vector", 2, 1, 0, 32, P)
+        quant_w1(1, 1, 0, PACK)
         quant_w1(2, 1, 0, PACK)
-        embed_pass(2, 1, 0)
-        embed_pass(2, 1, 1)
-        late = sb([P, 5 * PAIRS], F32, "late", "w_bf01")
-        lanes = [late[:, 3 * PAIRS :].bitcast(BF16)]
-        closeness(0, 0, dist_a[:, 0, :])
-        closeness(0, 1, dist_a[:, 1, :])
-        for a in range(K_PASSES):
-            embed_pass(a, 1, 2)
-        pick_negated(2, late[:, :PAIRS])
-        pick(3, 0, late[:, PAIRS : 2 * PAIRS])
-        pick_negated(3, late[:, 2 * PAIRS : 3 * PAIRS])
+        for t in range(PACK):
+            order = (1, 2) if t < 1 else (2, 1)
+            for half in range(2):
+                for a in order:
+                    embed_pass(a, 1, t, order[-1], (half,))
+        late = sb([P, 2, PAIRS], F32, "late", "w_bf21")
+        pick(3, late[:, 0, :])
+        diff03 = late[:, 1, :]
+        pick_less(3, late[:, 0, :], diff03)
+        dist0 = sb([P, PACK, PAIRS], F32, "dist0", "raw21_0")
+        closeness(diff0[:], dist0[:, 0:2, :], sim[0][:, 0:2, :])
         drain_h(1, 0)
-        for a in range(K_PASSES):
-            embed_pass(a, 1, 3)
+        closeness(diff02[:], dist0[:, 2, :], sim[0][:, 2, :])
         drain_h(1, 1)
-        turn(pick02[:], 0, 2, True)
-        turn(late[:, :PAIRS], 0, 2, False)
-        distance(0, 2, dist_a[:, 2, :])
+        closeness(diff03, dist0[:, 3, :], sim[0][:, 3, :])
         drain_h(1, 2)
-        closeness(0, 2, back[(0, 2)][:])
-        turn(late[:, PAIRS : 2 * PAIRS], 0, 3, True)
-        turn(late[:, 2 * PAIRS : 3 * PAIRS], 0, 3, False)
-        distance(0, 3, sb([P, PAIRS], F32, "dist03", "dist")[:])
         drain_h(1, 3)
-        closeness(0, 3, back[(0, 3)][:])
-        z0 = sb([P, PAIRS, PACK], BF16, "z0", "raw20_64")
-        for j0 in (0, PAIRS // 2):
-            cols = slice(j0, j0 + PAIRS // 2)
-            nc.gpsimd.tensor_scalar(z0[:, cols, :], lanes[0].rearrange("p (t j) -> p j t", t=PACK)[:, cols, :], 1.0, 0.0, ALU.mult, ALU.add)
-        for t, tag in enumerate(("raw00_0", "raw10_0")):
-            both = sb([P, 2, PAIRS], F32, "pick1%d" % t, tag)
-            pick_first(1, t, both[:, 0, :])
-            pick_second(1, t, both[:, 1, :])
-            distance(1, t, sb([P, PAIRS], F32, "dist1%d" % t, ("dist_other", "dist")[t])[:])
+        diff1 = sb([P, PACK, PAIRS], F32, "diff1", "raw10_0")
+        dist1 = sb([P, PACK, PAIRS], F32, "dist1", "raw01_0")
+        for t in range(PACK - 1):
+            pick(t, first[1][:, t, :])
+            pick_less(t, first[1][:, t, :], diff1[:, t, :])
+            closeness(diff1[:, t, :], dist1[:, t, :], sim[1][:, t, :])
+        t = PACK - 1
+        pick(t, first[1][:, t, :])
+        pick_less(t, first[1][:, t, :], diff1[:, t, :])
+        for cols in halves:
+            closeness(diff1[:, t, cols], dist1[:, t, cols], sim[1][:, t, cols])
 
-        halves = [slice(0, PAIRS // 2), slice(PAIRS // 2, PAIRS)]
-        both = sb([P, 2, PAIRS], F32, "pick12", "w_bf00")
-        last = sb([P, 2, PAIRS], F32, "last", "w_bf10")
-        diff = sb([P, 2, PAIRS], F32, "diff", "w_bf01")
-        dist_c = sb([P, 2, PAIRS], F32, "dist_c", "dist")
-        for side in range(2):
-            pick(2, side, both[:, side, :])
-        for cols in halves:
-            nc.gpsimd.tensor_tensor(diff[:, 0, cols], both[:, 0, cols], both[:, 1, cols], ALU.subtract)
-        lanes.append(sb([P, PACK * PAIRS], BF16, "lanes1", "w_bf00")[:])
-        closeness(1, 0, back[(1, 0)][:])
-        nc.scalar.activation(sim[1][1], back[(1, 1)][:], ACT.Exp, scale=-1.0)
-        for cols in halves:
-            nc.scalar.activation(dist_c[:, 0, cols], diff[:, 0, cols], ACT.Abs)
-            nc.scalar.activation(sim[1][2][:, cols], dist_c[:, 0, cols], ACT.Exp, scale=-1.0)
-        for side in range(2):
-            pick(3, side, last[:, side, :])
-        for cols in halves:
-            nc.vector.tensor_tensor(diff[:, 1, cols], last[:, 0, cols], last[:, 1, cols], ALU.subtract)
-            nc.scalar.activation(dist_c[:, 1, cols], diff[:, 1, cols], ACT.Abs)
-            nc.scalar.activation(sim[1][3][:, cols], dist_c[:, 1, cols], ACT.Exp, scale=-1.0)
-
-        z_c = [sb([P, PAIRS], U32, "z_c0", "h3"), sb([P, PAIRS], U32, "z_c1")]
+        z_c = [sb([P, PAIRS], U32, "z_c0"), sb([P, PAIRS], U32, "z_c1")]
         z_s = [sb([P, PAIRS], U8, "z_s%d" % b) for b in range(R_PASSES)]
-        z1 = sb([P, PAIRS, PACK], BF16, "z1")
+        z = [sb([P, PAIRS, PACK], BF16, "z0", "h3"), sb([P, PAIRS, PACK], BF16, "z1")]
 
         def quant_z(b, z_bf, cols):
             nc.vector.quantize_mx(out=z_c[b][:, cols].bitcast(FP8X4), scales=z_s[b][:, cols], in_=z_bf[:, cols, :].rearrange("p j t -> p (j t)"))
@@ -330,33 +253,36 @@ def tile_list_duplicate_pair_score_kernel(tc, tab_words, tab_scales, offs, w1, p
                 nc.scalar.activation(o[:, n0 : n0 + step, :], y[c][:, n0 : n0 + step, :], ACT.Sigmoid)
                 nc.sync.dma_start(out[P * n0 : P * (n0 + step), cols].rearrange("(nt p) j -> p nt j", p=P), o[:, n0 : n0 + step, :])
 
-        def weigh(t, cols):
-            nc.vector.tensor_scalar(lanes[1][:, t * PAIRS : (t + 1) * PAIRS][:, cols], sim[1][t][:, cols], gain_sb[:, 1, t : t + 1], None, ALU.mult)
-
-        def weave(c):
+        def weigh(b, c):
             cols = slice(JB * c, JB * (c + 1))
-            nc.vector.tensor_copy(
-                z1[:, cols, :].rearrange("p (c i) t -> p c t i", i=4),
-                lanes[1].rearrange("p (t j) -> p t j", t=PACK)[:, :, cols].rearrange("p t (c i) -> p c t i", i=4),
+            nc.vector.tensor_tensor(
+                z[b][:, cols, :].rearrange("p (c i) t -> p c t i", i=4),
+                sim[b][:, :, cols].rearrange("p t (c i) -> p c t i", i=4),
+                gain_sb[:, b, :].unsqueeze(1).unsqueeze(3).to_broadcast([P, JB // 4, PACK, 4]),
+                ALU.mult,
             )
 
-        def close(c):
-            quant_z(1, z1, slice(JB * c, JB * (c + 1)))
+        weigh(0, 0)
+        weigh(0, 1)
+        weigh(1, 0)
+        quant_z(0, z[0], slice(0, 2 * JB))
+        score(0, 0)
+        score(0, 1)
+        weigh(1, 1)
+        quant_z(1, z[1], slice(0, JB))
+        score(1, 0)
+        finish(0)
+        weigh(0, 2)
+        quant_z(1, z[1], slice(JB, 2 * JB))
+        score(1, 1)
+        finish(1)
+        weigh(0, 3)
+        weigh(1, 2)
+        quant_z(0, z[0], slice(2 * JB, 4 * JB))
+        score(0, 2)
+        score(0, 3)
+        weigh(1, 3)
+        for c in (2, 3):
+            quant_z(1, z[1], slice(JB * c, JB * (c + 1)))
             score(1, c)
             finish(c)
-
-        quant_z(0, z0, slice(0, PAIRS))
-        for c in range(PAIRS // JB):
-            score(0, c)
-        weigh(1, slice(0, PAIRS))
-        weigh(2, slice(0, PAIRS))
-        weigh(3, halves[0])
-        weave(0)
-        weave(1)
-        close(0)
-        weigh(3, halves[1])
-        close(1)
-        weave(2)
-        weave(3)
-        close(2)
-        close(3)

@@ -41,19 +41,16 @@ def tile_list_duplicate_pair_score_kernel(tc, tab_words, tab_scales, offs, w1, p
         pos_sb = [keep.tile([P, PAIRS // 16], U16, name="pos_sb%d" % i) for i in range(2)]
         tab_w = [sb([P, T], I32, "tab_w%d" % a) for a in range(K_PASSES)]
         tab_s = sb([P, T // 4], I32, "tab_s")
-        v_w = [sb([P, S], U32, "v_w%d" % a) for a in range(K_PASSES)]
+        v_w = [sb([P, S], U32, "v_w%d" % a) for a in range(K_PASSES - 1)]
         v_s = sb([P, S], U8, "v_s")
         gain_sb = sb([P, R_PASSES, PACK], F32, "gain_sb")
         w2_w = sb([P, R_PASSES, 2 * N // 4], I32, "w2_w")
         w2_s = sb([P, R_PASSES, N // 4], I32, "w2_s")
-        warm = sb([P, 2], F32, "warm")
         h = [sb([P, S], F32, "h%d" % t) for t in range(PACK)]
 
         nc.vector.memset(tab_s[:], 0)
         for q in range(2):
             nc.scalar.dma_start(tab_s[32 * q : 32 * q + 4 * K_PASSES, :], tab_scales[:, 4 * q : 4 * q + 4, :].bitcast(I32))
-        nc.gpsimd.memset(warm[:, 0:1], 0.0)
-        nc.scalar.activation(warm[:, 1:2], warm[:, 0:1], ACT.Exp)
         nc.gpsimd.memset(w2_s[:], 0)
 
         raw = {}
@@ -99,7 +96,9 @@ def tile_list_duplicate_pair_score_kernel(tc, tab_words, tab_scales, offs, w1, p
         def round_w1(engine, a, b, base, m0, m1):
             src = raw[(a, b, base)][:, :, PACK * (m0 - base) : PACK * (m1 - base)]
             dst = w_bf[(a, b)].rearrange("p (t m j) -> p t m j", t=PACK, j=PACK)[:, :, m0:m1, :]
-            if engine == "scalar":
+            if engine == "gpsimd":
+                nc.gpsimd.tensor_scalar(dst, src.rearrange("p j (m t) -> p t m j", t=PACK), 1.0, 0.0, ALU.mult, ALU.add)
+            elif engine == "scalar":
                 nc.scalar.copy(dst.rearrange("p t m j -> p m j t"), src.rearrange("p j (m t) -> p m j t", t=PACK))
             else:
                 nc.vector.tensor_copy(dst.rearrange("p t m j -> p m j t"), src.rearrange("p j (m t) -> p m j t", t=PACK))
@@ -117,9 +116,9 @@ def tile_list_duplicate_pair_score_kernel(tc, tab_words, tab_scales, offs, w1, p
 
         acc = {}
 
-        def embed_pass(a, b, t, last=K_PASSES - 1, halves=(0, 1)):
+        def embed_pass(a, b, t, last=K_PASSES - 1, halves=(0, 1), opening=0):
             for half in halves:
-                if a == 0:
+                if a == opening:
                     acc[(b, t, half)] = bank("acc", 2 * t + half)
                 cols = slice(BANK * half, BANK * (half + 1))
                 nc.tensor.matmul_mx(
@@ -128,7 +127,7 @@ def tile_list_duplicate_pair_score_kernel(tc, tab_words, tab_scales, offs, w1, p
                     lhsT_scale=w_s[(a, b)][:, P * t : P * (t + 1)],
                     rhs=v_w[a][:, cols].bitcast(FP8X4),
                     rhs_scale=v_s[4 * a : P, cols],
-                    start=(a == 0),
+                    start=(a == opening),
                     stop=(a == last),
                 )
 
@@ -142,9 +141,11 @@ def tile_list_duplicate_pair_score_kernel(tc, tab_words, tab_scales, offs, w1, p
 
         halves = [slice(0, PAIRS // 2), slice(PAIRS // 2, PAIRS)]
 
-        def pick(t, dst):
-            for cols in halves:
-                nc.vector.tensor_copy(dst[:, cols], h[t][:].indirect(pos_sb[0][:, cols.start // 16 : cols.stop // 16]))
+        whole = [slice(0, PAIRS)]
+
+        def pick(t, dst, side=0, parts=halves):
+            for cols in parts:
+                nc.vector.tensor_copy(dst[:, cols], h[t][:].indirect(pos_sb[side][:, cols.start // 16 : cols.stop // 16]))
 
         def pick_less(t, first, dst):
             for cols in halves:
@@ -161,12 +162,13 @@ def tile_list_duplicate_pair_score_kernel(tc, tab_words, tab_scales, offs, w1, p
         quant_w1(0, 0, 0, PACK)
         for t in range(PACK):
             embed_pass(0, 0, t)
+        v_w.append(sb([P, S], U32, "v_w2", "w_bf00"))
         gather_tab(2)
-        round_w1("scalar", 1, 0, 0, 0, P)
+        round_w1("gpsimd", 1, 0, 0, 88, P)
+        round_w1("scalar", 1, 0, 0, 0, 88)
         quant_w1(1, 0, 0, PACK)
-        round_w1("vector", 2, 0, 0, 0, 64)
-        round_w1("scalar", 2, 0, 64, 64, 88)
-        round_w1("vector", 2, 0, 64, 88, 128)
+        round_w1("scalar", 2, 0, 0, 0, 64)
+        round_w1("vector", 2, 0, 64, 64, P)
         for t in range(PACK):
             quant_w1(2, 0, t, t + 1)
             order = (1, 2) if t < 1 else (2, 1)
@@ -176,22 +178,25 @@ def tile_list_duplicate_pair_score_kernel(tc, tab_words, tab_scales, offs, w1, p
         drain_h(0, 0, (1,))
         for t in range(1, PACK):
             drain_h(0, t)
-        round_w1("scalar", 0, 1, 0, 0, P)
+        round_w1("gpsimd", 0, 1, 0, 0, 112)
+        round_w1("scalar", 0, 1, 0, 112, P)
         round_w1("scalar", 1, 1, 0, 0, P)
-        round_w1("scalar", 2, 1, 0, 0, 32)
+        round_w1("scalar", 2, 1, 0, 0, P)
         first = [sb([P, PACK, PAIRS], F32, "first%d" % b, "tab_w%d" % b) for b in range(R_PASSES)]
         sim = [sb([P, PACK, PAIRS], F32, "sim0", "tab_w2"), sb([P, PACK, PAIRS], F32, "sim1", "raw00_0")]
-        diff0 = sb([P, 2, PAIRS], F32, "diff0", "w_bf00")
+        second0 = sb([P, 2, PAIRS], F32, "second0", "raw20_64")
         for t in range(2):
-            pick(t, first[0][:, t, :])
-            pick_less(t, first[0][:, t, :], diff0[:, t, :])
-        pick(2, first[0][:, 2, :])
+            pick(t, first[0][:, t, :], 0, whole)
+            pick(t, second0[:, t, :], 1, whole)
         quant_w1(0, 1, 0, PACK)
         for t in range(PACK):
             embed_pass(0, 1, t)
-        diff02 = sb([P, PAIRS], F32, "diff02", "w_bf01")
-        pick_less(2, first[0][:, 2, :], diff02[:])
-        round_w1("vector", 2, 1, 0, 32, P)
+        mid = sb([P, 4, PAIRS], F32, "mid", "w_bf01")
+        diff0 = mid[:, 0:2, :]
+        for t in range(2):
+            nc.gpsimd.tensor_tensor(diff0[:, t, :], first[0][:, t, :], second0[:, t, :], ALU.subtract)
+        for side in range(2):
+            pick(2, mid[:, 2 + side, :], side, whole)
         quant_w1(1, 1, 0, PACK)
         quant_w1(2, 1, 0, PACK)
         for t in range(PACK):
@@ -199,24 +204,39 @@ def tile_list_duplicate_pair_score_kernel(tc, tab_words, tab_scales, offs, w1, p
             for half in range(2):
                 for a in order:
                     embed_pass(a, 1, t, order[-1], (half,))
-        late = sb([P, 2, PAIRS], F32, "late", "w_bf21")
-        pick(3, late[:, 0, :])
-        diff03 = late[:, 1, :]
-        pick_less(3, late[:, 0, :], diff03)
+        late = sb([P, 6 * PAIRS], F32, "late", "w_bf21")
+        pick(3, late[:, :PAIRS], 0, whole)
+        pick(3, late[:, 5 * PAIRS :], 1, whole)
+        diff02, diff03 = late[:, PAIRS : 2 * PAIRS], late[:, 2 * PAIRS : 3 * PAIRS]
+        lanes = late[:, 3 * PAIRS : 5 * PAIRS].bitcast(BF16).rearrange("p (t j) -> p t j", t=PACK)
+        nc.gpsimd.tensor_tensor(diff02, mid[:, 2, :], mid[:, 3, :], ALU.subtract)
+
+        def weigh_lane(t):
+            nc.gpsimd.tensor_scalar(lanes[:, t, :], sim[0][:, t, :], gain_sb[:, 0, t : t + 1], 0.0, ALU.mult, ALU.add)
+
         dist0 = sb([P, PACK, PAIRS], F32, "dist0", "raw21_0")
-        closeness(diff0[:], dist0[:, 0:2, :], sim[0][:, 0:2, :])
+        closeness(diff0[:, 0, :], dist0[:, 0, :], sim[0][:, 0, :])
         drain_h(1, 0)
-        closeness(diff02[:], dist0[:, 2, :], sim[0][:, 2, :])
+        closeness(diff0[:, 1, :], dist0[:, 1, :], sim[0][:, 1, :])
+        weigh_lane(0)
+        weigh_lane(1)
+        nc.gpsimd.tensor_tensor(diff03, late[:, :PAIRS], late[:, 5 * PAIRS :], ALU.subtract)
         drain_h(1, 1)
-        closeness(diff03, dist0[:, 3, :], sim[0][:, 3, :])
+        closeness(diff02, dist0[:, 2, :], sim[0][:, 2, :])
         drain_h(1, 2)
+        closeness(diff03, dist0[:, 3, :], sim[0][:, 3, :])
         drain_h(1, 3)
         diff1 = sb([P, PACK, PAIRS], F32, "diff1", "raw10_0")
-        dist1 = sb([P, PACK, PAIRS], F32, "dist1", "raw01_0")
+        dist1 = sb([P, PACK, PAIRS], F32, "dist1", "raw20_0")
+        second = sb([P, PACK - 1, PAIRS], F32, "second", "raw11_0")
         for t in range(PACK - 1):
-            pick(t, first[1][:, t, :])
-            pick_less(t, first[1][:, t, :], diff1[:, t, :])
-            closeness(diff1[:, t, :], dist1[:, t, :], sim[1][:, t, :])
+            pick(t, first[1][:, t, :], 0, whole)
+            pick(t, second[:, t, :], 1, whole)
+            diff = diff1[:, t, :] if t < 2 else sb([P, PAIRS], F32, "diff12", "tab_w2")[:]
+            nc.gpsimd.tensor_tensor(diff, first[1][:, t, :], second[:, t, :], ALU.subtract)
+            if t < 2:
+                weigh_lane(2 + t)
+            closeness(diff, dist1[:, t, :], sim[1][:, t, :])
         t = PACK - 1
         pick(t, first[1][:, t, :])
         pick_less(t, first[1][:, t, :], diff1[:, t, :])
@@ -253,36 +273,28 @@ def tile_list_duplicate_pair_score_kernel(tc, tab_words, tab_scales, offs, w1, p
                 nc.scalar.activation(o[:, n0 : n0 + step, :], y[c][:, n0 : n0 + step, :], ACT.Sigmoid)
                 nc.sync.dma_start(out[P * n0 : P * (n0 + step), cols].rearrange("(nt p) j -> p nt j", p=P), o[:, n0 : n0 + step, :])
 
-        def weigh(b, c):
+        def weave(cols):
+            nc.vector.tensor_copy(z[0][:, cols, :].rearrange("p (c i) t -> p c t i", i=4), lanes[:, :, cols].rearrange("p t (c i) -> p c t i", i=4))
+
+        def weigh(c):
             cols = slice(JB * c, JB * (c + 1))
             nc.vector.tensor_tensor(
-                z[b][:, cols, :].rearrange("p (c i) t -> p c t i", i=4),
-                sim[b][:, :, cols].rearrange("p t (c i) -> p c t i", i=4),
-                gain_sb[:, b, :].unsqueeze(1).unsqueeze(3).to_broadcast([P, JB // 4, PACK, 4]),
+                z[1][:, cols, :].rearrange("p (c i) t -> p c t i", i=4),
+                sim[1][:, :, cols].rearrange("p t (c i) -> p c t i", i=4),
+                gain_sb[:, 1, :].unsqueeze(1).unsqueeze(3).to_broadcast([P, JB // 4, PACK, 4]),
                 ALU.mult,
             )
 
-        weigh(0, 0)
-        weigh(0, 1)
-        weigh(1, 0)
-        quant_z(0, z[0], slice(0, 2 * JB))
-        score(0, 0)
-        score(0, 1)
-        weigh(1, 1)
-        quant_z(1, z[1], slice(0, JB))
-        score(1, 0)
-        finish(0)
-        weigh(0, 2)
-        quant_z(1, z[1], slice(JB, 2 * JB))
-        score(1, 1)
-        finish(1)
-        weigh(0, 3)
-        weigh(1, 2)
-        quant_z(0, z[0], slice(2 * JB, 4 * JB))
-        score(0, 2)
-        score(0, 3)
-        weigh(1, 3)
-        for c in (2, 3):
+        for cols in halves:
+            weave(cols)
+        quant_z(0, z[0], halves[0])
+        weigh(0)
+        quant_z(0, z[0], halves[1])
+        for c in range(PAIRS // JB):
+            score(0, c)
+        for c in range(PAIRS // JB):
+            if c + 1 < PAIRS // JB:
+                weigh(c + 1)
             quant_z(1, z[1], slice(JB * c, JB * (c + 1)))
             score(1, c)
             finish(c)

@@ -91,7 +91,7 @@ def tile_list_duplicate_pair_score_kernel(tc, tab_words, tab_scales, offs, w1, p
             for b in range(R_PASSES):
                 w_c[(a, b)] = sb([P, K_PASS], U32, "w_c%d%d" % (a, b))
                 w_s[(a, b)] = sb([P, K_PASS], U8, "w_s%d%d" % (a, b))
-                w_bf[(a, b)] = sb([P, PACK * K_PASS], BF16, "w_bf%d%d" % (a, b))[:]
+                w_bf[(a, b)] = sb([P, PACK * K_PASS], BF16, "w_bf%d%d" % (a, b), "w_bf20" if (a, b) == (0, 1) else None)[:]
 
         def round_w1(engine, a, b, base, m0, m1):
             src = raw[(a, b, base)][:, :, PACK * (m0 - base) : PACK * (m1 - base)]
@@ -101,7 +101,7 @@ def tile_list_duplicate_pair_score_kernel(tc, tab_words, tab_scales, offs, w1, p
             elif engine == "scalar":
                 nc.scalar.copy(dst.rearrange("p t m j -> p m j t"), src.rearrange("p j (m t) -> p m j t", t=PACK))
             else:
-                nc.vector.tensor_copy(dst.rearrange("p t m j -> p m j t"), src.rearrange("p j (m t) -> p m j t", t=PACK))
+                nc.vector.tensor_copy(dst.rearrange("p (s e) m j -> p s m j e", e=2), src.rearrange("p j (m s e) -> p s m j e", s=2, e=2))
 
         def quant_w1(a, b, t0, t1):
             cols = slice(P * t0, P * t1)
@@ -191,7 +191,7 @@ def tile_list_duplicate_pair_score_kernel(tc, tab_words, tab_scales, offs, w1, p
         quant_w1(0, 1, 0, PACK)
         for t in range(PACK):
             embed_pass(0, 1, t)
-        mid = sb([P, 4, PAIRS], F32, "mid", "w_bf01")
+        mid = sb([P, 4, PAIRS], F32, "mid", "w_bf20")
         diff0 = mid[:, 0:2, :]
         for t in range(2):
             nc.gpsimd.tensor_tensor(diff0[:, t, :], first[0][:, t, :], second0[:, t, :], ALU.subtract)

@@ -23,6 +23,7 @@ K_PASSES = K // K_PASS
 R_PASSES = H // K_PASS
 BANK = 512
 JB = 128
+CHUNK = 256
 
 
 def tile_list_duplicate_pair_score_kernel(tc, tab_words, tab_scales, offs, w1, pos1, pos2, gain, w2_words, w2_scales, out):
@@ -43,10 +44,10 @@ def tile_list_duplicate_pair_score_kernel(tc, tab_words, tab_scales, offs, w1, p
         tab_s = sb([P, T // 4], I32, "tab_s")
         v_w = [sb([P, S], U32, "v_w%d" % a) for a in range(K_PASSES - 1)]
         v_s = sb([P, S], U8, "v_s")
-        gain_sb = sb([P, R_PASSES, PACK], F32, "gain_sb")
+        gain_nat = sb([P, PACK], F32, "gain_nat")
+        gain_sb = sb([P, PACK], F32, "gain_sb")
         w2_w = sb([P, R_PASSES, 2 * N // 4], I32, "w2_w")
         w2_s = sb([P, R_PASSES, N // 4], I32, "w2_s")
-        h = [sb([P, S], F32, "h%d" % t) for t in range(PACK)]
 
         nc.vector.memset(tab_s[:], 0)
         for q in range(2):
@@ -58,28 +59,31 @@ def tile_list_duplicate_pair_score_kernel(tc, tab_words, tab_scales, offs, w1, p
         def load_tab(a):
             nc.sync.dma_start(tab_w[a][:], tab_words[a].rearrange("p t i -> p (t i)").bitcast(I32))
 
-        def load_w1(a, b, m0, m1):
-            t = sb([P, PACK, PACK * (m1 - m0)], F32, "raw%d%d_%d" % (a, b, m0))
-            cols = slice(K_PASS * b + PACK * m0, K_PASS * b + PACK * m1)
-            nc.sync.dma_start(t[:], w1[K_PASS * a : K_PASS * (a + 1), cols].rearrange("(p j) c -> p j c", j=PACK))
-            raw[(a, b, m0)] = t
+        def load_w1(a, c0, c1):
+            t = sb([P, PACK, c1 - c0], F32, "raw%d_%d" % (a, c0))
+            nc.sync.dma_start(t[:], w1[K_PASS * a : K_PASS * (a + 1), c0:c1].rearrange("(p j) c -> p j c", j=PACK))
+            raw[(a, c0)] = t
 
         nc.sync.dma_start(offs_sb[:], offs)
         load_tab(0)
         for q in range(2, 4):
             nc.sync.dma_start(tab_s[32 * q : 32 * q + 4 * K_PASSES, :], tab_scales[:, 4 * q : 4 * q + 4, :].bitcast(I32))
         load_tab(1)
-        load_w1(0, 0, 0, P)
+        load_w1(0, 0, CHUNK)
         load_tab(2)
-        load_w1(1, 0, 0, P)
-        load_w1(2, 0, 0, P // 2)
-        load_w1(2, 0, P // 2, P)
+        load_w1(1, 0, CHUNK)
+        load_w1(2, 0, CHUNK)
         nc.sync.dma_start(pos_sb[0][:], pos1)
         nc.sync.dma_start(pos_sb[1][:], pos2)
-        load_w1(0, 1, 0, P)
-        load_w1(1, 1, 0, P)
-        load_w1(2, 1, 0, P)
-        nc.sync.dma_start(gain_sb[:], gain.rearrange("(b p t) -> p b t", b=R_PASSES, t=PACK))
+        for a in range(K_PASSES):
+            load_w1(a, CHUNK, 2 * CHUNK)
+        load_w1(0, K_PASS, K_PASS + CHUNK)
+        load_w1(0, K_PASS + CHUNK, H)
+        load_w1(1, K_PASS, H)
+        load_w1(2, K_PASS, H)
+        with nc.allow_non_contiguous_dma(reason="one gain a partition"):
+            nc.sync.dma_start(gain_nat[:], gain[:K_PASS].rearrange("(u p) -> p u", p=P))
+        nc.sync.dma_start(gain_sb[:], gain[K_PASS:].rearrange("(p t) -> p t", t=PACK))
         for q in range(4):
             nc.sync.dma_start(w2_s[32 * q : 32 * q + 4, :, :], w2_scales[:, 4 * q : 4 * q + 4, :].bitcast(I32).rearrange("b r n -> r b n"))
         nc.sync.dma_start(w2_w[:], w2_words.bitcast(I32).rearrange("b p n -> p b n"))
@@ -87,15 +91,20 @@ def tile_list_duplicate_pair_score_kernel(tc, tab_words, tab_scales, offs, w1, p
         w_bf = {}
         w_c = {}
         w_s = {}
-        for a in range(K_PASSES):
-            for b in range(R_PASSES):
-                w_c[(a, b)] = sb([P, K_PASS], U32, "w_c%d%d" % (a, b))
-                w_s[(a, b)] = sb([P, K_PASS], U8, "w_s%d%d" % (a, b))
-                w_bf[(a, b)] = sb([P, PACK * K_PASS], BF16, "w_bf%d%d" % (a, b), "w_bf20" if (a, b) == (0, 1) else None)[:]
 
-        def round_w1(engine, a, b, base, m0, m1):
-            src = raw[(a, b, base)][:, :, PACK * (m0 - base) : PACK * (m1 - base)]
-            dst = w_bf[(a, b)].rearrange("p (t m j) -> p t m j", t=PACK, j=PACK)[:, :, m0:m1, :]
+        def round_plain(engine, a, c, c0, c1):
+            src = raw[(a, CHUNK * c)][:, :, c0:c1]
+            dst = w_bf[(a, c)].rearrange("p (c j) -> p c j", j=PACK)[:, c0:c1, :]
+            if engine == "gpsimd":
+                nc.gpsimd.tensor_scalar(dst, src.rearrange("p j c -> p c j"), 1.0, 0.0, ALU.mult, ALU.add)
+            elif engine == "scalar":
+                nc.scalar.copy(dst.rearrange("p (c i) j -> p c j i", i=4), src.rearrange("p j (c i) -> p c j i", i=4))
+            else:
+                nc.vector.tensor_copy(dst.rearrange("p (c i) j -> p c j i", i=4), src.rearrange("p j (c i) -> p c j i", i=4))
+
+        def round_dealt(engine, a, base, m0, m1):
+            src = raw[(a, K_PASS + PACK * base)][:, :, PACK * (m0 - base) : PACK * (m1 - base)]
+            dst = w_bf[(a, 2)].rearrange("p (t m j) -> p t m j", t=PACK, j=PACK)[:, :, m0:m1, :]
             if engine == "gpsimd":
                 nc.gpsimd.tensor_scalar(dst, src.rearrange("p j (m t) -> p t m j", t=PACK), 1.0, 0.0, ALU.mult, ALU.add)
             elif engine == "scalar":
@@ -103,164 +112,239 @@ def tile_list_duplicate_pair_score_kernel(tc, tab_words, tab_scales, offs, w1, p
             else:
                 nc.vector.tensor_copy(dst.rearrange("p (s e) m j -> p s m j e", e=2), src.rearrange("p j (m s e) -> p s m j e", s=2, e=2))
 
-        def quant_w1(a, b, t0, t1):
+        def quant_w1(a, c, t0, t1):
             cols = slice(P * t0, P * t1)
-            nc.vector.quantize_mx(
-                out=w_c[(a, b)][:, cols].bitcast(FP8X4),
-                scales=w_s[(a, b)][:, cols],
-                in_=w_bf[(a, b)][:, K_PASS * t0 : K_PASS * t1],
-            )
+            nc.vector.quantize_mx(out=w_c[(a, c)][:, cols].bitcast(FP8X4), scales=w_s[(a, c)][:, cols], in_=w_bf[(a, c)][:, K_PASS * t0 : K_PASS * t1])
 
         def gather_tab(a):
             nc.vector.tensor_copy(v_w[a][:], tab_w[a][:].bitcast(U32).indirect(offs_sb[:]))
 
         acc = {}
 
-        def embed_pass(a, b, t, last=K_PASSES - 1, halves=(0, 1), opening=0):
+        def embed_pass(a, c, t, opening, last, halves=(0, 1)):
+            u = 2 * c + t
             for half in halves:
                 if a == opening:
-                    acc[(b, t, half)] = bank("acc", 2 * t + half)
+                    acc[(u, half)] = bank("acc", (2 * u + half) % 8)
                 cols = slice(BANK * half, BANK * (half + 1))
                 nc.tensor.matmul_mx(
-                    out=acc[(b, t, half)][:],
-                    lhsT=w_c[(a, b)][:, P * t : P * (t + 1)].bitcast(FP8X4),
-                    lhsT_scale=w_s[(a, b)][:, P * t : P * (t + 1)],
+                    out=acc[(u, half)][:],
+                    lhsT=w_c[(a, c)][:, P * t : P * (t + 1)].bitcast(FP8X4),
+                    lhsT_scale=w_s[(a, c)][:, P * t : P * (t + 1)],
                     rhs=v_w[a][:, cols].bitcast(FP8X4),
                     rhs_scale=v_s[4 * a : P, cols],
                     start=(a == opening),
                     stop=(a == last),
                 )
 
-        def drain_h(b, t, vec_halves=()):
+        h = {}
+
+        def drain_h(u, tag, vec_halves=()):
+            h[u] = sb([P, S], F32, "h%d" % u, tag)
             for half in range(S // BANK):
-                dst = h[t][:, BANK * half : BANK * (half + 1)]
+                dst = h[u][:, BANK * half : BANK * (half + 1)]
                 if half in vec_halves:
-                    nc.vector.tensor_copy(dst, acc[(b, t, half)][:])
+                    nc.vector.tensor_copy(dst, acc[(u, half)][:])
                 else:
-                    nc.scalar.copy(dst, acc[(b, t, half)][:])
+                    nc.scalar.copy(dst, acc[(u, half)][:])
 
         halves = [slice(0, PAIRS // 2), slice(PAIRS // 2, PAIRS)]
-
         whole = [slice(0, PAIRS)]
 
-        def pick(t, dst, side=0, parts=halves):
+        def pick(u, dst, side, parts):
             for cols in parts:
-                nc.vector.tensor_copy(dst[:, cols], h[t][:].indirect(pos_sb[side][:, cols.start // 16 : cols.stop // 16]))
+                nc.vector.tensor_copy(dst[:, cols], h[u][:].indirect(pos_sb[side][:, cols.start // 16 : cols.stop // 16]))
 
-        def pick_less(t, first, dst):
-            for cols in halves:
-                nc.vector.tensor_tensor(dst[:, cols], h[t][:].indirect(pos_sb[1][:, cols.start // 16 : cols.stop // 16]), first[:, cols], ALU.subtract)
+        def pick_less(u, first, dst, parts):
+            for cols in parts:
+                nc.vector.tensor_tensor(dst[:, cols], h[u][:].indirect(pos_sb[1][:, cols.start // 16 : cols.stop // 16]), first[:, cols], ALU.subtract)
 
         def closeness(diff, dist, sim):
             nc.scalar.activation(dist, diff, ACT.Abs)
             nc.scalar.activation(sim, dist, ACT.Exp, scale=-1.0)
 
+        def less(diff, first, second):
+            nc.gpsimd.tensor_tensor(diff, first, second, ALU.subtract)
+
+        for a in range(K_PASSES):
+            w_bf[(a, 0)] = sb([P, PACK * CHUNK], BF16, "w_bf%d0" % a)[:]
+            w_c[(a, 0)] = sb([P, CHUNK], U32, "w_c%d0" % a)[:]
+            w_c[(a, 2)] = sb([P, K_PASS], U32, "w_c%d2" % a)[:]
+            for c in range(3):
+                w_s[(a, c)] = sb([P, K_PASS if c == 2 else CHUNK], U8, "w_s%d%d" % (a, c))[:]
+
         gather_tab(0)
         nc.vector.tensor_copy(v_s[:], tab_s[:].bitcast(U8).indirect(offs_sb[:]))
         gather_tab(1)
-        round_w1("scalar", 0, 0, 0, 0, P)
-        quant_w1(0, 0, 0, PACK)
-        for t in range(PACK):
-            embed_pass(0, 0, t)
+        round_plain("scalar", 0, 0, 0, CHUNK)
+        quant_w1(0, 0, 0, 2)
+        for t in range(2):
+            embed_pass(0, 0, t, 0, 2 - t)
         v_w.append(sb([P, S], U32, "v_w2", "w_bf00"))
         gather_tab(2)
-        round_w1("gpsimd", 1, 0, 0, 88, P)
-        round_w1("scalar", 1, 0, 0, 0, 88)
-        quant_w1(1, 0, 0, PACK)
-        round_w1("scalar", 2, 0, 0, 0, 64)
-        round_w1("vector", 2, 0, 64, 64, P)
-        for t in range(PACK):
-            quant_w1(2, 0, t, t + 1)
-            order = (1, 2) if t < 1 else (2, 1)
-            for a in order:
-                embed_pass(a, 0, t, order[-1])
+        round_plain("scalar", 1, 0, 0, CHUNK)
+        round_plain("vector", 2, 0, 0, P)
+        quant_w1(1, 0, 0, 2)
+        embed_pass(1, 0, 0, 0, 2)
+        round_plain("scalar", 2, 0, P, CHUNK)
+        quant_w1(2, 0, 0, 1)
+        embed_pass(2, 0, 0, 0, 2)
+        quant_w1(2, 0, 1, 2)
+        for a in (2, 1):
+            embed_pass(a, 0, 1, 0, 1)
+        drain_h(0, "h0", (1,))
+        drain_h(1, "h1")
 
-        drain_h(0, 0, (1,))
-        for t in range(1, PACK):
-            drain_h(0, t)
-        round_w1("gpsimd", 0, 1, 0, 0, 112)
-        round_w1("scalar", 0, 1, 0, 112, P)
-        round_w1("scalar", 1, 1, 0, 0, P)
-        round_w1("scalar", 2, 1, 0, 0, P)
-        first = [sb([P, PACK, PAIRS], F32, "first%d" % b, "tab_w%d" % b) for b in range(R_PASSES)]
-        sim = [sb([P, PACK, PAIRS], F32, "sim0", "tab_w2"), sb([P, PACK, PAIRS], F32, "sim1", "raw00_0")]
-        second0 = sb([P, 2, PAIRS], F32, "second0", "raw20_64")
+        for a in range(K_PASSES):
+            w_bf[(a, 1)] = sb([P, PACK * CHUNK], BF16, "w_bf%d1" % a, "w_bf20" if a == 0 else None)[:]
+        round_plain("gpsimd", 0, 1, 0, CHUNK)
+        round_plain("gpsimd", 1, 1, 0, CHUNK)
+        round_plain("scalar", 2, 1, 0, CHUNK)
+        first0 = sb([P, PAIRS], F32, "first0")
+        diff0 = sb([P, PAIRS], F32, "diff0", "w_bf20")
+        pick(0, first0, 0, whole)
+        w_c[(0, 1)] = sb([P, CHUNK], U32, "w_c01")[:]
+        quant_w1(0, 1, 0, 2)
         for t in range(2):
-            pick(t, first[0][:, t, :], 0, whole)
-            pick(t, second0[:, t, :], 1, whole)
-        quant_w1(0, 1, 0, PACK)
-        for t in range(PACK):
-            embed_pass(0, 1, t)
-        mid = sb([P, 4, PAIRS], F32, "mid", "w_bf20")
-        diff0 = mid[:, 0:2, :]
-        for t in range(2):
-            nc.gpsimd.tensor_tensor(diff0[:, t, :], first[0][:, t, :], second0[:, t, :], ALU.subtract)
+            embed_pass(0, 1, t, 0, 2 - t)
+        pick_less(0, first0, diff0, whole)
+        w_c1 = sb([P, 2 * CHUNK], U32, "w_c1", "first0")
+        for a in range(1, K_PASSES):
+            w_c[(a, 1)] = w_c1[:, CHUNK * (a - 1) : CHUNK * a]
+            quant_w1(a, 1, 0, 2)
+            embed_pass(a, 1, 0, 0, 2)
+        for a in (2, 1):
+            embed_pass(a, 1, 1, 0, 1)
+        pair1 = sb([P, 2, PAIRS], F32, "pair1", "w_bf21")
         for side in range(2):
-            pick(2, mid[:, 2 + side, :], side, whole)
-        quant_w1(1, 1, 0, PACK)
-        quant_w1(2, 1, 0, PACK)
-        for t in range(PACK):
-            order = (1, 2) if t < 1 else (2, 1)
+            pick(1, pair1[:, side, :], side, whole)
+        z_nat = sb([P, PACK, PAIRS], BF16, "z_nat")
+        lanes = sb([P, PACK, PAIRS], BF16, "lanes")
+
+        def deal(u):
+            if u == 0:
+                nc.scalar.activation(z_nat[:, u, :], sim[0][:, u, :], ACT.Copy, scale=gain_nat[:, u : u + 1])
+            else:
+                nc.gpsimd.tensor_scalar(z_nat[:, u, :], sim[0][:, u, :], gain_nat[:, u : u + 1], 0.0, ALU.mult, ALU.add)
+            for t in range(PACK):
+                nc.sync.dma_start(lanes[32 * u : 32 * (u + 1), t, :], z_nat[t:P:PACK, u, :])
+
+        dist0 = sb([P, PAIRS], F32, "dist0", "raw2_256")
+        nc.scalar.activation(dist0[:], diff0[:], ACT.Abs)
+        w_bf[(0, 2)] = sb([P, PACK * K_PASS], BF16, "w_bf02", "w_bf11")[:]
+        round_dealt("scalar", 0, 0, 0, 64)
+        round_dealt("gpsimd", 0, 64, 64, P)
+        drain_h(2, "h2")
+        drain_h(3, "h3")
+        quant_w1(0, 2, 0, PACK)
+        for t in range(2):
+            embed_pass(0, 2, t, 0, 2 - t)
+        mid = sb([P, 4 * PAIRS], F32, "mid", "w_bf11")
+        pair2 = mid[:, : 2 * PAIRS].rearrange("p (s j) -> p s j", s=2)
+        w_bf[(1, 2)] = mid[:, 2 * PAIRS :].bitcast(BF16)
+        for side in range(2):
+            pick(2, pair2[:, side, :], side, whole)
+        round_dealt("gpsimd", 1, 0, 64, P)
+        round_dealt("scalar", 1, 0, 0, 64)
+        quant_w1(1, 2, 0, PACK)
+        embed_pass(1, 2, 0, 0, 2)
+        w_bf[(2, 2)] = sb([P, PACK * K_PASS], BF16, "w_bf22")[:]
+        round_dealt("scalar", 2, 0, 0, 64)
+        round_dealt("vector", 2, 0, 64, P)
+        sim = [sb([P, PACK, PAIRS], F32, "sim0", "raw2_512"), sb([P, PACK, PAIRS], F32, "sim1", "tab_w2")]
+        nc.scalar.activation(sim[0][:, 0, :], dist0[:], ACT.Exp, scale=-1.0)
+        deal(0)
+        quant_w1(2, 2, 0, PACK)
+        embed_pass(2, 2, 0, 0, 2)
+        for a in (2, 1):
+            embed_pass(a, 2, 1, 0, 1)
+        for t in range(2, PACK):
             for half in range(2):
-                for a in order:
-                    embed_pass(a, 1, t, order[-1], (half,))
-        late = sb([P, 6 * PAIRS], F32, "late", "w_bf21")
-        pick(3, late[:, :PAIRS], 0, whole)
-        pick(3, late[:, 5 * PAIRS :], 1, whole)
-        diff02, diff03 = late[:, PAIRS : 2 * PAIRS], late[:, 2 * PAIRS : 3 * PAIRS]
-        lanes = late[:, 3 * PAIRS : 5 * PAIRS].bitcast(BF16).rearrange("p (t j) -> p t j", t=PACK)
-        nc.gpsimd.tensor_tensor(diff02, mid[:, 2, :], mid[:, 3, :], ALU.subtract)
+                for a in (2, 0, 1):
+                    embed_pass(a, 2, t, 2, 1, (half,))
+        late = sb([P, 4 * PAIRS], F32, "late", "w_bf22")
+        pair3 = late[:, : 2 * PAIRS].rearrange("p (s j) -> p s j", s=2)
+        for side in range(2):
+            pick(3, pair3[:, side, :], side, whole)
+        diffs = [diff0[:], late[:, 2 * PAIRS : 3 * PAIRS], late[:, 3 * PAIRS :], sb([P, PAIRS], F32, "diff3")[:]]
+        dist = sb([P, PACK - 1, PAIRS], F32, "dist", "tab_w0")
 
-        def weigh_lane(t):
-            nc.gpsimd.tensor_scalar(lanes[:, t, :], sim[0][:, t, :], gain_sb[:, 0, t : t + 1], 0.0, ALU.mult, ALU.add)
+        pairs = sb([P, 2 * PACK, PAIRS], F32, "pairs")
+        diffb = sb([P, PACK, PAIRS], F32, "diffb", "raw1_512")
+        distb = sb([P, PACK, PAIRS], F32, "distb")
 
-        dist0 = sb([P, PACK, PAIRS], F32, "dist0", "raw21_0")
-        closeness(diff0[:, 0, :], dist0[:, 0, :], sim[0][:, 0, :])
-        drain_h(1, 0)
-        closeness(diff0[:, 1, :], dist0[:, 1, :], sim[0][:, 1, :])
-        weigh_lane(0)
-        weigh_lane(1)
-        nc.gpsimd.tensor_tensor(diff03, late[:, :PAIRS], late[:, 5 * PAIRS :], ALU.subtract)
-        drain_h(1, 1)
-        closeness(diff02, dist0[:, 2, :], sim[0][:, 2, :])
-        drain_h(1, 2)
-        closeness(diff03, dist0[:, 3, :], sim[0][:, 3, :])
-        drain_h(1, 3)
-        diff1 = sb([P, PACK, PAIRS], F32, "diff1", "raw10_0")
-        dist1 = sb([P, PACK, PAIRS], F32, "dist1", "raw20_0")
-        second = sb([P, PACK - 1, PAIRS], F32, "second", "raw11_0")
+        def pick_lane(t):
+            for side in range(2):
+                pick(4 + t, pairs[:, 2 * t + side, :], side, whole)
+            less(diffb[:, t, :], pairs[:, 2 * t, :], pairs[:, 2 * t + 1, :])
+
+        def apart(u):
+            nc.scalar.activation(dist[:, u - 1, :], diffs[u], ACT.Abs)
+
+        def near(u):
+            nc.scalar.activation(sim[0][:, u, :], dist[:, u - 1, :], ACT.Exp, scale=-1.0)
+
+        def drain(u, half, tag=None):
+            if half == 0:
+                h[u] = sb([P, S], F32, "h%d" % u, tag)
+            nc.scalar.copy(h[u][:, BANK * half : BANK * (half + 1)], acc[(u, half)][:])
+
+        less(diffs[1], pair1[:, 0, :], pair1[:, 1, :])
+        less(diffs[2], pair2[:, 0, :], pair2[:, 1, :])
+        apart(1)
+        drain(4, 0, "h0")
+        drain(4, 1)
+        near(1)
+        less(diffs[3], pair3[:, 0, :], pair3[:, 1, :])
+        deal(1)
+        drain(5, 0, "h1")
+        apart(2)
+        drain(5, 1)
+        near(2)
+        deal(2)
+        pick_lane(0)
+        drain(6, 0, "h2")
+        apart(3)
+        drain(6, 1)
+        near(3)
+        deal(3)
+        pick_lane(1)
+        drain(7, 0, "h3")
+        drain(7, 1)
+        pick_lane(2)
         for t in range(PACK - 1):
-            pick(t, first[1][:, t, :], 0, whole)
-            pick(t, second[:, t, :], 1, whole)
-            diff = diff1[:, t, :] if t < 2 else sb([P, PAIRS], F32, "diff12", "tab_w2")[:]
-            nc.gpsimd.tensor_tensor(diff, first[1][:, t, :], second[:, t, :], ALU.subtract)
-            if t < 2:
-                weigh_lane(2 + t)
-            closeness(diff, dist1[:, t, :], sim[1][:, t, :])
+            closeness(diffb[:, t, :], distb[:, t, :], sim[1][:, t, :])
         t = PACK - 1
-        pick(t, first[1][:, t, :])
-        pick_less(t, first[1][:, t, :], diff1[:, t, :])
+        pick(4 + t, pairs[:, 2 * t, :], 0, halves)
+        pick_less(4 + t, pairs[:, 2 * t, :], diffb[:, t, :], halves)
         for cols in halves:
-            closeness(diff1[:, t, cols], dist1[:, t, cols], sim[1][:, t, cols])
+            closeness(diffb[:, t, cols], distb[:, t, cols], sim[1][:, t, cols])
 
-        z_c = [sb([P, PAIRS], U32, "z_c0"), sb([P, PAIRS], U32, "z_c1")]
-        z_s = [sb([P, PAIRS], U8, "z_s%d" % b) for b in range(R_PASSES)]
-        z = [sb([P, PAIRS, PACK], BF16, "z0", "h3"), sb([P, PAIRS, PACK], BF16, "z1")]
+        blocks = [slice(JB * c, JB * (c + 1)) for c in range(PAIRS // JB)]
+        z0 = sb([P, PAIRS, PACK], BF16, "z0", "h3")
+        z1_all = sb([P, PAIRS, PACK], BF16, "z1", "z_nat")
+        z1 = [z1_all[:, cols, :] for cols in blocks]
+        z_c = {}
+        z_s = {}
 
-        def quant_z(b, z_bf, cols):
-            nc.vector.quantize_mx(out=z_c[b][:, cols].bitcast(FP8X4), scales=z_s[b][:, cols], in_=z_bf[:, cols, :].rearrange("p j t -> p (j t)"))
+        def quant_z(b, c0, c1, z_bf, tag=None):
+            codes = sb([P, JB * (c1 - c0)], U32, "z_c%d%d" % (b, c0), tag)
+            scales = sb([P, JB * (c1 - c0)], U8, "z_s%d%d" % (b, c0))
+            nc.vector.quantize_mx(out=codes[:].bitcast(FP8X4), scales=scales[:], in_=z_bf.rearrange("p j t -> p (j t)"))
+            for c in range(c0, c1):
+                z_c[(b, c)] = codes[:, JB * (c - c0) : JB * (c - c0 + 1)]
+                z_s[(b, c)] = scales[:, JB * (c - c0) : JB * (c - c0 + 1)]
 
         y = [psum.tile([P, N // P, JB], F32, name="y", tag="bank%d" % (4 + c)) for c in range(PAIRS // JB)]
 
         def score(b, c):
-            cols = slice(JB * c, JB * (c + 1))
             for nt in range(N // P):
                 nc.tensor.matmul_mx(
                     out=y[c][:, nt, :],
                     lhsT=w2_w[:, b, :].bitcast(U8)[:, 2 * P * nt : 2 * P * (nt + 1)].bitcast(FP4X4),
                     lhsT_scale=w2_s[:, b, :].bitcast(U8)[:, P * nt : P * (nt + 1)],
-                    rhs=z_c[b][:, cols].bitcast(FP8X4),
-                    rhs_scale=z_s[b][:, cols],
+                    rhs=z_c[(b, c)].bitcast(FP8X4),
+                    rhs_scale=z_s[(b, c)],
                     start=(b == 0 and nt == 0),
                     stop=(b == 1 and nt == N // P - 1),
                 )
@@ -273,28 +357,29 @@ def tile_list_duplicate_pair_score_kernel(tc, tab_words, tab_scales, offs, w1, p
                 nc.scalar.activation(o[:, n0 : n0 + step, :], y[c][:, n0 : n0 + step, :], ACT.Sigmoid)
                 nc.sync.dma_start(out[P * n0 : P * (n0 + step), cols].rearrange("(nt p) j -> p nt j", p=P), o[:, n0 : n0 + step, :])
 
-        def weave(cols):
-            nc.vector.tensor_copy(z[0][:, cols, :].rearrange("p (c i) t -> p c t i", i=4), lanes[:, :, cols].rearrange("p t (c i) -> p c t i", i=4))
-
         def weigh(c):
-            cols = slice(JB * c, JB * (c + 1))
             nc.vector.tensor_tensor(
-                z[1][:, cols, :].rearrange("p (c i) t -> p c t i", i=4),
-                sim[1][:, :, cols].rearrange("p t (c i) -> p c t i", i=4),
-                gain_sb[:, 1, :].unsqueeze(1).unsqueeze(3).to_broadcast([P, JB // 4, PACK, 4]),
+                z1[c].rearrange("p (c i) t -> p c t i", i=4),
+                sim[1][:, :, blocks[c]].rearrange("p t (c i) -> p c t i", i=4),
+                gain_sb[:].unsqueeze(1).unsqueeze(3).to_broadcast([P, JB // 4, PACK, 4]),
                 ALU.mult,
             )
 
-        for cols in halves:
-            weave(cols)
-        quant_z(0, z[0], halves[0])
-        weigh(0)
-        quant_z(0, z[0], halves[1])
-        for c in range(PAIRS // JB):
-            score(0, c)
-        for c in range(PAIRS // JB):
-            if c + 1 < PAIRS // JB:
-                weigh(c + 1)
-            quant_z(1, z[1], slice(JB * c, JB * (c + 1)))
+        def weave(cols):
+            nc.vector.tensor_copy(z0[:, cols, :].rearrange("p (c i) t -> p c t i", i=4), lanes[:, :, cols].rearrange("p t (c i) -> p c t i", i=4))
+
+        def close(c):
+            quant_z(1, c, c + 1, z1[c])
             score(1, c)
             finish(c)
+
+        for half, cols in enumerate(halves):
+            c0 = 2 * half
+            weave(cols)
+            weigh(c0)
+            quant_z(0, c0, c0 + 2, z0[:, cols, :])
+            score(0, c0)
+            close(c0)
+            score(0, c0 + 1)
+            weigh(c0 + 1)
+            close(c0 + 1)

@@ -159,13 +159,6 @@ def tile_list_duplicate_pair_score_kernel(tc, tab_words, tab_scales, offs, w1, p
             for cols in parts:
                 nc.vector.tensor_tensor(dst[:, cols], h[u][:].indirect(pos_sb[1][:, cols.start // 16 : cols.stop // 16]), first[:, cols], ALU.subtract)
 
-        def closeness(diff, dist, sim):
-            nc.scalar.activation(dist, diff, ACT.Abs)
-            nc.scalar.activation(sim, dist, ACT.Exp, scale=-1.0)
-
-        def less(diff, first, second):
-            nc.gpsimd.tensor_tensor(diff, first, second, ALU.subtract)
-
         for a in range(K_PASSES):
             w_bf[(a, 0)] = sb([P, PACK * CHUNK], BF16, "w_bf%d0" % a)[:]
             w_c[(a, 0)] = sb([P, CHUNK], U32, "w_c%d0" % a)[:]
@@ -215,45 +208,61 @@ def tile_list_duplicate_pair_score_kernel(tc, tab_words, tab_scales, offs, w1, p
             embed_pass(a, 1, 0, 0, 2)
         for a in (2, 1):
             embed_pass(a, 1, 1, 0, 1)
-        pair1 = sb([P, 2, PAIRS], F32, "pair1", "w_bf21")
-        for side in range(2):
-            pick(1, pair1[:, side, :], side, whole)
-        z_nat = sb([P, PACK, PAIRS], BF16, "z_nat")
+        def pick_both(u, first, diff):
+            pick(u, first, 0, halves)
+            pick_less(u, first, diff, halves)
+
+        diffs = [diff0[:]] + [sb([P, PAIRS], F32, "diff%d" % u)[:] for u in range(1, H // P)]
+        pick_both(1, sb([P, PAIRS], F32, "first1", "w_bf21")[:], diffs[1])
         lanes = sb([P, PACK, PAIRS], BF16, "lanes")
+        dists = [sb([P, PAIRS], F32, "dist0", "raw2_256")[:]]
 
-        def deal(u):
+        def apart(u, cols=whole[0]):
+            nc.scalar.activation(dists[u][:, cols], diffs[u][:, cols], ACT.Abs)
+
+        def near(u, cols=whole[0]):
+            nc.scalar.activation(sim[u // PACK][:, u % PACK, cols], dists[u][:, cols], ACT.Exp, scale=-1.0)
+
+        def drain(u, half, tag=None):
+            if half == 0:
+                h[u] = sb([P, S], F32, "h%d" % u, tag)
+            nc.scalar.copy(h[u][:, BANK * half : BANK * (half + 1)], acc[(u, half)][:])
+
+        def deal(u, tag):
+            z_nat = sb([P, PAIRS], BF16, "z_nat%d" % u, tag)
             if u == 0:
-                nc.scalar.activation(z_nat[:, u, :], sim[0][:, u, :], ACT.Copy, scale=gain_nat[:, u : u + 1])
+                nc.scalar.activation(z_nat[:], sim[0][:, u, :], ACT.Copy, scale=gain_nat[:, u : u + 1])
             else:
-                nc.gpsimd.tensor_scalar(z_nat[:, u, :], sim[0][:, u, :], gain_nat[:, u : u + 1], 0.0, ALU.mult, ALU.add)
+                nc.gpsimd.tensor_scalar(z_nat[:], sim[0][:, u, :], gain_nat[:, u : u + 1], 0.0, ALU.mult, ALU.add)
             for t in range(PACK):
-                nc.sync.dma_start(lanes[32 * u : 32 * (u + 1), t, :], z_nat[t:P:PACK, u, :])
+                nc.sync.dma_start(lanes[32 * u : 32 * (u + 1), t, :], z_nat[t:P:PACK, :])
 
-        dist0 = sb([P, PAIRS], F32, "dist0", "raw2_256")
-        nc.scalar.activation(dist0[:], diff0[:], ACT.Abs)
+        apart(0)
         w_bf[(0, 2)] = sb([P, PACK * K_PASS], BF16, "w_bf02", "w_bf11")[:]
         round_dealt("scalar", 0, 0, 0, 64)
-        round_dealt("gpsimd", 0, 64, 64, P)
+        round_dealt("scalar", 0, 64, 64, 96)
+        round_dealt("gpsimd", 0, 64, 96, P)
         drain_h(2, "h2")
         drain_h(3, "h3")
         quant_w1(0, 2, 0, PACK)
         for t in range(2):
             embed_pass(0, 2, t, 0, 2 - t)
-        mid = sb([P, 4 * PAIRS], F32, "mid", "w_bf11")
-        pair2 = mid[:, : 2 * PAIRS].rearrange("p (s j) -> p s j", s=2)
-        w_bf[(1, 2)] = mid[:, 2 * PAIRS :].bitcast(BF16)
-        for side in range(2):
-            pick(2, pair2[:, side, :], side, whole)
-        round_dealt("gpsimd", 1, 0, 64, P)
-        round_dealt("scalar", 1, 0, 0, 64)
+        mid = sb([P, 3 * PAIRS], F32, "mid", "w_bf11")
+        w_bf[(1, 2)] = mid[:, PAIRS:].bitcast(BF16)
+        pick_both(2, mid[:, :PAIRS], diffs[2])
+        round_dealt("gpsimd", 1, 0, 96, P)
+        round_dealt("scalar", 1, 0, 0, 96)
         quant_w1(1, 2, 0, PACK)
         embed_pass(1, 2, 0, 0, 2)
         w_bf[(2, 2)] = sb([P, PACK * K_PASS], BF16, "w_bf22")[:]
         round_dealt("scalar", 2, 0, 0, 64)
         round_dealt("vector", 2, 0, 64, P)
-        sim = [sb([P, PACK, PAIRS], F32, "sim0", "raw2_512"), sb([P, PACK, PAIRS], F32, "sim1", "tab_w2")]
-        nc.scalar.activation(sim[0][:, 0, :], dist0[:], ACT.Exp, scale=-1.0)
-        deal(0)
+        late = sb([P, PACK + H // P - 2, PAIRS], F32, "late", "raw2_512")
+        sim = [late[:, :PACK, :], sb([P, PACK, PAIRS], F32, "sim1", "tab_w2")]
+        dists.extend([late[:, PACK + min(u, 6) - 1, :] for u in range(1, H // P)])
+        near(0)
+        apart(1)
+        deal(0, None)
         quant_w1(2, 2, 0, PACK)
         embed_pass(2, 2, 0, 0, 2)
         for a in (2, 1):
@@ -262,67 +271,37 @@ def tile_list_duplicate_pair_score_kernel(tc, tab_words, tab_scales, offs, w1, p
             for half in range(2):
                 for a in (2, 0, 1):
                     embed_pass(a, 2, t, 2, 1, (half,))
-        late = sb([P, 4 * PAIRS], F32, "late", "w_bf22")
-        pair3 = late[:, : 2 * PAIRS].rearrange("p (s j) -> p s j", s=2)
-        for side in range(2):
-            pick(3, pair3[:, side, :], side, whole)
-        diffs = [diff0[:], late[:, 2 * PAIRS : 3 * PAIRS], late[:, 3 * PAIRS :], sb([P, PAIRS], F32, "diff3")[:]]
-        dist = sb([P, PACK - 1, PAIRS], F32, "dist", "tab_w0")
-
-        pairs = sb([P, 2 * PACK, PAIRS], F32, "pairs")
-        diffb = sb([P, PACK, PAIRS], F32, "diffb", "raw1_512")
-        distb = sb([P, PACK, PAIRS], F32, "distb")
-
-        def pick_lane(t):
-            for side in range(2):
-                pick(4 + t, pairs[:, 2 * t + side, :], side, whole)
-            less(diffb[:, t, :], pairs[:, 2 * t, :], pairs[:, 2 * t + 1, :])
-
-        def apart(u):
-            nc.scalar.activation(dist[:, u - 1, :], diffs[u], ACT.Abs)
-
-        def near(u):
-            nc.scalar.activation(sim[0][:, u, :], dist[:, u - 1, :], ACT.Exp, scale=-1.0)
-
-        def drain(u, half, tag=None):
-            if half == 0:
-                h[u] = sb([P, S], F32, "h%d" % u, tag)
-            nc.scalar.copy(h[u][:, BANK * half : BANK * (half + 1)], acc[(u, half)][:])
-
-        less(diffs[1], pair1[:, 0, :], pair1[:, 1, :])
-        less(diffs[2], pair2[:, 0, :], pair2[:, 1, :])
-        apart(1)
+        pick_both(3, sb([P, PAIRS], F32, "first3", "w_bf22")[:], diffs[3])
         drain(4, 0, "h0")
         drain(4, 1)
         near(1)
-        less(diffs[3], pair3[:, 0, :], pair3[:, 1, :])
-        deal(1)
+        deal(1, "w_bf22")
+        pick_both(4, sb([P, PAIRS], F32, "first4")[:], diffs[4])
         drain(5, 0, "h1")
-        apart(2)
         drain(5, 1)
-        near(2)
-        deal(2)
-        pick_lane(0)
-        drain(6, 0, "h2")
+        apart(2)
         apart(3)
-        drain(6, 1)
+        near(2)
+        deal(2, "first4")
+        pick_both(5, sb([P, PAIRS], F32, "first5")[:], diffs[5])
         near(3)
-        deal(3)
-        pick_lane(1)
+        deal(3, "first5")
+        drain(6, 0, "h2")
+        drain(6, 1)
+        pick_both(6, sb([P, PAIRS], F32, "first6")[:], diffs[6])
         drain(7, 0, "h3")
         drain(7, 1)
-        pick_lane(2)
-        for t in range(PACK - 1):
-            closeness(diffb[:, t, :], distb[:, t, :], sim[1][:, t, :])
-        t = PACK - 1
-        pick(4 + t, pairs[:, 2 * t, :], 0, halves)
-        pick_less(4 + t, pairs[:, 2 * t, :], diffb[:, t, :], halves)
+        pick_both(7, sb([P, PAIRS], F32, "first7")[:], diffs[7])
+        for u in (4, 5, 6):
+            apart(u)
+            near(u)
         for cols in halves:
-            closeness(diffb[:, t, cols], distb[:, t, cols], sim[1][:, t, cols])
+            apart(7, cols)
+            near(7, cols)
 
         blocks = [slice(JB * c, JB * (c + 1)) for c in range(PAIRS // JB)]
         z0 = sb([P, PAIRS, PACK], BF16, "z0", "h3")
-        z1_all = sb([P, PAIRS, PACK], BF16, "z1", "z_nat")
+        z1_all = sb([P, PAIRS, PACK], BF16, "z1", "first5")
         z1 = [z1_all[:, cols, :] for cols in blocks]
         z_c = {}
         z_s = {}

@@ -21,31 +21,35 @@ PACK = 4
 K_PASS = P * PACK
 K_PASSES = K // K_PASS
 R_PASSES = H // K_PASS
+TILES = H // P
 BANK = 512
 JB = 128
-CHUNK = 256
+HALF = PAIRS // 2
+SLOT = 6656
+STEPS = TILES - 2
+ON_VECTOR = 7
 
 
 def tile_list_duplicate_pair_score_kernel(tc, tab_words, tab_scales, offs, w1, pos1, pos2, gain, w2_words, w2_scales, out):
     nc = tc.nc
     with ExitStack() as ctx:
         keep = ctx.enter_context(tc.tile_pool(name="keep", bufs=1))
+        shared = ctx.enter_context(tc.tile_pool(name="shared", bufs=1))
         psum = ctx.enter_context(tc.psum_pool(name="psum", bufs=1))
 
         def sb(shape, dtype, name, tag=None):
             return keep.tile(shape, dtype, name=name, tag=tag or name, align_bytes=64)
 
-        def bank(name, i):
-            return psum.tile([P, BANK], F32, name=name, tag="bank%d" % i)
+        def placed(shape, dtype, name, offset):
+            return shared.tile(shape, dtype, name=name, tag=name, align_bytes=64, offset=offset)
 
         offs_sb = keep.tile([P, S // 16], U16, name="offs_sb")
         pos_sb = [keep.tile([P, PAIRS // 16], U16, name="pos_sb%d" % i) for i in range(2)]
         tab_w = [sb([P, T], I32, "tab_w%d" % a) for a in range(K_PASSES)]
         tab_s = sb([P, T // 4], I32, "tab_s")
-        v_w = [sb([P, S], U32, "v_w%d" % a) for a in range(K_PASSES - 1)]
+        v_w = [sb([P, S], U32, "v_w%d" % a) for a in range(K_PASSES)]
         v_s = sb([P, S], U8, "v_s")
-        gain_nat = sb([P, PACK], F32, "gain_nat")
-        gain_sb = sb([P, PACK], F32, "gain_sb")
+        gain_sb = sb([P, TILES], F32, "gain_sb")
         w2_w = sb([P, R_PASSES, 2 * N // 4], I32, "w2_w")
         w2_s = sb([P, R_PASSES, N // 4], I32, "w2_s")
 
@@ -59,31 +63,30 @@ def tile_list_duplicate_pair_score_kernel(tc, tab_words, tab_scales, offs, w1, p
         def load_tab(a):
             nc.sync.dma_start(tab_w[a][:], tab_words[a].rearrange("p t i -> p (t i)").bitcast(I32))
 
-        def load_w1(a, c0, c1):
-            t = sb([P, PACK, c1 - c0], F32, "raw%d_%d" % (a, c0))
-            nc.sync.dma_start(t[:], w1[K_PASS * a : K_PASS * (a + 1), c0:c1].rearrange("(p j) c -> p j c", j=PACK))
-            raw[(a, c0)] = t
+        def load_w1(u, a):
+            if u >= 2 and a == 2:
+                raw[(u, a)] = placed([P, PACK, P], F32, "raw%d%d" % (u, a), SLOT * (u - 2) + 3584)
+            else:
+                raw[(u, a)] = sb([P, PACK, P], F32, "raw%d%d" % (u, a))
+            nc.sync.dma_start(raw[(u, a)][:], w1[K_PASS * a : K_PASS * (a + 1), P * u : P * (u + 1)].rearrange("(p j) c -> p j c", j=PACK))
 
         nc.sync.dma_start(offs_sb[:], offs)
         load_tab(0)
         for q in range(2, 4):
             nc.sync.dma_start(tab_s[32 * q : 32 * q + 4 * K_PASSES, :], tab_scales[:, 4 * q : 4 * q + 4, :].bitcast(I32))
+        for a in range(K_PASSES):
+            load_w1(0, a)
         load_tab(1)
-        load_w1(0, 0, CHUNK)
         load_tab(2)
-        load_w1(1, 0, CHUNK)
-        load_w1(2, 0, CHUNK)
+        for a in range(K_PASSES):
+            load_w1(1, a)
         nc.sync.dma_start(pos_sb[0][:], pos1)
         nc.sync.dma_start(pos_sb[1][:], pos2)
-        for a in range(K_PASSES):
-            load_w1(a, CHUNK, 2 * CHUNK)
-        load_w1(0, K_PASS, K_PASS + CHUNK)
-        load_w1(0, K_PASS + CHUNK, H)
-        load_w1(1, K_PASS, H)
-        load_w1(2, K_PASS, H)
+        for u in range(2, TILES):
+            for a in range(K_PASSES):
+                load_w1(u, a)
         with nc.allow_non_contiguous_dma(reason="one gain a partition"):
-            nc.sync.dma_start(gain_nat[:], gain[:K_PASS].rearrange("(u p) -> p u", p=P))
-        nc.sync.dma_start(gain_sb[:], gain[K_PASS:].rearrange("(p t) -> p t", t=PACK))
+            nc.sync.dma_start(gain_sb[:], gain.rearrange("(u p) -> p u", p=P))
         for q in range(4):
             nc.sync.dma_start(w2_s[32 * q : 32 * q + 4, :, :], w2_scales[:, 4 * q : 4 * q + 4, :].bitcast(I32).rearrange("b r n -> r b n"))
         nc.sync.dma_start(w2_w[:], w2_words.bitcast(I32).rearrange("b p n -> p b n"))
@@ -91,230 +94,223 @@ def tile_list_duplicate_pair_score_kernel(tc, tab_words, tab_scales, offs, w1, p
         w_bf = {}
         w_c = {}
         w_s = {}
+        planes = {}
 
-        def round_plain(engine, a, c, c0, c1):
-            src = raw[(a, CHUNK * c)][:, :, c0:c1]
-            dst = w_bf[(a, c)].rearrange("p (c j) -> p c j", j=PACK)[:, c0:c1, :]
+        def round_w1(engine, u, a, tag=None):
+            w_bf[(u, a)] = sb([P, P, PACK], BF16, "w_bf%d%d" % (u, a), tag)
             if engine == "gpsimd":
-                nc.gpsimd.tensor_scalar(dst, src.rearrange("p j c -> p c j"), 1.0, 0.0, ALU.mult, ALU.add)
+                nc.gpsimd.tensor_scalar(w_bf[(u, a)][:], raw[(u, a)][:].rearrange("p j c -> p c j"), 1.0, 0.0, ALU.mult, ALU.add)
             elif engine == "scalar":
-                nc.scalar.copy(dst.rearrange("p (c i) j -> p c j i", i=4), src.rearrange("p j (c i) -> p c j i", i=4))
+                nc.scalar.copy(w_bf[(u, a)][:].rearrange("p (c i) j -> p c j i", i=4), raw[(u, a)][:].rearrange("p j (c i) -> p c j i", i=4))
             else:
-                nc.vector.tensor_copy(dst.rearrange("p (c i) j -> p c j i", i=4), src.rearrange("p j (c i) -> p c j i", i=4))
-
-        def round_dealt(engine, a, base, m0, m1):
-            src = raw[(a, K_PASS + PACK * base)][:, :, PACK * (m0 - base) : PACK * (m1 - base)]
-            dst = w_bf[(a, 2)].rearrange("p (t m j) -> p t m j", t=PACK, j=PACK)[:, :, m0:m1, :]
-            if engine == "gpsimd":
-                nc.gpsimd.tensor_scalar(dst, src.rearrange("p j (m t) -> p t m j", t=PACK), 1.0, 0.0, ALU.mult, ALU.add)
-            elif engine == "scalar":
-                nc.scalar.copy(dst.rearrange("p t m j -> p m j t"), src.rearrange("p j (m t) -> p m j t", t=PACK))
-            else:
-                nc.vector.tensor_copy(dst.rearrange("p (s e) m j -> p s m j e", e=2), src.rearrange("p j (m s e) -> p s m j e", s=2, e=2))
-
-        def quant_w1(a, c, t0, t1):
-            cols = slice(P * t0, P * t1)
-            nc.vector.quantize_mx(out=w_c[(a, c)][:, cols].bitcast(FP8X4), scales=w_s[(a, c)][:, cols], in_=w_bf[(a, c)][:, K_PASS * t0 : K_PASS * t1])
-
-        def gather_tab(a):
-            nc.vector.tensor_copy(v_w[a][:], tab_w[a][:].bitcast(U32).indirect(offs_sb[:]))
+                nc.vector.tensor_copy(w_bf[(u, a)][:].rearrange("p (c i) j -> p c j i", i=4), raw[(u, a)][:].rearrange("p j (c i) -> p c j i", i=4))
 
         acc = {}
 
-        def embed_pass(a, c, t, opening, last, halves=(0, 1)):
-            u = 2 * c + t
-            for half in halves:
-                if a == opening:
-                    acc[(u, half)] = bank("acc", (2 * u + half) % 8)
-                cols = slice(BANK * half, BANK * (half + 1))
-                nc.tensor.matmul_mx(
-                    out=acc[(u, half)][:],
-                    lhsT=w_c[(a, c)][:, P * t : P * (t + 1)].bitcast(FP8X4),
-                    lhsT_scale=w_s[(a, c)][:, P * t : P * (t + 1)],
-                    rhs=v_w[a][:, cols].bitcast(FP8X4),
-                    rhs_scale=v_s[4 * a : P, cols],
-                    start=(a == opening),
-                    stop=(a == last),
-                )
+        def embed(u, a, half):
+            if a == 0:
+                acc[(u, half)] = psum.tile([P, BANK], F32, name="acc", tag="bank%d" % ((2 * u + half) % 8))
+            cols = slice(BANK * half, BANK * (half + 1))
+            nc.tensor.matmul_mx(
+                out=acc[(u, half)][:],
+                lhsT=w_c[(u, a)][:].bitcast(FP8X4),
+                lhsT_scale=w_s[(u, a)],
+                rhs=v_w[a][:, cols].bitcast(FP8X4),
+                rhs_scale=v_s[4 * a : P, cols],
+                start=(a == 0),
+                stop=(a == (1 if u >= 2 else 2)),
+            )
+
+        def quant_w1(u, a):
+            w_c[(u, a)] = sb([P, P], U32, "w_c%d%d" % (u, a))
+            if (u, a) == (ON_VECTOR, 0):
+                w_s[(u, a)] = sb([P, P], U8, "w_s_early")[:]
+            else:
+                if u not in planes and u >= 2:
+                    planes[u] = placed([P, K_PASSES * P], U8, "w_s%d" % u, SLOT * (u - 2) + 4096)
+                elif u not in planes:
+                    planes[u] = sb([P, K_PASSES * P], U8, "w_s%d" % u)
+                w_s[(u, a)] = planes[u][:, P * a : P * (a + 1)]
+            nc.vector.quantize_mx(out=w_c[(u, a)][:].bitcast(FP8X4), scales=w_s[(u, a)], in_=w_bf[(u, a)][:].rearrange("p c j -> p (c j)"))
+
+        def quant_embed(u, a):
+            quant_w1(u, a)
+            for half in range(2):
+                embed(u, a, half)
+
+        def gather_tab(a, c0, c1):
+            nc.vector.tensor_copy(v_w[a][:, c0:c1], tab_w[a][:].bitcast(U32).indirect(offs_sb[:, c0 // 16 : c1 // 16]))
 
         h = {}
 
-        def drain_h(u, tag, vec_halves=()):
-            h[u] = sb([P, S], F32, "h%d" % u, tag)
-            for half in range(S // BANK):
-                dst = h[u][:, BANK * half : BANK * (half + 1)]
-                if half in vec_halves:
-                    nc.vector.tensor_copy(dst, acc[(u, half)][:])
-                else:
-                    nc.scalar.copy(dst, acc[(u, half)][:])
-
-        halves = [slice(0, PAIRS // 2), slice(PAIRS // 2, PAIRS)]
-        whole = [slice(0, PAIRS)]
-
-        def pick(u, dst, side, parts):
-            for cols in parts:
-                nc.vector.tensor_copy(dst[:, cols], h[u][:].indirect(pos_sb[side][:, cols.start // 16 : cols.stop // 16]))
-
-        def pick_less(u, first, dst, parts):
-            for cols in parts:
-                nc.vector.tensor_tensor(dst[:, cols], h[u][:].indirect(pos_sb[1][:, cols.start // 16 : cols.stop // 16]), first[:, cols], ALU.subtract)
-
-        for a in range(K_PASSES):
-            w_bf[(a, 0)] = sb([P, PACK * CHUNK], BF16, "w_bf%d0" % a)[:]
-            w_c[(a, 0)] = sb([P, CHUNK], U32, "w_c%d0" % a)[:]
-            w_c[(a, 2)] = sb([P, K_PASS], U32, "w_c%d2" % a)[:]
-            for c in range(3):
-                w_s[(a, c)] = sb([P, K_PASS if c == 2 else CHUNK], U8, "w_s%d%d" % (a, c))[:]
-
-        gather_tab(0)
-        nc.vector.tensor_copy(v_s[:], tab_s[:].bitcast(U8).indirect(offs_sb[:]))
-        gather_tab(1)
-        round_plain("scalar", 0, 0, 0, CHUNK)
-        quant_w1(0, 0, 0, 2)
-        for t in range(2):
-            embed_pass(0, 0, t, 0, 2 - t)
-        v_w.append(sb([P, S], U32, "v_w2", "w_bf00"))
-        gather_tab(2)
-        round_plain("scalar", 1, 0, 0, CHUNK)
-        round_plain("vector", 2, 0, 0, P)
-        quant_w1(1, 0, 0, 2)
-        embed_pass(1, 0, 0, 0, 2)
-        round_plain("scalar", 2, 0, P, CHUNK)
-        quant_w1(2, 0, 0, 1)
-        embed_pass(2, 0, 0, 0, 2)
-        quant_w1(2, 0, 1, 2)
-        for a in (2, 1):
-            embed_pass(a, 0, 1, 0, 1)
-        drain_h(0, "h0", (1,))
-        drain_h(1, "h1")
-
-        for a in range(K_PASSES):
-            w_bf[(a, 1)] = sb([P, PACK * CHUNK], BF16, "w_bf%d1" % a, "w_bf20" if a == 0 else None)[:]
-        round_plain("gpsimd", 0, 1, 0, CHUNK)
-        round_plain("gpsimd", 1, 1, 0, CHUNK)
-        round_plain("scalar", 2, 1, 0, CHUNK)
-        first0 = sb([P, PAIRS], F32, "first0")
-        diff0 = sb([P, PAIRS], F32, "diff0", "w_bf20")
-        pick(0, first0, 0, whole)
-        w_c[(0, 1)] = sb([P, CHUNK], U32, "w_c01")[:]
-        quant_w1(0, 1, 0, 2)
-        for t in range(2):
-            embed_pass(0, 1, t, 0, 2 - t)
-        pick_less(0, first0, diff0, whole)
-        w_c1 = sb([P, 2 * CHUNK], U32, "w_c1", "first0")
-        for a in range(1, K_PASSES):
-            w_c[(a, 1)] = w_c1[:, CHUNK * (a - 1) : CHUNK * a]
-            quant_w1(a, 1, 0, 2)
-            embed_pass(a, 1, 0, 0, 2)
-        for a in (2, 1):
-            embed_pass(a, 1, 1, 0, 1)
-        def pick_both(u, first, diff):
-            pick(u, first, 0, halves)
-            pick_less(u, first, diff, halves)
-
-        diffs = [diff0[:]] + [sb([P, PAIRS], F32, "diff%d" % u)[:] for u in range(1, H // P)]
-        pick_both(1, sb([P, PAIRS], F32, "first1", "w_bf21")[:], diffs[1])
-        lanes = sb([P, PACK, PAIRS], BF16, "lanes")
-        dists = [sb([P, PAIRS], F32, "dist0", "raw2_256")[:]]
-
-        def apart(u, cols=whole[0]):
-            nc.scalar.activation(dists[u][:, cols], diffs[u][:, cols], ACT.Abs)
-
-        def near(u, cols=whole[0]):
-            nc.scalar.activation(sim[u // PACK][:, u % PACK, cols], dists[u][:, cols], ACT.Exp, scale=-1.0)
-
-        def drain(u, half, tag=None):
+        def drain(u, half, engine="scalar"):
             if half == 0:
-                h[u] = sb([P, S], F32, "h%d" % u, tag)
-            nc.scalar.copy(h[u][:, BANK * half : BANK * (half + 1)], acc[(u, half)][:])
-
-        def deal(u, tag):
-            z_nat = sb([P, PAIRS], BF16, "z_nat%d" % u, tag)
-            if u == 0:
-                nc.scalar.activation(z_nat[:], sim[0][:, u, :], ACT.Copy, scale=gain_nat[:, u : u + 1])
+                if 1 <= u <= STEPS:
+                    h[u] = placed([P, S], F32, "h%d" % u, SLOT * (u - 1))
+                else:
+                    h[u] = sb([P, S], F32, "h%d" % u, "raw11" if u == 0 else None)
+            dst = h[u][:, BANK * half : BANK * (half + 1)]
+            if engine == "vector":
+                nc.vector.tensor_copy(dst, acc[(u, half)][:])
             else:
-                nc.gpsimd.tensor_scalar(z_nat[:], sim[0][:, u, :], gain_nat[:, u : u + 1], 0.0, ALU.mult, ALU.add)
-            for t in range(PACK):
-                nc.sync.dma_start(lanes[32 * u : 32 * (u + 1), t, :], z_nat[t:P:PACK, :])
+                nc.scalar.copy(dst, acc[(u, half)][:])
 
-        apart(0)
-        w_bf[(0, 2)] = sb([P, PACK * K_PASS], BF16, "w_bf02", "w_bf11")[:]
-        round_dealt("scalar", 0, 0, 0, 64)
-        round_dealt("scalar", 0, 64, 64, 96)
-        round_dealt("gpsimd", 0, 64, 96, P)
-        drain_h(2, "h2")
-        drain_h(3, "h3")
-        quant_w1(0, 2, 0, PACK)
-        for t in range(2):
-            embed_pass(0, 2, t, 0, 2 - t)
-        mid = sb([P, 3 * PAIRS], F32, "mid", "w_bf11")
-        w_bf[(1, 2)] = mid[:, PAIRS:].bitcast(BF16)
-        pick_both(2, mid[:, :PAIRS], diffs[2])
-        round_dealt("gpsimd", 1, 0, 96, P)
-        round_dealt("scalar", 1, 0, 0, 96)
-        quant_w1(1, 2, 0, PACK)
-        embed_pass(1, 2, 0, 0, 2)
-        w_bf[(2, 2)] = sb([P, PACK * K_PASS], BF16, "w_bf22")[:]
-        round_dealt("scalar", 2, 0, 0, 64)
-        round_dealt("vector", 2, 0, 64, P)
-        late = sb([P, PACK + H // P - 2, PAIRS], F32, "late", "raw2_512")
-        sim = [late[:, :PACK, :], sb([P, PACK, PAIRS], F32, "sim1", "tab_w2")]
-        dists.extend([late[:, PACK + min(u, 6) - 1, :] for u in range(1, H // P)])
-        near(0)
-        apart(1)
-        deal(0, None)
-        quant_w1(2, 2, 0, PACK)
-        embed_pass(2, 2, 0, 0, 2)
-        for a in (2, 1):
-            embed_pass(a, 2, 1, 0, 1)
-        for t in range(2, PACK):
+        halves = [slice(0, HALF), slice(HALF, PAIRS)]
+        whole = slice(0, PAIRS)
+        first = {}
+        diff = {}
+        dist = {}
+        near = {}
+        z_nat = {}
+
+        def pick(u, tag):
+            first[u] = sb([P, PAIRS], F32, "first%d" % u, tag)
+            nc.vector.tensor_copy(first[u][:], h[u][:].indirect(pos_sb[0][:]))
+
+        def pick_less(u, dst, cols):
+            nc.vector.tensor_tensor(dst, h[u][:].indirect(pos_sb[1][:, cols.start // 16 : cols.stop // 16]), first[u][:, cols], ALU.subtract)
+
+        def apart(key):
+            dist[key] = sb([P, PAIRS], F32, "dist%s" % key)
+            nc.scalar.activation(dist[key][:], diff[key][:, :], ACT.Abs)
+
+        def similar(key):
+            near[key] = sb([P, PAIRS], F32, "near%s" % key)
+            nc.scalar.activation(near[key][:], dist[key][:], ACT.Exp, scale=-1.0)
+
+        early = sb([P, PACK, PAIRS], BF16, "lanes0")
+        lanes = [[early[:, :, cols] for cols in halves], [sb([P, PACK, HALF], BF16, "lanes1%d" % i)[:] for i in range(2)]]
+
+        def weigh(engine, u, cols, src):
+            if engine == "scalar":
+                nc.scalar.activation(z_nat[u][:, cols], src, ACT.Copy, scale=gain_sb[:, u : u + 1])
+            elif engine == "gpsimd":
+                nc.gpsimd.tensor_scalar(z_nat[u][:, cols], src, gain_sb[:, u : u + 1], 0.0, ALU.mult, ALU.add)
+            else:
+                nc.vector.tensor_scalar(z_nat[u][:, cols], src, gain_sb[:, u : u + 1], None, ALU.mult)
+            rows = slice(32 * (u % PACK), 32 * (u % PACK + 1))
+            if u < PACK:
+                nc.sync.dma_start(early[rows, :, :], z_nat[u][:, :])
+            else:
+                for i in range(cols.start // HALF, cols.stop // HALF):
+                    nc.sync.dma_start(lanes[1][i][rows, :, :], z_nat[u][:, halves[i]])
+
+        def weighed_tiles(u0, u1, tag):
+            both = sb([P, (u1 - u0) * PAIRS], BF16, "z_nat%d" % u0, tag)
+            for u in range(u0, u1):
+                z_nat[u] = both[:, PAIRS * (u - u0) : PAIRS * (u - u0 + 1)]
+
+        gather_tab(0, 0, S)
+        nc.vector.tensor_copy(v_s[:], tab_s[:].bitcast(U8).indirect(offs_sb[:]))
+        for a in range(K_PASSES):
+            round_w1("scalar", 0, a)
+            quant_w1(0, a)
+        for half in range(2):
+            embed(0, 0, half)
+        gather_tab(1, 0, S)
+        for half in range(2):
+            embed(0, 1, half)
+        for half in range(2):
+            gather_tab(2, BANK * half, BANK * (half + 1))
+            embed(0, 2, half)
+        for a in range(K_PASSES):
+            round_w1("scalar", 1, a)
+        for a in range(2):
+            quant_embed(1, a)
+        drain(0, 0)
+        drain(0, 1, "vector")
+        quant_embed(1, 2)
+        round_w1("scalar", 2, 0)
+
+        steps = [(f, u) for u in range(STEPS) for f in (apart, similar)]
+
+        def catch_up(upto):
+            f, u = steps[0]
+            if u <= upto:
+                f(u)
+                steps.remove((f, u))
+
+        for u in range(STEPS):
+            round_w1("gpsimd", u + 2, 1, "turn%d" % ((u - 1) % 2) if u else "w_bf12")
+            round_w1("scalar", u + 2, 2)
+            pick(u, "turn%d" % (u % 2) if u else "raw12")
+            passes = (0, 2, 1) if u + 2 < ON_VECTOR else (2, 1)
+            for a in passes[:-1]:
+                quant_w1(u + 2, a)
+            if u + 3 == ON_VECTOR:
+                round_w1("vector", u + 3, 0, "w_bf%d0" % (u + 2))
+            quant_w1(u + 2, passes[-1])
             for half in range(2):
-                for a in (2, 0, 1):
-                    embed_pass(a, 2, t, 2, 1, (half,))
-        pick_both(3, sb([P, PAIRS], F32, "first3", "w_bf22")[:], diffs[3])
-        drain(4, 0, "h0")
-        drain(4, 1)
-        near(1)
-        deal(1, "w_bf22")
-        pick_both(4, sb([P, PAIRS], F32, "first4")[:], diffs[4])
-        drain(5, 0, "h1")
-        drain(5, 1)
-        apart(2)
-        apart(3)
-        near(2)
-        deal(2, "first4")
-        pick_both(5, sb([P, PAIRS], F32, "first5")[:], diffs[5])
-        near(3)
-        deal(3, "first5")
-        drain(6, 0, "h2")
-        drain(6, 1)
-        pick_both(6, sb([P, PAIRS], F32, "first6")[:], diffs[6])
-        drain(7, 0, "h3")
-        drain(7, 1)
-        pick_both(7, sb([P, PAIRS], F32, "first7")[:], diffs[7])
-        for u in (4, 5, 6):
-            apart(u)
-            near(u)
-        for cols in halves:
-            apart(7, cols)
-            near(7, cols)
+                for a in passes:
+                    embed(u + 2, a, half)
+            if u + 3 == ON_VECTOR:
+                quant_embed(u + 3, 0)
+            diff[u] = placed([P, PAIRS], F32, "diff%d" % u, SLOT * u + 4608)
+            pick_less(u, diff[u][:], whole)
+            catch_up(u - 1)
+            drain(u + 1, 0)
+            if u + 3 < ON_VECTOR:
+                round_w1("scalar", u + 3, 0)
+            else:
+                catch_up(u - 1)
+            drain(u + 1, 1)
 
-        blocks = [slice(JB * c, JB * (c + 1)) for c in range(PAIRS // JB)]
-        z0 = sb([P, PAIRS, PACK], BF16, "z0", "h3")
-        z1_all = sb([P, PAIRS, PACK], BF16, "z1", "first5")
-        z1 = [z1_all[:, cols, :] for cols in blocks]
+        last = [TILES - 2, TILES - 1]
+        weighed_tiles(0, 3, "turn%d" % ((STEPS - 1) % 2))
+        for u in range(3):
+            weigh("gpsimd", u, whole, near[u][:])
+        for half in range(2):
+            drain(TILES - 1, half)
+        for u in last:
+            pick(u, None)
+        for k in range(len(steps)):
+            catch_up(STEPS)
+        both = placed([P, 2 * PAIRS], F32, "diff_last", SLOT * 4 + 1024)
+        z_nat[3] = placed([P, PAIRS], BF16, "z_nat3", SLOT * 4 + 5120)
+        weighed_tiles(4, 6, None)
+        apart_last = sb([P, 2 * PAIRS], F32, "dist_last")
+        near_last = sb([P, 2 * PAIRS], F32, "near_last")
+        weighed_tiles(6, TILES, None)
+        pieces = [(u, cols) for cols in halves for u in last]
+
+        def own(k):
+            return slice(HALF * k, HALF * (k + 1))
+
+        def close(k):
+            nc.scalar.activation(near_last[:, own(k)], apart_last[:, own(k)], ACT.Exp, scale=-1.0)
+
+        for k, (u, cols) in enumerate(pieces):
+            pick_less(u, both[:, own(k)], cols)
+            if k > 0:
+                weigh("vector", 2 + k, whole, near[2 + k][:])
+            nc.scalar.activation(apart_last[:, own(k)], both[:, own(k)], ACT.Abs)
+            if k > 0:
+                close(k - 1)
+        close(len(pieces) - 1)
+
+        z = [[sb([P, HALF, PACK], BF16, "z00", "h7"), sb([P, HALF, PACK], BF16, "z01", "dist_last")], [sb([P, HALF, PACK], BF16, "z1%d" % i) for i in range(2)]]
         z_c = {}
         z_s = {}
+        y = [psum.tile([P, N // P, JB], F32, name="y", tag="bank%d" % c) for c in range(PAIRS // JB)]
 
-        def quant_z(b, c0, c1, z_bf, tag=None):
-            codes = sb([P, JB * (c1 - c0)], U32, "z_c%d%d" % (b, c0), tag)
-            scales = sb([P, JB * (c1 - c0)], U8, "z_s%d%d" % (b, c0))
-            nc.vector.quantize_mx(out=codes[:].bitcast(FP8X4), scales=scales[:], in_=z_bf.rearrange("p j t -> p (j t)"))
-            for c in range(c0, c1):
-                z_c[(b, c)] = codes[:, JB * (c - c0) : JB * (c - c0 + 1)]
-                z_s[(b, c)] = scales[:, JB * (c - c0) : JB * (c - c0 + 1)]
+        def weave(engine, b, c0, c1):
+            i = c0 // HALF
+            cols = slice(c0 - HALF * i, c1 - HALF * i)
+            dst = z[b][i][:, cols, :].rearrange("p (c i) t -> p c t i", i=4)
+            src = lanes[b][i][:, :, cols].rearrange("p t (c i) -> p c t i", i=4)
+            if engine == "scalar":
+                nc.scalar.copy(dst, src)
+            else:
+                nc.vector.tensor_copy(dst, src)
 
-        y = [psum.tile([P, N // P, JB], F32, name="y", tag="bank%d" % (4 + c)) for c in range(PAIRS // JB)]
+        def quant_z(b, c0, c1, tag=None):
+            i = c0 // HALF
+            codes = sb([P, c1 - c0], U32, "z_c%d_%d" % (b, c0), tag)
+            scales = sb([P, c1 - c0], U8, "z_s%d_%d" % (b, c0))
+            nc.vector.quantize_mx(out=codes[:].bitcast(FP8X4), scales=scales[:], in_=z[b][i][:, c0 - HALF * i : c1 - HALF * i, :].rearrange("p j t -> p (j t)"))
+            for c in range(c0 // JB, c1 // JB):
+                z_c[(b, c)] = codes[:, JB * c - c0 : JB * (c + 1) - c0]
+                z_s[(b, c)] = scales[:, JB * c - c0 : JB * (c + 1) - c0]
 
         def score(b, c):
             for nt in range(N // P):
@@ -330,35 +326,31 @@ def tile_list_duplicate_pair_score_kernel(tc, tab_words, tab_scales, offs, w1, p
 
         def finish(c):
             cols = slice(JB * c, JB * (c + 1))
-            o = sb([P, N // P, JB], F32, "o%d" % c)
+            o = sb([P, N // P, JB], F32, "o%d" % c, "raw0%d" % c if c < K_PASSES else "raw10")
             step = 2 if c == PAIRS // JB - 1 else N // P
             for n0 in range(0, N // P, step):
                 nc.scalar.activation(o[:, n0 : n0 + step, :], y[c][:, n0 : n0 + step, :], ACT.Sigmoid)
                 nc.sync.dma_start(out[P * n0 : P * (n0 + step), cols].rearrange("(nt p) j -> p nt j", p=P), o[:, n0 : n0 + step, :])
 
-        def weigh(c):
-            nc.vector.tensor_tensor(
-                z1[c].rearrange("p (c i) t -> p c t i", i=4),
-                sim[1][:, :, blocks[c]].rearrange("p t (c i) -> p c t i", i=4),
-                gain_sb[:].unsqueeze(1).unsqueeze(3).to_broadcast([P, JB // 4, PACK, 4]),
-                ALU.mult,
-            )
-
-        def weave(cols):
-            nc.vector.tensor_copy(z0[:, cols, :].rearrange("p (c i) t -> p c t i", i=4), lanes[:, :, cols].rearrange("p t (c i) -> p c t i", i=4))
-
-        def close(c):
-            quant_z(1, c, c + 1, z1[c])
-            score(1, c)
-            finish(c)
-
         for half, cols in enumerate(halves):
-            c0 = 2 * half
-            weave(cols)
-            weigh(c0)
-            quant_z(0, c0, c0 + 2, z0[:, cols, :])
-            score(0, c0)
-            close(c0)
-            score(0, c0 + 1)
-            weigh(c0 + 1)
-            close(c0 + 1)
+            for i, u in enumerate(last):
+                weigh("vector", u, cols, near_last[:, own(2 * half + i)])
+            if half == 0:
+                weave("vector", 0, 0, HALF)
+        weave("scalar", 0, HALF, PAIRS)
+        quant_z(0, 0, HALF)
+        for c in range(2):
+            score(0, c)
+        for half in range(2):
+            blocks = (2 * half, 2 * half + 1)
+            for c in blocks:
+                weave("vector", 1, JB * c, JB * (c + 1))
+            for c in blocks:
+                quant_z(1, JB * c, JB * (c + 1))
+                score(1, c)
+                finish(c)
+                if c == 0:
+                    quant_z(0, HALF, PAIRS, "lanes10")
+            if half == 0:
+                for c in range(2, 4):
+                    score(0, c)

@@ -25,9 +25,8 @@ TILES = H // P
 BANK = 512
 JB = 128
 HALF = PAIRS // 2
-SLOT = 6656
+CHUNK = 2 * P
 STEPS = TILES - 2
-ON_VECTOR = 7
 
 
 def tile_list_duplicate_pair_score_kernel(tc, tab_words, tab_scales, offs, w1, pos1, pos2, gain, w2_words, w2_scales, out):
@@ -63,28 +62,29 @@ def tile_list_duplicate_pair_score_kernel(tc, tab_words, tab_scales, offs, w1, p
         def load_tab(a):
             nc.sync.dma_start(tab_w[a][:], tab_words[a].rearrange("p t i -> p (t i)").bitcast(I32))
 
-        def load_w1(u, a):
-            if u >= 2 and a == 2:
-                raw[(u, a)] = placed([P, PACK, P], F32, "raw%d%d" % (u, a), SLOT * (u - 2) + 3584)
+        spot = {(1, 0): 3584, (1, 2): 9216, (3, 2): 19968}
+
+        def load_w1(c, a):
+            if (c, a) in spot:
+                raw[(c, a)] = placed([P, PACK, CHUNK], F32, "raw%d%d" % (c, a), spot[(c, a)])
             else:
-                raw[(u, a)] = sb([P, PACK, P], F32, "raw%d%d" % (u, a))
-            nc.sync.dma_start(raw[(u, a)][:], w1[K_PASS * a : K_PASS * (a + 1), P * u : P * (u + 1)].rearrange("(p j) c -> p j c", j=PACK))
+                raw[(c, a)] = sb([P, PACK, CHUNK], F32, "raw%d%d" % (c, a))
+            nc.sync.dma_start(raw[(c, a)][:], w1[K_PASS * a : K_PASS * (a + 1), CHUNK * c : CHUNK * (c + 1)].rearrange("(p j) c -> p j c", j=PACK))
 
         nc.sync.dma_start(offs_sb[:], offs)
         load_tab(0)
         for q in range(2, 4):
             nc.sync.dma_start(tab_s[32 * q : 32 * q + 4 * K_PASSES, :], tab_scales[:, 4 * q : 4 * q + 4, :].bitcast(I32))
-        for a in range(K_PASSES):
-            load_w1(0, a)
+        load_w1(0, 0)
         load_tab(1)
+        load_w1(0, 1)
         load_tab(2)
-        for a in range(K_PASSES):
-            load_w1(1, a)
+        load_w1(0, 2)
         nc.sync.dma_start(pos_sb[0][:], pos1)
         nc.sync.dma_start(pos_sb[1][:], pos2)
-        for u in range(2, TILES):
+        for c in range(1, H // CHUNK):
             for a in range(K_PASSES):
-                load_w1(u, a)
+                load_w1(c, a)
         with nc.allow_non_contiguous_dma(reason="one gain a partition"):
             nc.sync.dma_start(gain_sb[:], gain.rearrange("(u p) -> p u", p=P))
         for q in range(4):
@@ -94,16 +94,19 @@ def tile_list_duplicate_pair_score_kernel(tc, tab_words, tab_scales, offs, w1, p
         w_bf = {}
         w_c = {}
         w_s = {}
-        planes = {}
 
-        def round_w1(engine, u, a, tag=None):
-            w_bf[(u, a)] = sb([P, P, PACK], BF16, "w_bf%d%d" % (u, a), tag)
-            if engine == "gpsimd":
-                nc.gpsimd.tensor_scalar(w_bf[(u, a)][:], raw[(u, a)][:].rearrange("p j c -> p c j"), 1.0, 0.0, ALU.mult, ALU.add)
-            elif engine == "scalar":
-                nc.scalar.copy(w_bf[(u, a)][:].rearrange("p (c i) j -> p c j i", i=4), raw[(u, a)][:].rearrange("p j (c i) -> p c j i", i=4))
+        def round_w1(engine, u, a, tag=None, offset=None):
+            if offset is None:
+                w_bf[(u, a)] = sb([P, P, PACK], BF16, "w_bf%d%d" % (u, a), tag)
             else:
-                nc.vector.tensor_copy(w_bf[(u, a)][:].rearrange("p (c i) j -> p c j i", i=4), raw[(u, a)][:].rearrange("p j (c i) -> p c j i", i=4))
+                w_bf[(u, a)] = placed([P, P, PACK], BF16, "w_bf%d%d" % (u, a), offset)
+            src = raw[(u // 2, a)][:, :, P * (u % 2) : P * (u % 2 + 1)]
+            if engine == "gpsimd":
+                nc.gpsimd.tensor_scalar(w_bf[(u, a)][:], src.rearrange("p j c -> p c j"), 1.0, 0.0, ALU.mult, ALU.add)
+            elif engine == "scalar":
+                nc.scalar.copy(w_bf[(u, a)][:].rearrange("p (c i) j -> p c j i", i=4), src.rearrange("p j (c i) -> p c j i", i=4))
+            else:
+                nc.vector.tensor_copy(w_bf[(u, a)][:].rearrange("p (c i) j -> p c j i", i=4), src.rearrange("p j (c i) -> p c j i", i=4))
 
         acc = {}
 
@@ -118,25 +121,20 @@ def tile_list_duplicate_pair_score_kernel(tc, tab_words, tab_scales, offs, w1, p
                 rhs=v_w[a][:, cols].bitcast(FP8X4),
                 rhs_scale=v_s[4 * a : P, cols],
                 start=(a == 0),
-                stop=(a == (1 if u >= 2 else 2)),
+                stop=(a == K_PASSES - 1),
             )
 
-        def quant_w1(u, a):
-            w_c[(u, a)] = sb([P, P], U32, "w_c%d%d" % (u, a))
-            if (u, a) == (ON_VECTOR, 0):
-                w_s[(u, a)] = sb([P, P], U8, "w_s_early")[:]
-            else:
-                if u not in planes and u >= 2:
-                    planes[u] = placed([P, K_PASSES * P], U8, "w_s%d" % u, SLOT * (u - 2) + 4096)
-                elif u not in planes:
-                    planes[u] = sb([P, K_PASSES * P], U8, "w_s%d" % u)
-                w_s[(u, a)] = planes[u][:, P * a : P * (a + 1)]
-            nc.vector.quantize_mx(out=w_c[(u, a)][:].bitcast(FP8X4), scales=w_s[(u, a)], in_=w_bf[(u, a)][:].rearrange("p c j -> p (c j)"))
-
-        def quant_embed(u, a):
-            quant_w1(u, a)
-            for half in range(2):
-                embed(u, a, half)
+        def quant_embed(pieces, planes=None):
+            if planes is None:
+                planes = sb([P, P * len(pieces)], U8, "w_s%d%d" % pieces[0])
+            for i, (u, a) in enumerate(pieces):
+                w_c[(u, a)] = sb([P, P], U32, "w_c%d%d" % (u, a))
+                w_s[(u, a)] = planes[:, P * i : P * (i + 1)]
+                nc.vector.quantize_mx(out=w_c[(u, a)][:].bitcast(FP8X4), scales=w_s[(u, a)], in_=w_bf[(u, a)][:].rearrange("p c j -> p (c j)"))
+            for u in sorted(set(u for u, a in pieces)):
+                for half in range(2):
+                    for a in [a for v, a in pieces if v == u]:
+                        embed(u, a, half)
 
         def gather_tab(a, c0, c1):
             nc.vector.tensor_copy(v_w[a][:, c0:c1], tab_w[a][:].bitcast(U32).indirect(offs_sb[:, c0 // 16 : c1 // 16]))
@@ -145,10 +143,7 @@ def tile_list_duplicate_pair_score_kernel(tc, tab_words, tab_scales, offs, w1, p
 
         def drain(u, half, engine="scalar"):
             if half == 0:
-                if 1 <= u <= STEPS:
-                    h[u] = placed([P, S], F32, "h%d" % u, SLOT * (u - 1))
-                else:
-                    h[u] = sb([P, S], F32, "h%d" % u, "raw11" if u == 0 else None)
+                h[u] = placed([P, S], F32, "h1", 0) if u == 1 else sb([P, S], F32, "h%d" % u)
             dst = h[u][:, BANK * half : BANK * (half + 1)]
             if engine == "vector":
                 nc.vector.tensor_copy(dst, acc[(u, half)][:])
@@ -171,7 +166,7 @@ def tile_list_duplicate_pair_score_kernel(tc, tab_words, tab_scales, offs, w1, p
             nc.vector.tensor_tensor(dst, h[u][:].indirect(pos_sb[1][:, cols.start // 16 : cols.stop // 16]), first[u][:, cols], ALU.subtract)
 
         def apart(key):
-            dist[key] = sb([P, PAIRS], F32, "dist%s" % key)
+            dist[key] = placed([P, PAIRS], F32, "dist%d" % key, {2: 14336, 4: 24576}[key]) if key in (2, 4) else sb([P, PAIRS], F32, "dist%s" % key, "w_c%d2" % (key + 1) if key in (1, 3) else None)
             nc.scalar.activation(dist[key][:], diff[key][:, :], ACT.Abs)
 
         def similar(key):
@@ -191,9 +186,9 @@ def tile_list_duplicate_pair_score_kernel(tc, tab_words, tab_scales, offs, w1, p
             rows = slice(32 * (u % PACK), 32 * (u % PACK + 1))
             if u < PACK:
                 nc.sync.dma_start(early[rows, :, :], z_nat[u][:, :])
-            else:
-                for i in range(cols.start // HALF, cols.stop // HALF):
-                    nc.sync.dma_start(lanes[1][i][rows, :, :], z_nat[u][:, halves[i]])
+
+        def deal(u, i):
+            nc.sync.dma_start(lanes[1][i][32 * (u % PACK) : 32 * (u % PACK + 1), :, :], z_nat[u][:, halves[i]])
 
         def weighed_tiles(u0, u1, tag):
             both = sb([P, (u1 - u0) * PAIRS], BF16, "z_nat%d" % u0, tag)
@@ -202,25 +197,20 @@ def tile_list_duplicate_pair_score_kernel(tc, tab_words, tab_scales, offs, w1, p
 
         gather_tab(0, 0, S)
         nc.vector.tensor_copy(v_s[:], tab_s[:].bitcast(U8).indirect(offs_sb[:]))
-        for a in range(K_PASSES):
-            round_w1("scalar", 0, a)
-            quant_w1(0, a)
-        for half in range(2):
-            embed(0, 0, half)
+        for u in range(2):
+            round_w1("scalar", u, 0)
+        quant_embed([(0, 0), (1, 0)])
         gather_tab(1, 0, S)
-        for half in range(2):
-            embed(0, 1, half)
+        for u in range(2):
+            round_w1("scalar", u, 1)
+        quant_embed([(0, 1), (1, 1)])
         for half in range(2):
             gather_tab(2, BANK * half, BANK * (half + 1))
-            embed(0, 2, half)
-        for a in range(K_PASSES):
-            round_w1("scalar", 1, a)
-        for a in range(2):
-            quant_embed(1, a)
+        for u in range(2):
+            round_w1("scalar", u, 2)
+            quant_embed([(u, 2)])
         drain(0, 0)
         drain(0, 1, "vector")
-        quant_embed(1, 2)
-        round_w1("scalar", 2, 0)
 
         steps = [(f, u) for u in range(STEPS) for f in (apart, similar)]
 
@@ -230,43 +220,60 @@ def tile_list_duplicate_pair_score_kernel(tc, tab_words, tab_scales, offs, w1, p
                 f(u)
                 steps.remove((f, u))
 
-        for u in range(STEPS):
-            round_w1("gpsimd", u + 2, 1, "turn%d" % ((u - 1) % 2) if u else "w_bf12")
-            round_w1("scalar", u + 2, 2)
-            pick(u, "turn%d" % (u % 2) if u else "raw12")
-            passes = (0, 2, 1) if u + 2 < ON_VECTOR else (2, 1)
-            for a in passes[:-1]:
-                quant_w1(u + 2, a)
-            if u + 3 == ON_VECTOR:
-                round_w1("vector", u + 3, 0, "w_bf%d0" % (u + 2))
-            quant_w1(u + 2, passes[-1])
-            for half in range(2):
-                for a in passes:
-                    embed(u + 2, a, half)
-            if u + 3 == ON_VECTOR:
-                quant_embed(u + 3, 0)
-            diff[u] = placed([P, PAIRS], F32, "diff%d" % u, SLOT * u + 4608)
-            pick_less(u, diff[u][:], whole)
-            catch_up(u - 1)
-            drain(u + 1, 0)
-            if u + 3 < ON_VECTOR:
-                round_w1("scalar", u + 3, 0)
+        held = {0: 4096, 2: 9216, 4: 14336}
+        last = [TILES - 2, TILES - 1]
+        for u in range(0, STEPS, 2):
+            even, odd = u + 2, u + 3
+            round_w1("gpsimd", odd, 0, "turn%d" % (u - 2) if u else "w_bf12")
+            if u == 0:
+                round_w1("scalar", even, 0, "turn_w")
             else:
                 catch_up(u - 1)
+            pick(u, "turn%d" % u)
+            quant_embed([(even, 0), (odd, 0)], placed([P, 2 * P], U8, "w_s%d0" % even, held[u] + 256))
+            diff[u] = placed([P, PAIRS], F32, "diff%d" % u, held[u] + 512)
+            pick_less(u, diff[u][:], whole)
+            drain(u + 1, 0)
+            round_w1("scalar", even, 1, None, held[u] - 768 if u else None)
             drain(u + 1, 1)
+            quant_embed([(even, 1)])
+            round_w1("scalar", odd, 1, "turn_w")
 
-        last = [TILES - 2, TILES - 1]
-        weighed_tiles(0, 3, "turn%d" % ((STEPS - 1) % 2))
-        for u in range(3):
+            round_w1("gpsimd", odd, 2, "turn%d" % u)
+            round_w1("scalar", even, 2, "w_c%d2" % (even - 1))
+            pick(u + 1, "turn1")
+            quant_embed([(even, 2)])
+            rest = [(odd, 1), (odd, 2)]
+            if odd == TILES - 1:
+                quant_embed(rest, placed([P, 2 * P], U8, "w_s_last", 19968))
+                diff[u + 1] = placed([P, PAIRS], F32, "diff%d" % (u + 1), 20480)
+            elif u == 0:
+                diff[u + 1] = placed([P, PAIRS], F32, "diff1", held[2])
+            else:
+                diff[u + 1] = sb([P, PAIRS], F32, "diff%d" % (u + 1), "raw%d2" % (odd // 2))
+            pick_less(u + 1, diff[u + 1][:], whole)
+            if odd < TILES - 1:
+                quant_embed(rest, sb([P, 2 * P], U8, "w_s%d1" % odd, "w_c%d2" % (even - 1)))
+                round_w1("vector", even + 2, 0, "turn_w")
+            else:
+                weighed_tiles(0, 1, "turn_w")
+                weigh("vector", 0, whole, near[0][:])
+            for k in range(2 if odd < TILES - 1 else 3):
+                catch_up(u)
+            for half in range(2):
+                drain(even, half)
+
+        weighed_tiles(1, PACK, "turn1")
+        for u in range(1, PACK):
             weigh("gpsimd", u, whole, near[u][:])
         for half in range(2):
             drain(TILES - 1, half)
         for u in last:
             pick(u, None)
-        for k in range(len(steps)):
-            catch_up(STEPS)
-        both = placed([P, 2 * PAIRS], F32, "diff_last", SLOT * 4 + 1024)
-        z_nat[3] = placed([P, PAIRS], BF16, "z_nat3", SLOT * 4 + 5120)
+        apart(STEPS - 1)
+        similar(STEPS - 2)
+        similar(STEPS - 1)
+        both = placed([P, 2 * PAIRS], F32, "diff_last", 24576)
         weighed_tiles(4, 6, None)
         apart_last = sb([P, 2 * PAIRS], F32, "dist_last")
         near_last = sb([P, 2 * PAIRS], F32, "near_last")
@@ -281,17 +288,17 @@ def tile_list_duplicate_pair_score_kernel(tc, tab_words, tab_scales, offs, w1, p
 
         for k, (u, cols) in enumerate(pieces):
             pick_less(u, both[:, own(k)], cols)
-            if k > 0:
-                weigh("vector", 2 + k, whole, near[2 + k][:])
             nc.scalar.activation(apart_last[:, own(k)], both[:, own(k)], ACT.Abs)
             if k > 0:
                 close(k - 1)
         close(len(pieces) - 1)
+        for u in (4, 5):
+            weigh("vector", u, whole, near[u][:])
 
         z = [[sb([P, HALF, PACK], BF16, "z00", "h7"), sb([P, HALF, PACK], BF16, "z01", "dist_last")], [sb([P, HALF, PACK], BF16, "z1%d" % i) for i in range(2)]]
         z_c = {}
         z_s = {}
-        y = [psum.tile([P, N // P, JB], F32, name="y", tag="bank%d" % c) for c in range(PAIRS // JB)]
+        y = [[psum.tile([P, 2, HALF], F32, name="y", tag="bank%d" % (2 * half + g)) for g in range(2)] for half in range(2)]
 
         def weave(engine, b, c0, c1):
             i = c0 // HALF
@@ -315,26 +322,27 @@ def tile_list_duplicate_pair_score_kernel(tc, tab_words, tab_scales, offs, w1, p
         def score(b, c):
             for nt in range(N // P):
                 nc.tensor.matmul_mx(
-                    out=y[c][:, nt, :],
+                    out=y[c // 2][nt // 2][:, nt % 2, JB * (c % 2) : JB * (c % 2 + 1)],
                     lhsT=w2_w[:, b, :].bitcast(U8)[:, 2 * P * nt : 2 * P * (nt + 1)].bitcast(FP4X4),
                     lhsT_scale=w2_s[:, b, :].bitcast(U8)[:, P * nt : P * (nt + 1)],
                     rhs=z_c[(b, c)].bitcast(FP8X4),
                     rhs_scale=z_s[(b, c)],
-                    start=(b == 0 and nt == 0),
-                    stop=(b == 1 and nt == N // P - 1),
+                    start=(b == 0 and c % 2 == 0 and nt % 2 == 0),
+                    stop=(b == 1 and c % 2 == 1 and nt % 2 == 1),
                 )
 
-        def finish(c):
-            cols = slice(JB * c, JB * (c + 1))
-            o = sb([P, N // P, JB], F32, "o%d" % c, "raw0%d" % c if c < K_PASSES else "raw10")
-            step = 2 if c == PAIRS // JB - 1 else N // P
-            for n0 in range(0, N // P, step):
-                nc.scalar.activation(o[:, n0 : n0 + step, :], y[c][:, n0 : n0 + step, :], ACT.Sigmoid)
-                nc.sync.dma_start(out[P * n0 : P * (n0 + step), cols].rearrange("(nt p) j -> p nt j", p=P), o[:, n0 : n0 + step, :])
+        def finish(half):
+            for g in range(2):
+                o = sb([P, 2, HALF], F32, "o%d%d" % (half, g))
+                nc.scalar.activation(o[:], y[half][g][:], ACT.Sigmoid)
+                nc.sync.dma_start(out[2 * P * g : 2 * P * (g + 1), halves[half]].rearrange("(nt p) j -> p nt j", p=P), o[:])
 
         for half, cols in enumerate(halves):
+            for u in (4, 5):
+                deal(u, half)
             for i, u in enumerate(last):
                 weigh("vector", u, cols, near_last[:, own(2 * half + i)])
+                deal(u, half)
             if half == 0:
                 weave("vector", 0, 0, HALF)
         weave("scalar", 0, HALF, PAIRS)
@@ -348,9 +356,8 @@ def tile_list_duplicate_pair_score_kernel(tc, tab_words, tab_scales, offs, w1, p
             for c in blocks:
                 quant_z(1, JB * c, JB * (c + 1))
                 score(1, c)
-                finish(c)
-                if c == 0:
-                    quant_z(0, HALF, PAIRS, "lanes10")
+            finish(half)
             if half == 0:
+                quant_z(0, HALF, PAIRS, "lanes10")
                 for c in range(2, 4):
                     score(0, c)

@@ -173,8 +173,7 @@ def tile_list_duplicate_pair_score_kernel(tc, tab_words, tab_scales, offs, w1, p
             near[key] = sb([P, PAIRS], F32, "near%s" % key)
             nc.scalar.activation(near[key][:], dist[key][:], ACT.Exp, scale=-1.0)
 
-        early = sb([P, PACK, PAIRS], BF16, "lanes0")
-        lanes = [[early[:, :, cols] for cols in halves], [sb([P, PACK, HALF], BF16, "lanes1%d" % i)[:] for i in range(2)]]
+        lanes = [[sb([P, PACK, HALF], BF16, "lanes%d%d" % (b, i))[:] for i in range(2)] for b in range(R_PASSES)]
 
         def weigh(engine, u, cols, src):
             if engine == "scalar":
@@ -183,12 +182,12 @@ def tile_list_duplicate_pair_score_kernel(tc, tab_words, tab_scales, offs, w1, p
                 nc.gpsimd.tensor_scalar(z_nat[u][:, cols], src, gain_sb[:, u : u + 1], 0.0, ALU.mult, ALU.add)
             else:
                 nc.vector.tensor_scalar(z_nat[u][:, cols], src, gain_sb[:, u : u + 1], None, ALU.mult)
-            rows = slice(32 * (u % PACK), 32 * (u % PACK + 1))
             if u < PACK:
-                nc.sync.dma_start(early[rows, :, :], z_nat[u][:, :])
+                for i in range(2):
+                    deal(u, i)
 
         def deal(u, i):
-            nc.sync.dma_start(lanes[1][i][32 * (u % PACK) : 32 * (u % PACK + 1), :, :], z_nat[u][:, halves[i]])
+            nc.sync.dma_start(lanes[u // PACK][i][32 * (u % PACK) : 32 * (u % PACK + 1), :, :], z_nat[u][:, halves[i]])
 
         def weighed_tiles(u0, u1, tag):
             both = sb([P, (u1 - u0) * PAIRS], BF16, "z_nat%d" % u0, tag)
@@ -273,29 +272,28 @@ def tile_list_duplicate_pair_score_kernel(tc, tab_words, tab_scales, offs, w1, p
         apart(STEPS - 1)
         similar(STEPS - 2)
         similar(STEPS - 1)
-        both = placed([P, 2 * PAIRS], F32, "diff_last", 24576)
         weighed_tiles(4, 6, None)
+        weigh("scalar", 4, whole, near[4][:])
+        both = placed([P, 2 * PAIRS], F32, "diff_last", 24576)
         apart_last = sb([P, 2 * PAIRS], F32, "dist_last")
-        near_last = sb([P, 2 * PAIRS], F32, "near_last")
-        weighed_tiles(6, TILES, None)
+        near_last = [sb([P, PAIRS], F32, "near_last%d" % i) for i in range(2)]
         pieces = [(u, cols) for cols in halves for u in last]
 
         def own(k):
             return slice(HALF * k, HALF * (k + 1))
 
         def close(k):
-            nc.scalar.activation(near_last[:, own(k)], apart_last[:, own(k)], ACT.Exp, scale=-1.0)
+            nc.scalar.activation(near_last[k // 2][:, halves[k % 2]], apart_last[:, own(k)], ACT.Exp, scale=-1.0)
 
         for k, (u, cols) in enumerate(pieces):
             pick_less(u, both[:, own(k)], cols)
             nc.scalar.activation(apart_last[:, own(k)], both[:, own(k)], ACT.Abs)
-            if k > 0:
+            if k % 2:
                 close(k - 1)
-        close(len(pieces) - 1)
-        for u in (4, 5):
-            weigh("vector", u, whole, near[u][:])
+                close(k)
+        weigh("vector", 5, whole, near[5][:])
 
-        z = [[sb([P, HALF, PACK], BF16, "z00", "h7"), sb([P, HALF, PACK], BF16, "z01", "dist_last")], [sb([P, HALF, PACK], BF16, "z1%d" % i) for i in range(2)]]
+        z = [[sb([P, HALF, PACK], BF16, "z00", "h7"), sb([P, HALF, PACK], BF16, "z01", "h6")], [sb([P, HALF, PACK], BF16, "z1%d" % i) for i in range(2)]]
         z_c = {}
         z_s = {}
         y = [[psum.tile([P, 2, HALF], F32, name="y", tag="bank%d" % (2 * half + g)) for g in range(2)] for half in range(2)]
@@ -340,13 +338,14 @@ def tile_list_duplicate_pair_score_kernel(tc, tab_words, tab_scales, offs, w1, p
         for half, cols in enumerate(halves):
             for u in (4, 5):
                 deal(u, half)
+            pair = sb([P, PAIRS], BF16, "z_last%d" % half, "turn1" if half else None)
             for i, u in enumerate(last):
-                weigh("vector", u, cols, near_last[:, own(2 * half + i)])
-                deal(u, half)
+                nc.vector.tensor_scalar(pair[:, halves[i]], near_last[half][:, halves[i]], gain_sb[:, u : u + 1], None, ALU.mult)
+                nc.sync.dma_start(lanes[1][half][32 * (u % PACK) : 32 * (u % PACK + 1), :, :], pair[:, halves[i]])
             if half == 0:
                 weave("vector", 0, 0, HALF)
-        weave("scalar", 0, HALF, PAIRS)
         quant_z(0, 0, HALF)
+        weave("vector", 0, HALF, PAIRS)
         for c in range(2):
             score(0, c)
         for half in range(2):

@@ -296,7 +296,7 @@ def tile_list_duplicate_pair_score_kernel(tc, tab_words, tab_scales, offs, w1, p
         z = [[sb([P, HALF, PACK], BF16, "z00", "h7"), sb([P, HALF, PACK], BF16, "z01", "h6")], [sb([P, HALF, PACK], BF16, "z1%d" % i) for i in range(2)]]
         z_c = {}
         z_s = {}
-        y = [[psum.tile([P, 2, HALF], F32, name="y", tag="bank%d" % (2 * half + g)) for g in range(2)] for half in range(2)]
+        y = [[psum.tile([P, HALF], F32, name="y", tag="bank%d" % (4 * half + nt)) for nt in range(N // P)] for half in range(2)]
 
         def weave(engine, b, c0, c1):
             i = c0 // HALF
@@ -320,20 +320,20 @@ def tile_list_duplicate_pair_score_kernel(tc, tab_words, tab_scales, offs, w1, p
         def score(b, c):
             for nt in range(N // P):
                 nc.tensor.matmul_mx(
-                    out=y[c // 2][nt // 2][:, nt % 2, JB * (c % 2) : JB * (c % 2 + 1)],
+                    out=y[c // 2][nt][:, JB * (c % 2) : JB * (c % 2 + 1)],
                     lhsT=w2_w[:, b, :].bitcast(U8)[:, 2 * P * nt : 2 * P * (nt + 1)].bitcast(FP4X4),
                     lhsT_scale=w2_s[:, b, :].bitcast(U8)[:, P * nt : P * (nt + 1)],
                     rhs=z_c[(b, c)].bitcast(FP8X4),
                     rhs_scale=z_s[(b, c)],
-                    start=(b == 0 and c % 2 == 0 and nt % 2 == 0),
-                    stop=(b == 1 and c % 2 == 1 and nt % 2 == 1),
+                    start=(b == 0 and c % 2 == 0),
+                    stop=(b == 1 and c % 2 == 1),
                 )
 
         def finish(half):
-            for g in range(2):
-                o = sb([P, 2, HALF], F32, "o%d%d" % (half, g))
-                nc.scalar.activation(o[:], y[half][g][:], ACT.Sigmoid)
-                nc.sync.dma_start(out[2 * P * g : 2 * P * (g + 1), halves[half]].rearrange("(nt p) j -> p nt j", p=P), o[:])
+            for nt in range(N // P):
+                o = sb([P, HALF], F32, "o%d%d" % (half, nt))
+                nc.scalar.activation(o[:], y[half][nt][:], ACT.Sigmoid)
+                nc.sync.dma_start(out[P * nt : P * (nt + 1), halves[half]], o[:])
 
         for half, cols in enumerate(halves):
             for u in (4, 5):

@@ -62,7 +62,7 @@ def tile_list_duplicate_pair_score_kernel(tc, tab_words, tab_scales, offs, w1, p
         def load_tab(a):
             nc.sync.dma_start(tab_w[a][:], tab_words[a].rearrange("p t i -> p (t i)").bitcast(I32))
 
-        spot = {(1, 0): 3584, (1, 2): 9216, (3, 2): 19968}
+        spot = {(1, 0): 3584, (1, 2): 9216, (3, 2): 19968, (3, 1): 24064}
 
         def load_w1(c, a):
             if (c, a) in spot:
@@ -166,7 +166,7 @@ def tile_list_duplicate_pair_score_kernel(tc, tab_words, tab_scales, offs, w1, p
             nc.vector.tensor_tensor(dst, h[u][:].indirect(pos_sb[1][:, cols.start // 16 : cols.stop // 16]), first[u][:, cols], ALU.subtract)
 
         def apart(key):
-            dist[key] = placed([P, PAIRS], F32, "dist%d" % key, {2: 14336, 4: 24576}[key]) if key in (2, 4) else sb([P, PAIRS], F32, "dist%s" % key, "w_c%d2" % (key + 1) if key in (1, 3) else None)
+            dist[key] = placed([P, PAIRS], F32, "dist%d" % key, 14336) if key == 2 else sb([P, PAIRS], F32, "dist%s" % key, "w_c%d2" % (key + 1) if key in (1, 3) else None)
             nc.scalar.activation(dist[key][:], diff[key][:, :], ACT.Abs)
 
         def similar(key):
@@ -232,20 +232,30 @@ def tile_list_duplicate_pair_score_kernel(tc, tab_words, tab_scales, offs, w1, p
             quant_embed([(even, 0), (odd, 0)], placed([P, 2 * P], U8, "w_s%d0" % even, held[u] + 256))
             diff[u] = placed([P, PAIRS], F32, "diff%d" % u, held[u] + 512)
             pick_less(u, diff[u][:], whole)
-            drain(u + 1, 0)
-            round_w1("scalar", even, 1, None, held[u] - 768 if u else None)
-            drain(u + 1, 1)
-            quant_embed([(even, 1)])
+            ending = odd == TILES - 1
+            if ending:
+                round_w1("scalar", even, 1, None, held[u] - 768)
+                round_w1("scalar", even, 2, "w_s%d2" % u)
+                drain(u + 1, 0)
+                drain(u + 1, 1)
+                quant_embed([(even, 1), (even, 2)])
+            else:
+                drain(u + 1, 0)
+                round_w1("scalar", even, 1, None, held[u] - 768 if u else None)
+                drain(u + 1, 1)
+                quant_embed([(even, 1)])
             round_w1("scalar", odd, 1, "turn_w")
 
             round_w1("gpsimd", odd, 2, "turn%d" % u)
-            round_w1("scalar", even, 2, "w_c%d2" % (even - 1))
+            if not ending:
+                round_w1("scalar", even, 2, "w_c%d2" % (even - 1))
             pick(u + 1, "turn1")
-            quant_embed([(even, 2)])
+            if not ending:
+                quant_embed([(even, 2)])
             rest = [(odd, 1), (odd, 2)]
             if odd == TILES - 1:
-                quant_embed(rest, placed([P, 2 * P], U8, "w_s_last", 19968))
-                diff[u + 1] = placed([P, PAIRS], F32, "diff%d" % (u + 1), 20480)
+                quant_embed(rest, placed([P, 2 * P], U8, "w_s_last", 23936))
+                diff[u + 1] = placed([P, PAIRS], F32, "diff%d" % (u + 1), 24192)
             elif u == 0:
                 diff[u + 1] = placed([P, PAIRS], F32, "diff1", held[2])
             else:
@@ -257,10 +267,11 @@ def tile_list_duplicate_pair_score_kernel(tc, tab_words, tab_scales, offs, w1, p
             else:
                 weighed_tiles(0, 1, "turn_w")
                 weigh("vector", 0, whole, near[0][:])
-            for k in range(2 if odd < TILES - 1 else 3):
+            for k in range(1 if ending else 2):
                 catch_up(u)
             for half in range(2):
                 drain(even, half)
+        catch_up(STEPS)
 
         weighed_tiles(1, PACK, "turn1")
         for u in range(1, PACK):
@@ -269,13 +280,14 @@ def tile_list_duplicate_pair_score_kernel(tc, tab_words, tab_scales, offs, w1, p
             drain(TILES - 1, half)
         for u in last:
             pick(u, None)
+        apart(STEPS - 2)
         apart(STEPS - 1)
         similar(STEPS - 2)
         similar(STEPS - 1)
         weighed_tiles(4, 6, None)
         weigh("scalar", 4, whole, near[4][:])
-        both = placed([P, 2 * PAIRS], F32, "diff_last", 24576)
-        apart_last = sb([P, 2 * PAIRS], F32, "dist_last")
+        both = placed([P, 2 * PAIRS], F32, "diff_last", 14848)
+        apart_last = [sb([P, PAIRS], F32, "dist_last%d" % i) for i in range(2)]
         near_last = [sb([P, PAIRS], F32, "near_last%d" % i) for i in range(2)]
         pieces = [(u, cols) for cols in halves for u in last]
 
@@ -283,17 +295,17 @@ def tile_list_duplicate_pair_score_kernel(tc, tab_words, tab_scales, offs, w1, p
             return slice(HALF * k, HALF * (k + 1))
 
         def close(k):
-            nc.scalar.activation(near_last[k // 2][:, halves[k % 2]], apart_last[:, own(k)], ACT.Exp, scale=-1.0)
+            nc.scalar.activation(near_last[k // 2][:, halves[k % 2]], apart_last[k // 2][:, halves[k % 2]], ACT.Exp, scale=-1.0)
 
         for k, (u, cols) in enumerate(pieces):
             pick_less(u, both[:, own(k)], cols)
-            nc.scalar.activation(apart_last[:, own(k)], both[:, own(k)], ACT.Abs)
+            nc.scalar.activation(apart_last[k // 2][:, halves[k % 2]], both[:, own(k)], ACT.Abs)
             if k % 2:
                 close(k - 1)
                 close(k)
         weigh("vector", 5, whole, near[5][:])
 
-        z = [[sb([P, HALF, PACK], BF16, "z00", "h7"), sb([P, HALF, PACK], BF16, "z01", "h6")], [sb([P, HALF, PACK], BF16, "z1%d" % i) for i in range(2)]]
+        z = [[sb([P, HALF, PACK], BF16, "z00", "dist_last0"), sb([P, HALF, PACK], BF16, "z01", "dist_last1")], [sb([P, HALF, PACK], BF16, "z1%d" % i) for i in range(2)]]
         z_c = {}
         z_s = {}
         y = [[psum.tile([P, HALF], F32, name="y", tag="bank%d" % (4 * half + nt)) for nt in range(N // P)] for half in range(2)]

from contextlib import ExitStack

import concourse.mybir as mybir

K, T, S, PAIRS, H, N = 1536, 2048, 1024, 512, 1024, 512
FLOPS = 2 * K * H * S + 2 * H * N * PAIRS

F32 = mybir.dt.float32
BF16 = mybir.dt.bfloat16
I32 = mybir.dt.int32
U32 = mybir.dt.uint32
U16 = mybir.dt.uint16
U8 = mybir.dt.uint8
FP8X4 = mybir.dt.float8_e4m3fn_x4
FP4X4 = mybir.dt.float4_e2m1fn_x4
ACT = mybir.ActivationFunctionType
ALU = mybir.AluOpType

P = 128
PACK = 4
K_PASS = P * PACK
K_PASSES = K // K_PASS
R_PASSES = H // K_PASS
TILES = H // P
BANK = 512
JB = 128
HALF = PAIRS // 2
CHUNK = 2 * P
STEPS = TILES - 2


def tile_list_duplicate_pair_score_kernel(tc, tab_words, tab_scales, offs, w1, pos1, pos2, gain, w2_words, w2_scales, out):
    nc = tc.nc
    with ExitStack() as ctx:
        keep = ctx.enter_context(tc.tile_pool(name="keep", bufs=1))
        shared = ctx.enter_context(tc.tile_pool(name="shared", bufs=1))
        psum = ctx.enter_context(tc.psum_pool(name="psum", bufs=1))

        def sb(shape, dtype, name, tag=None):
            return keep.tile(shape, dtype, name=name, tag=tag or name, align_bytes=64)

        def placed(shape, dtype, name, offset):
            return shared.tile(shape, dtype, name=name, tag=name, align_bytes=64, offset=offset)

        offs_sb = keep.tile([P, S // 16], U16, name="offs_sb")
        pos_sb = [keep.tile([P, PAIRS // 16], U16, name="pos_sb%d" % i) for i in range(2)]
        tab_w = [sb([P, T], I32, "tab_w%d" % a) for a in range(K_PASSES)]
        tab_s = sb([P, T // 4], I32, "tab_s")
        v_w = [sb([P, S], U32, "v_w%d" % a) for a in range(K_PASSES)]
        v_s = sb([P, S], U8, "v_s")
        gain_sb = sb([P, TILES], F32, "gain_sb")
        w2_w = sb([P, R_PASSES, 2 * N // 4], I32, "w2_w")
        w2_s = sb([P, R_PASSES, N // 4], I32, "w2_s")

        nc.vector.memset(tab_s[:], 0)
        for q in range(2):
            nc.scalar.dma_start(tab_s[32 * q : 32 * q + 4 * K_PASSES, :], tab_scales[:, 4 * q : 4 * q + 4, :].bitcast(I32))
        nc.gpsimd.memset(w2_s[:], 0)

        raw = {}

        def load_tab(a):
            nc.sync.dma_start(tab_w[a][:], tab_words[a].rearrange("p t i -> p (t i)").bitcast(I32))

        spot = {(1, 0): 3584, (1, 2): 9216, (3, 2): 19968, (3, 1): 24064}

        def load_w1(c, a):
            if (c, a) in spot:
                raw[(c, a)] = placed([P, PACK, CHUNK], F32, "raw%d%d" % (c, a), spot[(c, a)])
            else:
                raw[(c, a)] = sb([P, PACK, CHUNK], F32, "raw%d%d" % (c, a))
            nc.sync.dma_start(raw[(c, a)][:], w1[K_PASS * a : K_PASS * (a + 1), CHUNK * c : CHUNK * (c + 1)].rearrange("(p j) c -> p j c", j=PACK))

        nc.sync.dma_start(offs_sb[:], offs)
        load_tab(0)
        for q in range(2, 4):
            nc.sync.dma_start(tab_s[32 * q : 32 * q + 4 * K_PASSES, :], tab_scales[:, 4 * q : 4 * q + 4, :].bitcast(I32))
        load_w1(0, 0)
        load_tab(1)
        load_w1(0, 1)
        load_tab(2)
        load_w1(0, 2)
        nc.sync.dma_start(pos_sb[0][:], pos1)
        nc.sync.dma_start(pos_sb[1][:], pos2)
        for c in range(1, H // CHUNK):
            for a in range(K_PASSES):
                load_w1(c, a)
        with nc.allow_non_contiguous_dma(reason="one gain a partition"):
            nc.sync.dma_start(gain_sb[:], gain.rearrange("(u p) -> p u", p=P))
        for q in range(4):
            nc.sync.dma_start(w2_s[32 * q : 32 * q + 4, :, :], w2_scales[:, 4 * q : 4 * q + 4, :].bitcast(I32).rearrange("b r n -> r b n"))
        nc.sync.dma_start(w2_w[:], w2_words.bitcast(I32).rearrange("b p n -> p b n"))

        w_bf = {}
        w_c = {}
        w_s = {}

        def round_w1(engine, u, a, tag=None, offset=None):
            if offset is None:
                w_bf[(u, a)] = sb([P, P, PACK], BF16, "w_bf%d%d" % (u, a), tag)
            else:
                w_bf[(u, a)] = placed([P, P, PACK], BF16, "w_bf%d%d" % (u, a), offset)
            src = raw[(u // 2, a)][:, :, P * (u % 2) : P * (u % 2 + 1)]
            if engine == "gpsimd":
                nc.gpsimd.tensor_scalar(w_bf[(u, a)][:], src.rearrange("p j c -> p c j"), 1.0, 0.0, ALU.mult, ALU.add)
            elif engine == "scalar":
                nc.scalar.copy(w_bf[(u, a)][:].rearrange("p (c i) j -> p c j i", i=4), src.rearrange("p j (c i) -> p c j i", i=4))
            else:
                nc.vector.tensor_copy(w_bf[(u, a)][:].rearrange("p (c i) j -> p c j i", i=4), src.rearrange("p j (c i) -> p c j i", i=4))

        acc = {}

        def embed(u, a, half):
            if a == 0:
                acc[(u, half)] = psum.tile([P, BANK], F32, name="acc", tag="bank%d" % ((2 * u + half) % 8))
            cols = slice(BANK * half, BANK * (half + 1))
            nc.tensor.matmul_mx(
                out=acc[(u, half)][:],
                lhsT=w_c[(u, a)][:].bitcast(FP8X4),
                lhsT_scale=w_s[(u, a)],
                rhs=v_w[a][:, cols].bitcast(FP8X4),
                rhs_scale=v_s[4 * a : P, cols],
                start=(a == 0),
                stop=(a == K_PASSES - 1),
            )

        def quant_embed(pieces, planes=None):
            if planes is None:
                planes = sb([P, P * len(pieces)], U8, "w_s%d%d" % pieces[0])
            for i, (u, a) in enumerate(pieces):
                w_c[(u, a)] = sb([P, P], U32, "w_c%d%d" % (u, a))
                w_s[(u, a)] = planes[:, P * i : P * (i + 1)]
                nc.vector.quantize_mx(out=w_c[(u, a)][:].bitcast(FP8X4), scales=w_s[(u, a)], in_=w_bf[(u, a)][:].rearrange("p c j -> p (c j)"))
            for u in sorted(set(u for u, a in pieces)):
                for half in range(2):
                    for a in [a for v, a in pieces if v == u]:
                        embed(u, a, half)

        def gather_tab(a, c0, c1):
            nc.vector.tensor_copy(v_w[a][:, c0:c1], tab_w[a][:].bitcast(U32).indirect(offs_sb[:, c0 // 16 : c1 // 16]))

        h = {}

        def drain(u, half, engine="scalar"):
            if half == 0:
                h[u] = placed([P, S], F32, "h1", 0) if u == 1 else sb([P, S], F32, "h%d" % u)
            dst = h[u][:, BANK * half : BANK * (half + 1)]
            if engine == "vector":
                nc.vector.tensor_copy(dst, acc[(u, half)][:])
            else:
                nc.scalar.copy(dst, acc[(u, half)][:])

        halves = [slice(0, HALF), slice(HALF, PAIRS)]
        whole = slice(0, PAIRS)
        first = {}
        diff = {}
        dist = {}
        near = {}
        z_nat = {}

        def pick(u, tag):
            first[u] = sb([P, PAIRS], F32, "first%d" % u, tag)
            nc.vector.tensor_copy(first[u][:], h[u][:].indirect(pos_sb[0][:]))

        def pick_less(u, dst, cols):
            nc.vector.tensor_tensor(dst, h[u][:].indirect(pos_sb[1][:, cols.start // 16 : cols.stop // 16]), first[u][:, cols], ALU.subtract)

        def apart(key):
            dist[key] = placed([P, PAIRS], F32, "dist%d" % key, 14336) if key == 2 else sb([P, PAIRS], F32, "dist%s" % key, "w_c%d2" % (key + 1) if key in (1, 3) else None)
            nc.scalar.activation(dist[key][:], diff[key][:, :], ACT.Abs)

        def similar(key):
            near[key] = sb([P, PAIRS], F32, "near%s" % key)
            nc.scalar.activation(near[key][:], dist[key][:], ACT.Exp, scale=-1.0)

        lanes = [[sb([P, PACK, HALF], BF16, "lanes%d%d" % (b, i))[:] for i in range(2)] for b in range(R_PASSES)]

        def weigh(engine, u, cols, src):
            if engine == "scalar":
                nc.scalar.activation(z_nat[u][:, cols], src, ACT.Copy, scale=gain_sb[:, u : u + 1])
            elif engine == "gpsimd":
                nc.gpsimd.tensor_scalar(z_nat[u][:, cols], src, gain_sb[:, u : u + 1], 0.0, ALU.mult, ALU.add)
            else:
                nc.vector.tensor_scalar(z_nat[u][:, cols], src, gain_sb[:, u : u + 1], None, ALU.mult)
            if u < PACK:
                for i in range(2):
                    deal(u, i)

        def deal(u, i):
            nc.sync.dma_start(lanes[u // PACK][i][32 * (u % PACK) : 32 * (u % PACK + 1), :, :], z_nat[u][:, halves[i]])

        def weighed_tiles(u0, u1, tag):
            both = sb([P, (u1 - u0) * PAIRS], BF16, "z_nat%d" % u0, tag)
            for u in range(u0, u1):
                z_nat[u] = both[:, PAIRS * (u - u0) : PAIRS * (u - u0 + 1)]

        gather_tab(0, 0, S)
        nc.vector.tensor_copy(v_s[:], tab_s[:].bitcast(U8).indirect(offs_sb[:]))
        for u in range(2):
            round_w1("scalar", u, 0)
        quant_embed([(0, 0), (1, 0)])
        gather_tab(1, 0, S)
        for u in range(2):
            round_w1("scalar", u, 1)
        quant_embed([(0, 1), (1, 1)])
        for half in range(2):
            gather_tab(2, BANK * half, BANK * (half + 1))
        for u in range(2):
            round_w1("scalar", u, 2)
            quant_embed([(u, 2)])
        drain(0, 0)
        drain(0, 1, "vector")

        steps = [(f, u) for u in range(STEPS) for f in (apart, similar)]

        def catch_up(upto):
            f, u = steps[0]
            if u <= upto:
                f(u)
                steps.remove((f, u))

        held = {0: 4096, 2: 9216, 4: 14336}
        last = [TILES - 2, TILES - 1]
        for u in range(0, STEPS, 2):
            even, odd = u + 2, u + 3
            round_w1("gpsimd", odd, 0, "turn%d" % (u - 2) if u else "w_bf12")
            if u == 0:
                round_w1("scalar", even, 0, "turn_w")
            else:
                catch_up(u - 1)
            pick(u, "turn%d" % u)
            quant_embed([(even, 0), (odd, 0)], placed([P, 2 * P], U8, "w_s%d0" % even, held[u] + 256))
            diff[u] = placed([P, PAIRS], F32, "diff%d" % u, held[u] + 512)
            pick_less(u, diff[u][:], whole)
            ending = odd == TILES - 1
            if ending:
                round_w1("scalar", even, 1, None, held[u] - 768)
                round_w1("scalar", even, 2, "w_s%d2" % u)
                drain(u + 1, 0)
                drain(u + 1, 1)
                quant_embed([(even, 1), (even, 2)])
            else:
                drain(u + 1, 0)
                round_w1("scalar", even, 1, None, held[u] - 768 if u else None)
                drain(u + 1, 1)
                quant_embed([(even, 1)])
            round_w1("scalar", odd, 1, "turn_w")

            round_w1("gpsimd", odd, 2, "turn%d" % u)
            if not ending:
                round_w1("scalar", even, 2, "w_c%d2" % (even - 1))
            pick(u + 1, "turn1")
            if not ending:
                quant_embed([(even, 2)])
            rest = [(odd, 1), (odd, 2)]
            if odd == TILES - 1:
                quant_embed(rest, placed([P, 2 * P], U8, "w_s_last", 23936))
                diff[u + 1] = placed([P, PAIRS], F32, "diff%d" % (u + 1), 24192)
            elif u == 0:
                diff[u + 1] = placed([P, PAIRS], F32, "diff1", held[2])
            else:
                diff[u + 1] = sb([P, PAIRS], F32, "diff%d" % (u + 1), "raw%d2" % (odd // 2))
            pick_less(u + 1, diff[u + 1][:], whole)
            if odd < TILES - 1:
                quant_embed(rest, sb([P, 2 * P], U8, "w_s%d1" % odd, "w_c%d2" % (even - 1)))
                round_w1("vector", even + 2, 0, "turn_w")
            else:
                weighed_tiles(0, 1, "turn_w")
                weigh("vector", 0, whole, near[0][:])
            for k in range(1 if ending else 2):
                catch_up(u)
            for half in range(2):
                drain(even, half)
        catch_up(STEPS)

        weighed_tiles(1, PACK, "turn1")
        for u in range(1, PACK):
            weigh("gpsimd", u, whole, near[u][:])
        for half in range(2):
            drain(TILES - 1, half)
        for u in last:
            pick(u, None)
        apart(STEPS - 2)
        apart(STEPS - 1)
        similar(STEPS - 2)
        similar(STEPS - 1)
        weighed_tiles(4, 6, None)
        weigh("scalar", 4, whole, near[4][:])
        both = placed([P, 2 * PAIRS], F32, "diff_last", 14848)
        apart_last = [sb([P, PAIRS], F32, "dist_last%d" % i) for i in range(2)]
        near_last = [sb([P, PAIRS], F32, "near_last%d" % i) for i in range(2)]
        pieces = [(u, cols) for cols in halves for u in last]

        def own(k):
            return slice(HALF * k, HALF * (k + 1))

        def close(k):
            nc.scalar.activation(near_last[k // 2][:, halves[k % 2]], apart_last[k // 2][:, halves[k % 2]], ACT.Exp, scale=-1.0)

        for k, (u, cols) in enumerate(pieces):
            pick_less(u, both[:, own(k)], cols)
            nc.scalar.activation(apart_last[k // 2][:, halves[k % 2]], both[:, own(k)], ACT.Abs)
            if k % 2:
                close(k - 1)
                close(k)
        weigh("vector", 5, whole, near[5][:])

        z = [[sb([P, HALF, PACK], BF16, "z00", "dist_last0"), sb([P, HALF, PACK], BF16, "z01", "dist_last1")], [sb([P, HALF, PACK], BF16, "z1%d" % i) for i in range(2)]]
        z_c = {}
        z_s = {}
        y = [[psum.tile([P, HALF], F32, name="y", tag="bank%d" % (4 * half + nt)) for nt in range(N // P)] for half in range(2)]

        def weave(engine, b, c0, c1):
            i = c0 // HALF
            cols = slice(c0 - HALF * i, c1 - HALF * i)
            dst = z[b][i][:, cols, :].rearrange("p (c i) t -> p c t i", i=4)
            src = lanes[b][i][:, :, cols].rearrange("p t (c i) -> p c t i", i=4)
            if engine == "scalar":
                nc.scalar.copy(dst, src)
            else:
                nc.vector.tensor_copy(dst, src)

        def quant_z(b, c0, c1, tag=None):
            i = c0 // HALF
            codes = sb([P, c1 - c0], U32, "z_c%d_%d" % (b, c0), tag)
            scales = sb([P, c1 - c0], U8, "z_s%d_%d" % (b, c0))
            nc.vector.quantize_mx(out=codes[:].bitcast(FP8X4), scales=scales[:], in_=z[b][i][:, c0 - HALF * i : c1 - HALF * i, :].rearrange("p j t -> p (j t)"))
            for c in range(c0 // JB, c1 // JB):
                z_c[(b, c)] = codes[:, JB * c - c0 : JB * (c + 1) - c0]
                z_s[(b, c)] = scales[:, JB * c - c0 : JB * (c + 1) - c0]

        def score(b, c):
            for nt in range(N // P):
                nc.tensor.matmul_mx(
                    out=y[c // 2][nt][:, JB * (c % 2) : JB * (c % 2 + 1)],
                    lhsT=w2_w[:, b, :].bitcast(U8)[:, 2 * P * nt : 2 * P * (nt + 1)].bitcast(FP4X4),
                    lhsT_scale=w2_s[:, b, :].bitcast(U8)[:, P * nt : P * (nt + 1)],
                    rhs=z_c[(b, c)].bitcast(FP8X4),
                    rhs_scale=z_s[(b, c)],
                    start=(b == 0 and c % 2 == 0),
                    stop=(b == 1 and c % 2 == 1),
                )

        def finish(half):
            for nt in range(N // P):
                o = sb([P, HALF], F32, "o%d%d" % (half, nt))
                nc.scalar.activation(o[:], y[half][nt][:], ACT.Sigmoid)
                nc.sync.dma_start(out[P * nt : P * (nt + 1), halves[half]], o[:])

        for half, cols in enumerate(halves):
            for u in (4, 5):
                deal(u, half)
            pair = sb([P, PAIRS], BF16, "z_last%d" % half, "turn1" if half else None)
            for i, u in enumerate(last):
                nc.vector.tensor_scalar(pair[:, halves[i]], near_last[half][:, halves[i]], gain_sb[:, u : u + 1], None, ALU.mult)
                nc.sync.dma_start(lanes[1][half][32 * (u % PACK) : 32 * (u % PACK + 1), :, :], pair[:, halves[i]])
            if half == 0:
                weave("vector", 0, 0, HALF)
        quant_z(0, 0, HALF)
        weave("vector", 0, HALF, PAIRS)
        for c in range(2):
            score(0, c)
        for half in range(2):
            blocks = (2 * half, 2 * half + 1)
            for c in blocks:
                weave("vector", 1, JB * c, JB * (c + 1))
            for c in blocks:
                quant_z(1, JB * c, JB * (c + 1))
                score(1, c)
            finish(half)
            if half == 0:
                quant_z(0, HALF, PAIRS, "lanes10")
                for c in range(2, 4):
                    score(0, c)
